import numpy as np, ml_dtypes
CORES = [9,25,41,57]
N = 4
import mx_ref
BF = ml_dtypes.bfloat16
def gcols(t, e):
    v = np.concatenate([t.reshape(8, 16, -1, 4), np.zeros((8, 16, 1, 4), BF)], axis=2)
    return np.ascontiguousarray(np.stack([v[g][:, e[g]] for g in range(8)])).reshape(128, -1)
def tile(rs):
    return np.stack(rs, axis=2).reshape(128, -1).astype(BF)
def pick(q, e):
    c = np.concatenate([q[0].reshape(128, -1, 4), np.zeros((128, 1, 4), np.uint8)], axis=1); s = np.concatenate([q[1], np.ones((16, 1), np.uint8)], axis=1)
    return (np.ascontiguousarray(c[:, e].reshape(128, -1)), np.ascontiguousarray(s[:, e]))
def join(*qs):
    return (np.concatenate([q[0] for q in qs], axis=1), np.concatenate([q[1] for q in qs], axis=1))
def put(q, e, v):
    c, s = q[0].reshape(128, -1, 4).copy(), q[1].copy(); c[:, e] = v[0].reshape(128, -1, 4); s[:, e] = v[1]
    return (c.reshape(128, -1), s)
def pk(c, s):
    return (np.ascontiguousarray(c), mx_ref.live(s))
def emit(q):
    return q[0], q[1]
def packed(v, rng):
    q = [mx_ref.quantize(np.ascontiguousarray(v[r])) for r in range(N)]
    return np.stack([a for a, b in q]), np.stack([mx_ref.plane(b, rng) for a, b in q])
def values_of_codes():
    e, c = np.zeros((128, 128, 4), np.float32), np.zeros((128, 2, 4), np.uint8)
    e[np.arange(128), np.arange(128), 0] = 1
    c[:127, :, 0] = np.arange(256).reshape(2, 128).T[:127]
    return mx_ref.matmul(mx_ref.quantize(e.reshape(128, 512).astype(BF)), (c.reshape(128, 8), np.full((16, 2), 127, np.uint8))).T.reshape(-1).astype(np.float64)
CODE_VALUE, SCALE_VALUE = values_of_codes(), 2.0 ** (np.arange(256) - 127.0)
def decode(q):
    return (CODE_VALUE[q[0]].reshape(16, 8, -1, 4) * SCALE_VALUE[q[1]][:, None, :, None] + 0.0).reshape(128, -1).astype(np.float32)
def f(rng, *shape):
    return mx_ref.flush((rng.standard_normal(shape, dtype=np.float32) * np.exp2(rng.integers(-2, 3, shape[:-1] + (1,)))).astype(BF))
def wide(rng, *shape, cols=0):
    v = rng.standard_normal(shape, dtype=np.float32) * np.exp2(rng.integers(-12, 13, shape)).astype(np.float32)
    if cols: v *= np.repeat(np.exp2(rng.integers(-cols, cols + 1, shape[:-2] + (1, shape[-1] // 4))) * (rng.random(shape[:-2] + (1, shape[-1] // 4)) > 0.0625), 4, axis=-1).astype(np.float32)
    return mx_ref.flush(v.astype(BF))
C, K, R = 384, 52, 3
H = C // 2
STEP = [1, 2, 1]
def partner(r, t):
    return r ^ STEP[t]
def chains(sl, sr, f):
    a = np.flatnonzero(np.concatenate([[0], f[:-1]]) == 0)
    b = np.flatnonzero(f == 0)
    at = np.stack([a, b], axis=1).reshape(-1)
    o = np.argsort(-(np.stack([sl[a], sr[b]], axis=1).reshape(-1) + np.float32(0.0)), kind="stable")
    own = np.arange(len(a))
    near = [[k - 1 if k > 0 and f[k - 1] else -1, k + 1 if f[k] else -1] for k in range(C)]
    for i in range(K):
        d, e = int(o[2 * i]), int(o[2 * i + 1])
        if own[d // 2] != own[e // 2]:
            own[own == own[e // 2]] = own[d // 2]
            near[at[d]][d % 2], near[at[e]][e % 2] = int(at[e]), int(at[d])
    ways, seen = [], set()
    for k in range(C):
        if min(near[k]) < 0 and k not in seen:
            way, came = [k], -1
            while True:
                on = [j for j in near[way[-1]] if j >= 0 and j != came]
                if not on: break
                came = way[-1]
                way.append(on[0])
            seen.update((way[0], way[-1]))
            ways.append(way)
    ways.sort(key=min)
    return np.concatenate(ways), np.concatenate([[1] * (len(way) - 1) + [0] for way in ways])
def numbers_of(rng):
    return {"x": np.array(f(rng, N, 128, 4 * C)), "u": np.array(f(rng, N, 128, 512)), "v": np.array(f(rng, N, 128, 512))}
def weights(rng, w):
    c, p = packed(w, rng)
    return {"wc": c, "ws": p}
def layer(rng):
    w = np.array(f(rng, N, 128, 2048)).reshape(N, 8, 16, 4, 8, 16, 4)
    w[:, :, :, :, :, 8:] = 0
    w[:, :, :, :, :, 0] = 0
    return weights(rng, w.reshape(N, 128, 2048))
def signs(rng):
    k = np.stack([rng.permutation(8) % 4 for r in range(N)])
    return np.stack([k % 2, k // 2], axis=2) * 2.0 - 1.0
def digits(s):
    b = ((s[..., None] >> np.arange(8)) & 1) * np.exp2(np.arange(8.0))
    return b.reshape(N, 8, C, 2, 4).transpose(0, 1, 3, 2, 4)
def own_part(u, k):
    k = k.astype(np.float32).astype(BF)
    u = u.reshape(N, 8, 16, 128, 4)
    u[:, :, :, ::16] = 0
    u[:, :, :, 1::16] = 0
    for g in range(8):
        for s in range(2):
            u[:, g, 0, 16 * g + s, s] = k
            u[:, g, 8 + 2 * s:10 + 2 * s, 16 * g + s] = k[:, None, None]
    return u.reshape(N, 128, 512)
def setup_inputs(rng):
    return {**numbers_of(rng), **weights(rng, f(rng, N, 128, 2048))}
def setup_inputs_ties(rng):
    d = numbers_of(rng)
    e = rng.permutation(N)
    x = d["x"].reshape(N, 8, 16, C, 4)
    for r in range(N):
        k = np.zeros(C, int) if r == e[0] else rng.permutation(C) % 3
        a = x[r][:, :8, :3].copy()
        a[:, :, 2] = 0
        x[r][:, :8] = a[:, :, k]
    x[e[1]] = 0
    u = d["u"].reshape(N, 8, 16, 128, 4)
    u[:, :, 8:, ::16] = 0
    u[:, :, 8:, 1::16] = 0
    w = np.array(f(rng, N, 128, 2048)).reshape(N, 8, 16, 4, 8, 16, 4)
    w[:, :, 8:, :, :, :8] = 0
    return {"x": x.reshape(N, 128, 4 * C), "u": u.reshape(N, 128, 512), "v": d["v"], **weights(rng, w.reshape(N, 128, 2048))}
def setup_inputs_near(rng):
    d = numbers_of(rng)
    x = d["x"].astype(np.float32).reshape(N, 8, 16, C, 4)
    c = np.arange(C)
    x[:, :, 0] = 0
    x[:, :, 0, :, :2] = signs(rng)[:, :, None]
    x[:, :, 8:10] = digits(np.tile(C // 2 - 1 - (C - 1 - c) // 3, (N, 8, 1))) * 2.0 ** -23
    x[:, :, 10:12] = digits((c // 2 + rng.integers(0, C // 2, (N, 8, 1))) % (C // 2)) * 2.0 ** -23
    x[:, :, 12:] = rng.integers(4, 8, (N, 8, 4, C, 4)) * rng.choice([-1.0, 1.0], (N, 8, 4, C, 4)) * 2.0 ** -20
    k = np.where(rng.permutation(N) < N // 2, 2.0 ** -30, 1.0)
    return {"x": x.reshape(N, 128, 4 * C).astype(BF), "u": own_part(d["u"], k), "v": d["v"], **layer(rng)}
def setup_inputs_loops(rng):
    d = numbers_of(rng)
    s = np.zeros((N, 8, C, 2), int)
    q = int(rng.integers(8))
    for r in range(N):
        kind = np.insert(rng.permutation(7) % 5, q, 5)
        for g in range(8):
            if g == q:
                if r & STEP[1]:
                    s[r, g, H + 1:H + 3 * K - 2, 0] = 3
                    s[r, g, H:H + 3 * K - 3, 1] = 3
                    s[r, g, H, 0] = 2
                    s[r, g, H + 3 * K - 2, 0] = 1
                else:
                    s[r, g, 3:2 * K + 3, 0] = 3
                    s[r, g, 2:2 * K + 2, 1] = 3
                    s[r, g, 2, 0] = 2
                    s[r, g, 2 * K + 2, 1] = 2
                    s[r, g, 0] = (2, 1)
                continue
            left, e, free = K, [], rng.permutation(C)
            while left:
                n, closed = ((K, 1), (K, 0), (int(rng.integers(1, 4)), 1), (int(rng.integers(1, 8)), int(rng.integers(2))), (1, 1))[kind[g]]
                n = min(n, left)
                m = n + 1 - closed
                c, free = free[:m], free[m:]
                side = rng.integers(0, 2, m)
                e += [(c[j], side[j], c[(j + 1) % m], 1 - side[(j + 1) % m]) for j in range(n)]
                left -= n
            e = np.array(e)
            i = K - rng.permutation(K)
            s[r, g, e[:, 0], e[:, 1]] = i
            s[r, g, e[:, 2], e[:, 3]] = i
    tiny = rng.permutation(N) < N // 2
    size = np.where(tiny[:, None] | (np.arange(8) == q), 2.0 ** -27, 2.0 ** -4)[:, :, None, None, None]
    x = d["x"].astype(np.float32).reshape(N, 8, 16, C, 4)
    x[:, :, 0] = 0
    x[:, :, 8:10] = digits(s[..., 0]) * size
    x[:, :, 10:12] = digits(s[..., 1]) * size
    x[:, :, 12:] = rng.integers(4, 8, (N, 8, 4, C, 4)) * rng.choice([-1.0, 1.0], (N, 8, 4, C, 4)) * size
    return {"x": x.reshape(N, 128, 4 * C).astype(BF), "u": own_part(d["u"], np.where(tiny, 2.0 ** -30, 1.0)), "v": d["v"], **layer(rng)}
def setup_inputs_huge(rng):
    d = numbers_of(rng)
    x = 2.0 ** 30 * (0.45 + 0.15 * rng.random((N, 128, C, 4)))
    for r in range(N):
        x[r][:, rng.permutation(C)[:8]] = 2.0 ** 30 * (0.76 + 0.04 * rng.random((128, 8, 4)))
    u = d["u"].reshape(N, 128, 8, 16, 4)
    u[:, :, :, :2] = (2.0 ** 30 * (1 - 0.25 * rng.random((N, 128, 8, 2, 4))) * signs(rng)[:, None, :, :, None]).astype(np.float32).astype(BF)
    w = mx_ref.flush((f(rng, N, 128, 2048).astype(np.float32) * np.float32(2.0 ** -6)).astype(BF))
    return {"x": x.astype(np.float32).reshape(N, 128, 4 * C).astype(BF), "u": u.reshape(N, 128, 512), "v": d["v"], **weights(rng, w)}
def setup_inputs_spread(rng):
    d = setup_inputs(rng)
    d["x"] = wide(rng, N, 128, 4 * C, cols=6)
    return d
def check_inputs(d):
    b = []
    for k in ("x", "u", "v"):
        a = np.abs(d[k].astype(np.float32))
        if not (np.isfinite(a).all() and ((a == 0) | (a >= 2.0 ** -30) & (a <= 2.0 ** 30)).all()): b.append("a value of " + k)
    if ((d["wc"] & 127) == 127).any(): b.append("a code of wc")
    for r in range(N):
        s = mx_ref.live(d["ws"][r]).astype(int)
        if ((s > 1) & (np.abs(s - 127) > 46)).any(): b.append("a scale of ws")
    return b
def reference(x, u, v, wc, ws):
    qu = [mx_ref.quantize(u[r]) for r in range(N)]
    lay = [pk(wc[r], ws[r]) for r in range(N)]
    now = [x[r] for r in range(N)]
    flag = [np.zeros((8, C), np.int64) for r in range(N)]
    for t in range(R):
        p, new, made = [], [], []
        for r in range(N):
            q = mx_ref.quantize(now[r])
            s = mx_ref.matmul(qu[r], q)
            e = [chains(s[16 * g], s[16 * g + 1], flag[r][g]) for g in range(8)]
            p.append(np.stack([a for a, b in e]))
            new.append(np.stack([b for a, b in e]))
            d = decode(q).astype(BF)
            one = gcols(d, p[r])
            two = gcols(d, np.where(new[r] == 1, np.roll(p[r], -1, axis=1), p[r]))
            made.append(mx_ref.quantize(((one.astype(np.float32) + two.astype(np.float32)) * np.float32(0.5)).astype(BF)))
            new[r][:, H - 1] = 0
        for r in range(N):
            e = partner(r, t)
            flag[r] = np.concatenate([new[r][:, :H], new[e][:, H:]], axis=1)
            z = join(pick(made[r], np.arange(H)), pick(made[e], np.arange(H, C)))
            d = decode(z).reshape(128, C, 4)
            now[r] = tile([d[:, :, b] + np.maximum(mx_ref.matmul(pick(lay[r], np.arange(128 * b, 128 * b + 128)), z), np.float32(0.0)) * np.float32(0.015625) for b in range(4)])
    y, ol = np.zeros((N, 128, C), np.float32), np.zeros((N, 8, 2 * C), np.float32)
    oc, osc = np.zeros((N, 128, 4 * C), np.uint8), np.zeros((N, 16, C), np.uint8)
    for r in range(N):
        q = mx_ref.quantize(now[r])
        y[r] = mx_ref.matmul(mx_ref.quantize(v[r]), q)
        ol[r] = np.concatenate([p[r], flag[r]], axis=1)
        oc[r], osc[r] = emit(q)
    return {"y": y, "ol": ol, "oc": oc, "osc": osc}

@@ -1,0 +1,598 @@
+import numpy as np
+from concourse.mybir import dt, AluOpType as ALU, ActivationFunctionType as AF, AxisListType as AX
+
+C, H, K2, NS = 384, 192, 104, 112
+N1, N2 = 192, 208
+STEP = [1, 2, 1]
+WAKE, FAR = 100.0, 3000.0
+LOOK = {"v": 0.0, "a": 150.0, "p": 0.0, "g": 300.0, "s": 0.0, "r": 0.0}
+NA = (6, 6, 6)
+F, B, I, U, Q, S8 = "float32", "bfloat16", "int32", "uint16", "float8_e4m3fn_x4", "uint8"
+
+
+def _sb(n, d):
+    return ("sbuf", [128, n], d)
+
+
+SCRATCH = {
+    "xin": _sb(1536, B), "uin": _sb(512, B), "vin": _sb(512, B), "ein": _sb(2048, B), "ones": _sb(N2, B), "on5": _sb(512, B),
+    "xt": _sb(1536, B), "yt": _sb(1536, B), "dx": _sb(1536, B), "y1": _sb(1536, B), "rl": _sb(1536, F),
+    "wq": _sb(512, Q), "wsc": _sb(512, S8), "uq": _sb(128, Q), "us": _sb(128, S8), "vq": _sb(128, Q), "vs": _sb(128, S8),
+    "u2q": _sb(256, Q), "u2s": _sb(256, S8), "eq": _sb(512, Q), "es": _sb(512, S8),
+    "xq": _sb(C, Q), "xs": _sb(C, S8), "sq": _sb(3 * H, Q), "ss": _sb(3 * H, S8),
+    "zq0": _sb(C, Q), "zq1": _sb(C, Q), "zq2": _sb(C, Q), "zs0": _sb(C, S8), "zs1": _sb(C, S8), "zs2": _sb(C, S8),
+    "nl0": _sb(12, U), "nl1": _sb(12, U), "nl2": _sb(12, U), "ns": _sb(72, U),
+    "ps": ("psum", [128, 4096], F),
+    "t16": _sb(C, F), "lm": _sb(224, F), "c0": _sb(N2, F), "z0": _sb(N2, B), "cv": _sb(C, F), "cv2": _sb(C, F), "ik": _sb(392, F),
+    "selt": _sb(N2, B), "cpl": _sb(392, F), "cpr": _sb(392, F), "cpv": _sb(C, F), "rx": _sb(NS, F), "pn": _sb(NS, F), "pn0": _sb(NS, F),
+    "one": _sb(C, F), "cs": _sb(128, F), "ci": _sb(8, I), "cu": _sb(64, U), "w01": _sb(16, F), "z3": _sb(24, F), "lm0": _sb(224, F),
+    "fb": _sb(400, F), "fr": _sb(C, F), "fc": _sb(C, F), "kr": _sb(C, F), "pkl": _sb(392, F), "pkr": _sb(392, F), "cap": _sb(392, F),
+    "hc": _sb(C, F), "kd": _sb(64, F), "sc": _sb(C, F), "sc2": _sb(C, F), "sc3": _sb(C, F), "dk": _sb(64, I),
+    "sl": _sb(392, F), "sr": _sb(392, F), "pm": _sb(392, F), "w": _sb(N1, F), "x1": _sb(224, F), "x2": _sb(N2, F), "x3": _sb(N2, B), "x4": _sb(N2, B),
+    "cmp": _sb(8 * N2, B), "cum2": _sb(8 * N2, B), "tau": _sb(8 * N2, B), "junk": _sb(4 * N2, B), "acc": _sb(112, F), "ru": _sb(16, U),
+    "sel": _sb(N2, B), "pre": _sb(N2, B), "cnt": _sb(3 * 120, B), "l3": _sb(32, U), "r2": _sb(224, F), "r3": _sb(224, F),
+    "i2": _sb(224, F), "i3": _sb(NS, F), "k2": _sb(224, F), "ew": _sb(N2, F),
+    "di": _sb(256, I), "df": _sb(256, F), "du": _sb(160, U), "inv": _sb(784, F),
+    "jp": _sb(512, F), "ja": _sb(768, F), "jm": _sb(768, F), "jn": _sb(768, F), "jy": _sb(6 * 224, F), "js": _sb(9 * NS, F),
+    "f0": _sb(224, F), "f1": _sb(224, F), "f2": _sb(224, F), "h0": _sb(336, F), "h1": _sb(336, F), "h2": _sb(336, F),
+    "ja2": _sb(NS, F), "jn2": _sb(NS, F), "si": _sb(8 * NS, I), "sf": _sb(13 * NS, F),
+    "tl": _sb(504, F), "tn": _sb(504, F), "tg": _sb(504, F), "cum": _sb(400, F), "vr": _sb(C, F), "gr": _sb(C, F),
+    "vw": _sb(392, F), "pl": _sb(72, U), "oi": _sb(C, I), "of": _sb(C, F), "yo": _sb(C, F),
+}
+SEMAPHORES = (["v", "a", "p", "g"] + ["d%d" % i for i in range(1, 25)]
+              + ["%s%d" % (n, t) for n in ("ln", "lc", "ls", "rn", "rc", "rs") for t in range(3)])
+
+
+def A(n, lo=0, hi=None, st=1):
+    return (n, lo, SCRATCH[n][1][1] if hi is None else hi, st)
+
+
+def half(*xs):
+    return 0.5 if all(x[0] != "*" and SCRATCH[x[0]][2] in (B, U) for x in xs) else 1.0
+
+
+def col(n, c):
+    return (n, c, c + 1, 1)
+
+
+def IND(w, o):
+    return ("*", w, o)
+
+
+def rank_program(g, core, T, topo):
+    rank = T.rank_of(core)
+    if rank is None:
+        return
+    eng = {"v": g.vector, "a": g.scalar, "p": g.tensor, "g": g, "s": g.sync}
+    ops, nd = [], [0]
+    lastw = {n: np.full(v[1][1], -1) for n, v in SCRATCH.items()}
+    reads = {n: [] for n in SCRATCH}
+    bank = [{} for _ in range(8)]
+
+    def ap(x):
+        if not isinstance(x, tuple):
+            return x
+        if x[0] == "*":
+            return ap(x[1]).indirect(ap(x[2]))
+        return T[x[0]][:, x[1]:x[2]:x[3]] if x[3] != 1 else T[x[0]][:, x[1]:x[2]]
+
+    def note(e, rd, wr, call, sem, inc, busy, lat):
+        need, me, r2, w2 = set(), len(ops), [], []
+        for x in rd:
+            if isinstance(x, tuple):
+                r2 += [x[1], x[2]] if x[0] == "*" else [x]
+        for x in wr:
+            if x[0] == "*":
+                w2.append(x[1])
+                r2.append(x[2])
+            else:
+                w2.append(x)
+        for x in r2 + w2:
+            need.update(np.unique(lastw[x[0]][x[1]:x[2]:x[3]]).tolist())
+            if x[0] == "ps":
+                for b in range(x[1] // 512, (x[2] - 1) // 512 + 1):
+                    need.update(i for k, v in bank[b].items() if k != e for i in v)
+                    bank[b] = {e: bank[b].get(e, []) + [me]}
+        for x in w2:
+            mine, keep = set(range(x[1], x[2], x[3])), []
+            for i, cols in reads[x[0]]:
+                if cols & mine:
+                    need.add(i)
+                if not cols <= mine:
+                    keep.append((i, cols))
+            reads[x[0]] = keep
+        for x in r2:
+            reads[x[0]].append((me, set(range(x[1], x[2], x[3]))))
+        for x in w2:
+            lastw[x[0]][x[1]:x[2]:x[3]] = me
+        need.discard(-1)
+        ops.append((e, sorted(need), call, sem, inc, busy, lat))
+
+    def run(e, rd, wr, call, per=1.0):
+        x = rd[0] if rd else wr[0]
+        if wr[0][0] == "*":
+            c = 50 + 3.5 * len(range(*x[1:]))
+        elif x[0] == "*":
+            c = 55 + 1.5 * len(range(*wr[0][1:]))
+        elif e in "va":
+            c = max(64, per * len(range(*x[1:])))
+        else:
+            c = 150 + 2 * len(range(*wr[0][1:])) if e == "g" else 0.6 * (16 + len(range(*wr[0][1:])))
+        note(e, rd, wr, lambda s: call().then_inc(T.sem[s], 1), e, 1, c, c)
+
+    def issue():
+        n = len(ops)
+        after, way = [[] for _ in ops], [0.0] * n
+        for i, o in enumerate(ops):
+            for d in o[1]:
+                after[d].append(i)
+        for i in range(n - 1, -1, -1):
+            way[i] = ops[i][6] + max([way[j] + WAKE for j in after[i]] + [0.0])
+        left, ready, free = [len(o[1]) for o in ops], [0.0] * n, {e: 0.0 for e in list(eng) + ["r"]}
+        cand = {e: [i for i in range(n) if ops[i][0] == e and not left[i]] for e in free}
+        tok, cnt, seen = [None] * n, {}, {e: {} for e in free}
+        for _ in range(n):
+            e = min((max(free[e], min(ready[i] for i in c)), e) for e, c in cand.items() if c)[1]
+            now = max(free[e], min(ready[i] for i in cand[e]))
+            i = -max((way[i], -i) for i in cand[e] if ready[i] <= now + LOOK[e])[1]
+            cand[e].remove(i)
+            now = max(now, ready[i])
+            _, need, call, sem, inc, busy, lat = ops[i]
+            free[e] = now + busy
+            for j in after[i]:
+                ready[j] = max(ready[j], now + lat + WAKE)
+                left[j] -= 1
+                if not left[j]:
+                    cand[ops[j][0]].append(j)
+            cnt[sem] = cnt.get(sem, 0) + inc
+            tok[i] = (sem, cnt[sem])
+            if e == "r":
+                continue
+            most = {}
+            for d in need:
+                most[tok[d][0]] = max(most.get(tok[d][0], 0), tok[d][1])
+            for s in sorted(most):
+                if seen[e].get(s, 0) < most[s]:
+                    eng[e].wait_ge(T.sem[s], most[s])
+                    seen[e][s] = most[s]
+            call(sem)
+        for s in sorted(cnt):
+            g.wait_ge(T.sem[s], cnt[s])
+
+    def tt(o, a, b, op):
+        run("v", [a, b], [o], lambda: g.vector.tensor_tensor(ap(o), ap(a), ap(b), op), 1.0 if "ps" in (a[0], b[0]) else 2.0)
+
+    def ts(o, a, s1, op0, s2=None, op1=None):
+        if op1 is None:
+            run("v", [a, s1], [o], lambda: g.vector.tensor_scalar(ap(o), ap(a), ap(s1), None, op0), half(o, a))
+        else:
+            run("v", [a, s1, s2], [o], lambda: g.vector.tensor_scalar(ap(o), ap(a), ap(s1), ap(s2), op0, op1), half(o, a))
+
+    def cp(o, a):
+        run("v", [a], [o], lambda: g.vector.tensor_copy(ap(o), ap(a)))
+
+    def ms(o, c):
+        run("v", [], [o], lambda: g.vector.memset(ap(o), c), half(o))
+
+    def scan(o, a, b, op0, op1):
+        run("v", [a, b], [o], lambda: g.vector.tensor_tensor_scan(ap(o), ap(a), ap(b), 0.0, op0, op1), half(o, a, b))
+
+    def red(o, a):
+        run("v", [a], [o], lambda: g.vector.tensor_reduce(ap(o), ap(a), AX.X, ALU.add))
+
+    def act(o, a, f=None, bias=None, scale=None, acc=None):
+        kw = {}
+        if bias is not None:
+            kw["bias"] = ap(bias)
+        if scale is not None:
+            kw["scale"] = scale
+        if acc is not None:
+            kw["accum_out"] = ap(acc)
+        fn = f if f is not None else (AF.Copy if bias is None and acc is None else AF.Identity)
+        run("a", [a, bias], [o] + ([acc] if acc else []), lambda: g.scalar.activation(ap(o), ap(a), fn, **kw))
+
+    def iota(o, pat, base, cm=0, behind=()):
+        if SCRATCH[o[0]][2] == I:
+            run("g", [], [o], lambda: g.iota(ap(o), pat, base, cm))
+        else:
+            run("g", list(behind), [o], lambda: g.iota(ap(o), pat, base, cm, allow_small_or_imprecise_dtypes=True))
+
+    def qz(oq, os_, a):
+        run("v", [a], [oq, os_], lambda: g.vector.quantize_mx(ap(oq), ap(os_), ap(a)), 0.23)
+
+    def mm(b, wq, ws, xq, xs):
+        o = A("ps", 512 * b, 512 * b + xq[2] - xq[1])
+        run("p", [wq, ws, xq, xs], [o], lambda: g.tensor.matmul_mx(ap(o), ap(wq), ap(ws), ap(xq), ap(xs), True, True))
+
+    def dma(e, rd, wr, out, in_, lat=2500.0):
+        nd[0] += 1
+        note(e, rd, wr, lambda s: eng[e].dma_start(out, in_).then_inc(T.sem[s], 16), "d%d" % nd[0], 16, 60.0, lat)
+
+    def send(src, dst, kind, t, cast):
+        to = T.cores[rank ^ STEP[t]]
+        rid, pid = topo.addr(to)[:2]
+        a, b = (ap(dst).bitcast(dt.uint8), ap(src).bitcast(dt.uint8)) if cast else (ap(dst), ap(src))
+        note("g", [src], [], lambda s: g.remote_dma(a, b, T.sem["r%s%d" % (kind, t)], T.sem[s], pid, rid, topo.mask(core, to)),
+             "l%s%d" % (kind, t), len(topo.engines(core, to)), 500.0, FAR)
+        ops.append(("r", [len(ops) - 1], None, "r%s%d" % (kind, t), len(topo.engines(to, core)), 0.0, 0.0))
+        lastw[dst[0]][dst[1]:dst[2]] = len(ops) - 1
+
+    def to_d(tmp, src, n, lo=0):
+        scan(A(tmp, lo, lo + n), A("cv", 0, n), src, ALU.add, ALU.max)
+        return A(tmp, lo + 15, lo + n, 16)
+
+    qf, q1, corr, corr7, kD, kB, kP = col("cs", 0), col("cs", 1), col("cs", 2), col("cs", 3), A("cs", 8, 32), 32, 40
+    jk, jl = A("cs", 72, 79), A("cs", 64, 71)
+    ONV = (4, 5, 6)
+
+    def window(n, m):
+        w = n - K2 + 16
+        lo = min(16 * m, n - w)
+        return lo, lo + w
+
+    dma("a", [], [A("uin")], T.uin[:], T.u[:])
+    dma("s", [], [A("xin", 0, 768)], T.xin[:, 0:768], T.x[:, 0:768], 3000.0)
+    dma("a", [], [A("xin", 768, 1536)], T.xin[:, 768:1536], T.x[:, 768:1536], 3500.0)
+    iota(col("ci", 0), [[0, 1]], 0, 1)
+    iota(A("cs", 96, 120), [[16, 24]], 0)
+    iota(A("t16"), [[0, 24], [1, 16]], 0)
+    iota(A("ik"), [[1, 392]], 0)
+    ms(A("ones"), 1.0)
+    ms(A("c0"), 0.0)
+    ms(A("z0"), 1.0)
+    cp(A("cu", 0, 8), A("cs", 96, 104))
+    ts(A("cu", 8, 16), A("cs", 96, 104), 1.0, ALU.add)
+    ts(col("ci", 1), col("ci", 0), 15, ALU.bitwise_and)
+    ms(A("c0", 0, N2, 16), 5e29)
+    cp(qf, col("ci", 1))
+    ms(A("z0", 0, N2, 16), 0.0)
+    ts(q1, qf, 1.0, ALU.add)
+    ts(corr, qf, 15.0, ALU.is_lt, 2.0 ** 21, ALU.mult)
+    ts(kD, A("cs", 96, 120), qf, ALU.add)
+    ms(A("selt", 0, K2), 1.0)
+    ms(A("selt", K2, N2), 0.0)
+    ts(A("cs", kP, kP + 7), A("cs", 8, 15), 0.5, ALU.add)
+    ts(A("cs", kB, kB + 7), A("cs", 8, 15), 0.5, ALU.add, -1.0, ALU.mult)
+    ts(A("lm0"), A("t16", 0, 224), qf, ALU.not_equal, 8e29, ALU.mult)
+    act(A("lm"), A("lm0"), bias=-3e29)
+    ms(A("z3", 0, 24, 3), 0.0)
+    ms(A("z3", 1, 24, 3), -1.0)
+    ms(A("z3", 2, 24, 3), 1.0)
+    for n in ("pm", "sl", "sr"):
+        ms(A(n, C, 392), -2e29)
+    for k, n in enumerate((N1, N2)):
+        for m in range(7):
+            lo, hi = window(n, m)
+            ms(col("cs", 48 + 8 * k + m), float(-2 * lo - (hi - lo) * (2 if m in ONV else 1)))
+    qz(A("uq"), A("us"), A("uin"))
+
+    def repeat_u(k):
+        o, w, l = A("u2q", 128 * k, 128 * k + 128), A("uq"), A("cu", 8 * k, 8 * k + 8)
+        run("v", [w, l], [o], lambda: g.vector.tensor_copy(ap(o).bitcast(dt.uint32), ap(w).bitcast(dt.uint32).indirect(ap(l))), 2.0)
+        act(A("u2s", 128 * k, 128 * k + 128), IND(A("us"), l))
+
+    def unpacker(b):
+        o = A("ein", 512 * b, 512 * b + 512)
+        run("g", [A("on5")], [o], lambda: g.affine_select(ap(o), T.on5[:], [[-1, 128], [1000, 4]], ALU.is_equal, 0.0, -1000 * b, 1))
+
+    repeat_u(0)
+    repeat_u(1)
+    for h in range(2):
+        qz(A("xq", H * h, H * h + H), A("xs", H * h, H * h + H), A("xin", 768 * h, 768 * h + 768))
+    dma("s", [A("xin")], [A("wq")], T.wq[:].bitcast(dt.uint8), T.wc[:])
+    dma("s", [A("xin")], [A("wsc")], T.wsc[:], T.ws[:])
+    dma("s", [A("xin")], [A("vin")], T.vin[:], T.v[:])
+    ts(A("cv"), A("t16"), qf, ALU.is_equal, -2.0 ** 22, ALU.mult)
+    ts(A("cv2"), A("t16"), q1, ALU.is_equal, 2.0 ** 21, ALU.mult)
+    tt(A("cv"), A("cv"), A("cv2"), ALU.add)
+    iota(A("cpr"), [[2050, 392]], 1024)
+    iota(A("cpl"), [[2050, 392]], 1)
+    iota(A("rx", 0, K2), [[4, 52], [-2, 2]], 3)
+    iota(A("ja", 0, 768, 2), [[0, 384]], 2 ** 24 - 1)
+    iota(A("jp"), [[0, 512]], 225)
+    iota(A("jn"), [[0, 768]], 1024000)
+    iota(A("f0", 0, 224, 2), [[0, NS]], 0)
+    iota(A("h0"), [[0, NS], [1, 3]], -1)
+    ms(A("h0", 0, 336, 3), 0.0)
+    iota(A("pn0"), [[-1, 56], [0, 2]], 56)
+    iota(A("on5"), [[0, 512]], 1)
+    for b in range(4):
+        unpacker(b)
+    iota(A("one"), [[0, C]], 1)
+    iota(A("cpv"), [[-2050, C]], 2050 * (C - 1) + 1)
+    qz(A("eq"), A("es"), A("ein"))
+    act(A("pn"), A("pn0"), scale=2.0 ** 18)
+    ms(A("rx", K2, NS), 225.0)
+    ms(A("ja", 225, 768, 256), 0.0)
+    ms(A("jm", 224, 768, 256), 2.0 ** 24)
+    ms(A("jm", 225, 768, 256), 2.0 ** 24)
+    ms(A("jm", 0, 224, 2), 0.0)
+    ts(jk, A("cs", 8, 15), 104.0, ALU.is_lt)
+    ts(jl, A("cs", 8, 15), 392.0, ALU.add)
+    ts(corr7, corr, -7.0 * 1024, ALU.add)
+    ts(col("cs", 4), corr, 384.0, ALU.add)
+    ts(col("cs", 5), corr, 0.25, ALU.add)
+    ms(A("cum", 0, 8), 0.0)
+    ms(A("vw", C, 392), 2.0 ** 20)
+    ms(A("w01", 0, 1), 0.0)
+    ms(A("w01", 1, 16), 1.0)
+    ms(A("fb", 0, 8), 0.0)
+    ms(A("pkl", C, 392), 0.0)
+    ms(A("pkr", C, 392), 0.0)
+    ts(A("cu", 16, 40), kD, -1.0, ALU.mult, 383.0, ALU.add)
+    qz(A("vq"), A("vs"), A("vin"))
+
+    fp, fk = A("fb", 7, 7 + C), A("fb", 8, 8 + C)
+    rev = A("cu", 16, 40)
+
+    def tables():
+        act(A("cap", 0, C + 1), A("fb", 7, 8 + C), bias=1e29, scale=-2e29)
+        act(A("fc"), fp, bias=2.0 ** 21, scale=2048.0 - 2.0 ** 21)
+        act(A("fr"), IND(fk, rev), bias=-2.0 ** 21, scale=2.0 ** 21 - 2048.0)
+        scan(A("pkr", 0, C), A("fc"), A("cpr", 0, C), ALU.add, ALU.min)
+        d = to_d("sc3", A("pkr", 0, C), C)
+        ts(A("dk", 0, 24), d, corr, ALU.subtract)
+        scan(A("kr"), A("fr"), A("cpv"), ALU.add, ALU.max)
+        ts(A("dk", 32, 56), A("dk", 0, 24), 1023, ALU.bitwise_and, 1, ALU.logical_shift_right)
+        tt(A("kd", 0, 24), kD, A("dk", 32, 56), ALU.subtract)
+        cp(A("cu", 40, 64), A("dk", 32, 56))
+        ts(A("kd", 32, 56), A("kd", 0, 24), 2.0, ALU.mult)
+        act(A("pkl", 0, C), IND(A("kr"), rev))
+        act(A("hc"), fp, bias=2.0 ** 20, scale=1.0 - 2.0 ** 20)
+
+    def ranks(n, rn, na):
+        L = n // 16
+        scan(A("x2", 0, n), A("c0", 0, n), A("x1", 0, n), ALU.add, ALU.min)
+        for m in range(na):
+            e, j = 16 * m + 16, N2 * (m % 4)
+            act(A("tau", m * n, m * n + n), A(rn, 0, n), AF.Sign, bias=col("x2", 16 * m + 15), scale=-1.0)
+            act(A("junk", j, j + e), A("tau", m * n, m * n + e), AF.Relu, acc=col("acc", 3 * m))
+            act(A("junk", j + e, j + n), A("tau", m * n + e, m * n + n), AF.Relu, scale=-1.0, acc=col("acc", 3 * m + 1))
+        tt(A("x3", 0, n), A("x2", 0, n), A(rn, 0, n), ALU.is_equal)
+        scan(A("x4", 0, n), A("z0", 0, n), A("x3", 0, n), ALU.mult, ALU.add)
+        for m in range(na, L):
+            k, e, o = col("x2", 16 * m + 15), 16 * m + 16, (m - na) * n
+            ts(A("cmp", o, o + e), A(rn, 0, e), k, ALU.is_ge)
+            if e < n:
+                ts(A("cmp", o + e, o + n), A(rn, e, n), k, ALU.is_gt)
+            scan(A("cum2", o, o + n), A("ones", 0, n), A("cmp", o, o + n), ALU.mult, ALU.add)
+        tt(A("acc", 2, 3 * na, 3), A("cs", 97, 97 + na), A("x4", 15, 16 * na, 16), ALU.subtract)
+        tt(A("acc", 64 + 3 * na + 2, 64 + 3 * L, 3), A("cum2", n - 1, o + n, n), A("x4", 16 * na + 15, n, 16), ALU.subtract)
+        scan(A("acc", 64, 64 + 3 * na), A("z3", 0, 3 * na), A("acc", 0, 3 * na), ALU.mult, ALU.add)
+        cp(A("ru", 0, L), A("acc", 66, 64 + 3 * L, 3))
+        return A("ru", 0, L)
+
+    def best(n, r, lvl):
+        cp(A("sel", 0, n), IND(A("selt", 0, n), r))
+        scan(A("pre", 0, n), A("ones", 0, n), A("sel", 0, n), ALU.mult, ALU.add)
+        for m in range(7):
+            lo, hi = window(n, m)
+            if m in ONV:
+                o = A("cnt", 120 * (m - 4), 120 * (m - 4) + hi - lo)
+                ts(o, A("pre", lo, hi), col("cs", kP + m), ALU.is_gt, 2.0, ALU.mult)
+                red(col("acc", 48 + m), o)
+            else:
+                act(A("junk", N2 * m, N2 * m + hi - lo), A("pre", lo, hi), AF.Sign, bias=col("cs", kB + m), acc=col("acc", 48 + m))
+        tt(A("acc", 56, 63), A("acc", 48, 55), A("cs", 48 + 8 * lvl, 55 + 8 * lvl), ALU.add)
+        return A("acc", 56, 63)
+
+    def si(k, o=0, st=1):
+        return A("si", NS * k + o, NS * k + NS, st)
+
+    def sf(k, o=0, st=1):
+        return A("sf", NS * k + o, NS * k + NS, st)
+
+    def J(n, k, o=1, st=2, w=224):
+        k = k % 2 if n == "jp" else (k and 1 + k % 2) if n == "jn" else k % 3
+        return A(n, 256 * k + o, 256 * k + w, st)
+
+    def finish(h, b):
+        r, k = A("rl", C * b + H * h, C * b + H * h + H), b % 3
+        act(r, A("ps", 512 * k, 512 * k + H), AF.Relu, scale=0.015625)
+        tt(A("xt", 768 * h + b, 768 * h + 768, 4), A("ps", 512 * (3 + k), 512 * (3 + k) + H), r, ALU.add)
+
+    def half_layer(t, h):
+        zq, zs = A("zq%d" % t, H * h, H * h + H), A("zs%d" % t, H * h, H * h + H)
+        for b in range(4):
+            mm(b % 3, A("wq", 128 * b, 128 * b + 128), A("wsc", 128 * b, 128 * b + 128), zq, zs)
+            mm(3 + b % 3, A("eq", 128 * b, 128 * b + 128), A("es", 128 * b, 128 * b + 128), zq, zs)
+            finish(h, b)
+        qz(A("xq", H * h, H * h + H), A("xs", H * h, H * h + H), A("xt", 768 * h, 768 * h + 768))
+
+    def scores(h, k0):
+        lo, hi = H * h, H * h + H
+        for k in range(2):
+            mm(k0 + k, A("u2q", 128 * k, 128 * k + 128), A("u2s", 128 * k, 128 * k + 128), A("xq", lo, hi), A("xs", lo, hi))
+        tt(A("sl", lo, hi), A("ps", 512 * k0, 512 * k0 + H), A("cap", lo, hi), ALU.min)
+        tt(A("sr", lo, hi), A("ps", 512 * k0 + 512, 512 * k0 + 512 + H), A("cap", 1 + lo, 1 + hi), ALU.min)
+        tt(A("pm", lo, hi), A("sl", lo, hi), A("sr", lo, hi), ALU.max)
+        tt(A("w", lo // 2, hi // 2), A("pm", lo, hi, 2), A("pm", lo + 1, hi, 2), ALU.max)
+        tt(A("x1", lo // 2, hi // 2), A("w", lo // 2, hi // 2), A("lm", lo // 2, hi // 2), ALU.max)
+
+    def store(h):
+        lo, hi = H * h, H * h + H
+        mm(6 + h, A("vq"), A("vs"), A("xq", lo, hi), A("xs", lo, hi))
+        dma("a", [A("xq", lo, hi)], [], T.oc[:, 4 * lo:4 * hi], T.xq[:, lo:hi].bitcast(dt.uint8))
+        cp(A("yo", lo, hi), A("ps", 512 * (6 + h), 512 * (6 + h) + H))
+        dma("s", [A("yo", lo, hi)], [], T.y[:, lo:hi], T.yo[:, lo:hi])
+
+    for k in range(2):
+        mm(k, A("u2q", 128 * k, 128 * k + 128), A("u2s", 128 * k, 128 * k + 128), A("xq"), A("xs"))
+    act(A("sl", 0, C), A("ps", 0, C))
+    tt(A("pm", 0, C), A("ps", 512, 512 + C), A("sl", 0, C), ALU.max)
+    act(A("sr", 0, C), A("ps", 512, 512 + C))
+    tt(A("w"), A("pm", 0, C, 2), A("pm", 1, C, 2), ALU.max)
+    tt(A("x1", 0, N1), A("w"), A("lm", 0, N1), ALU.max)
+    for t in range(3):
+        x = best(N1, ranks(N1, "w", NA[0]), 0)
+        for k in range(2):
+            l = A("l3", 8 * k, 8 * k + 7)
+            ts(l, x, -1.0, ALU.mult, float(k), ALU.add)
+            act(A("r2", k, 224, 2), IND(A("pm"), l))
+            tt(A("x1", k, 224, 2), IND(A("pm"), l), A("lm", k, 224, 2), ALU.max)
+        behind = [A("l3", 0, 7)] if t else []
+        iota(A("inv"), [[0, 784]], 225, 0, behind)
+        iota(A("tn", 0, C), [[1025, C]], 0, 0, behind)
+        iota(A("tl", 0, C), [[0, C]], 0, 0, behind)
+        r = ranks(N2, "r2", NA[1])
+        for k in range(2):
+            act(A("i2", k, 224, 2), IND(A("ik"), A("l3", 8 * k, 8 * k + 7)))
+        x = best(N2, r, 1)
+        ts(A("l3", 16, 23), x, -0.5, ALU.mult)
+        cp(A("i3"), IND(A("i2"), A("l3", 16, 23)))
+        d = to_d("js", A("i3"), NS, 7 * NS)
+        l = A("l3", 24, 31)
+        ts(l, d, corr, ALU.subtract)
+        for k, n in enumerate(("sl", "sr")):
+            act(A("r3", k, 224, 2), IND(A(n), l))
+            tt(A("x1", k, 224, 2), IND(A(n), l), A("lm", k, 224, 2), ALU.max)
+        r = ranks(N2, "r3", NA[2])
+        for k, n in enumerate(("pkl", "pkr") if t else ("cpl", "cpr")):
+            act(A("k2", k, 224, 2), IND(A(n), l))
+        cp(IND(A("ew"), r), A("k2", 0, N2))
+        for b in range(4):
+            mm(4 + b, A("eq", 128 * b, 128 * b + 128), A("es", 128 * b, 128 * b + 128), A("xq"), A("xs"))
+            act(A("dx", C * b, C * b + C), A("ps", 512 * (4 + b), 512 * (4 + b) + C), scale=0.5)
+        d = to_d("js", A("ew", 0, NS), NS, 8 * NS)
+        pi, ei, oi_ = A("di", 0, 7), A("di", 8, 15), A("di", 16, 23)
+        PK, PE, TO, PO, MI, TT, DD = [si(k) for k in range(7)]
+        a_, mx, df, mb, ab, rh, cc, cc2, nc, nm, tv, gv = [sf(k) for k in range(12)]
+        ts(A("du", 0, 7), d, col("cs", 4), ALU.subtract, 1.0 / 1024, ALU.mult)
+        ts(pi, d, corr, ALU.subtract)
+        cp(PK, A("ew", 0, NS))
+        ts(ei, pi, 10, ALU.logical_shift_right)
+        ts(oi_, pi, 1023, ALU.bitwise_and)
+        cp(A("du", 8, 15), oi_)
+        cp(IND(A("inv"), A("du", 0, 7)), A("rx"))
+        act(J("jp", 0), IND(A("inv"), A("du", 8, 15)))
+        act(cc, J("jp", 0), bias=56 * 2.0 ** 18 + 2.0 ** 17, scale=-2.0 ** 16)
+        ts(PE, PK, 10, ALU.logical_shift_right)
+        ts(PO, PK, 1023, ALU.bitwise_and)
+        tt(df, PO, PE, ALU.subtract)
+        act(ab, df, AF.Abs, scale=256.0)
+        act(J("ja", 0), ab, bias=256.0)
+        d = to_d("js", J("jp", 0), NS)
+        tt(mx, PE, PO, ALU.min)
+        ts(A("du", 16, 23), d, corr, ALU.subtract)
+        act(J("jn", 0), mx, scale=512.0)
+        act(A("jn2"), mx, scale=512.0)
+        ts(TO, PK, 1023, ALU.bitwise_and, 1, ALU.logical_shift_right)
+        ts(cc2, cc, 1.5 * 2.0 ** 41, ALU.add, 1.5 * 2.0 ** 41, ALU.subtract)
+        tt(mb, TO, J("ja", 0), ALU.add)
+        tt(J("jm", 0), cc2, mb, ALU.add)
+        act(A("f1", 1, 224, 2), J("ja", 0), scale=-1.0 / 512)
+        act(A("h1", 2, 336, 3), df, AF.Relu, scale=-0.5)
+        act(a_, mx, scale=0.5)
+        lc = A("du", 64, 71)
+        ts(A("df", 0, 7), d, corr, ALU.subtract, 225.0, ALU.is_equal)
+        tt(A("df", 8, 15), ei, oi_, ALU.is_lt)
+        tt(A("di", 24, 31), ei, oi_, ALU.min)
+        tt(A("df", 16, 23), A("df", 8, 15), A("df", 0, 7), ALU.max)
+        ts(A("di", 32, 39), A("di", 24, 31), 1, ALU.logical_shift_right)
+        tt(A("df", 24, 31), A("di", 32, 39), jl, ALU.subtract)
+        tt(A("df", 48, 55), A("df", 16, 23), jk, ALU.min)
+        tt(A("df", 32, 39), A("df", 24, 31), A("df", 48, 55), ALU.mult)
+        tt(A("df", 40, 47), A("df", 32, 39), jl, ALU.add)
+        cp(lc, A("df", 40, 47))
+        for k in range(6):
+            l = A("du", 16 + 8 * k, 23 + 8 * k)
+            if k < 5:
+                act(J("jp", k + 1), IND(J("jp", k, 0, 1, 226), l))
+                act(A("ja2"), J("ja", k))
+                d = to_d("js", J("jp", k + 1), NS, (k + 1) * NS)
+                ts(A("du", 24 + 8 * k, 31 + 8 * k), d, corr, ALU.subtract)
+                tt(J("ja", k + 1), IND(J("ja", k, 0, 1, 226), l), A("ja2"), ALU.add)
+            tt(J("jn", k + 1), IND(J("jn", k, 0, 1, 226), l), A("jn2"), ALU.min)
+            if k < 5:
+                act(A("jn2"), J("jn", k + 1))
+            act(A("jy", 224 * k + 1, 224 * k + 224, 2), J("jm", k))
+            act(A("jy", 224 * k, 224 * k + 224, 2), IND(J("jm", k, 0, 1, 226), l))
+            scan(J("jm", k + 1, 0, 1), J("ja", k, 0, 1), A("jy", 224 * k, 224 * k + 224), ALU.add, ALU.min)
+        cp(MI, J("jm", 6))
+        for j in range(2):
+            tt(sf(9, j, 2), J("jn", 6, 1, 4), J("jn", 6, 3, 4), ALU.min)
+        tt(A("f0", 1, 224, 2), J("jn", 0), nm, ALU.is_equal)
+        tt(nc, J("jm", 6), A("pn"), ALU.is_lt)
+        ts(DD, MI, 9, ALU.logical_shift_right, 511, ALU.bitwise_and)
+        ts(TT, MI, 511, ALU.bitwise_and)
+        for k in range(2):
+            tt(A("h1", 3 * k + 1, 336, 6), si(6, 1 - k, 2), sf(8, k, 2), ALU.mult)
+            tt(A("h0", 3 * k + 1, 336, 6), si(5, 1 - k, 2), si(5, k, 2), ALU.is_ge)
+        d = to_d("js", nm, NS, 6 * NS)
+        Lf = A("f1", 0, 224, 2)
+        tt(Lf, DD, A("h1", 1, 336, 3), ALU.add)
+        act(A("h1", 0, 336, 3), Lf, bias=0.5, scale=-1.0)
+        ts(A("du", 72, 79), d, corr7, ALU.subtract, 1.0 / 1024, ALU.mult)
+        scan(A("f2"), A("f0"), A("f1"), ALU.mult, ALU.add)
+        cp(IND(A("tl"), lc), A("f2", 1, 224, 2))
+        scan(A("h2"), A("h0"), A("h1"), ALU.mult, ALU.add)
+        scan(A("cum", 8, 8 + C), A("tl", 0, C), A("one"), ALU.add, ALU.add)
+        act(rh, A("h2", 2, 336, 3), AF.Abs)
+        act(A("tg", 0, C), A("cum", 7, 7 + C))
+        tt(tv, nm, a_, ALU.add)
+        tt(gv, IND(A("cum", 0, 392), A("du", 72, 79)), rh, ALU.add)
+        cp(IND(A("tn"), lc), tv)
+        cp(IND(A("tg"), lc), gv)
+        pos = A("du", 80, 104)
+        if t:
+            act(A("gr", 0, H), IND(A("tg", 0, C), A("cu", 40, 52)))
+            cp(A("gr", H, C), IND(A("tg", 0, C), A("cu", 52, 64)))
+            scan(A("vr"), A("hc"), A("tn", 0, C), ALU.add, ALU.min)
+            d = to_d("sc", A("gr"), C)
+            gi, pa, db = A("di", 64, 88), A("di", 96, 120), A("di", 128, 152)
+            ts(gi, d, corr, ALU.subtract, 2.0, ALU.mult)
+            ts(pa, d, col("cs", 5), ALU.subtract)
+            ts(db, gi, 1, ALU.bitwise_and)
+            tt(A("df", 64, 88), pa, A("kd", 0, 24), ALU.add)
+            tt(A("df", 96, 120), db, A("kd", 32, 56), ALU.mult)
+            tt(A("df", 128, 152), A("df", 64, 88), A("df", 96, 120), ALU.subtract)
+            cp(pos, A("df", 128, 152))
+        else:
+            ts(pos, to_d("sc", A("tg", 0, C), C), col("cs", 5), ALU.subtract)
+        cp(IND(A("vw", 0, C), pos), A("vr") if t else A("tn", 0, C))
+        v1, p1 = A("di", 160, 184), A("di", 192, 216)
+        d = to_d("sc", A("vw", 0, C), C)
+        d2 = to_d("sc2", A("vw", 1, C + 1), C)
+        ts(v1, d, corr, ALU.subtract)
+        tt(A("df", 96, 120), d2, d, ALU.subtract)
+        ts(p1, v1, 511, ALU.bitwise_and)
+        ts(A("df", 128, 152), A("df", 96, 120), 512.0, ALU.is_lt)
+        cp(A("pl", 0, 24), p1)
+        tt(A("df", 160, 184), A("df", 96, 120), A("df", 128, 152), ALU.mult)
+        cp(A("ns", 24 * t, 24 * t + 24), A("df", 128, 152))
+        tt(A("df", 192, 216), A("df", 160, 184), p1, ALU.add)
+        cp(A("pl", 24, 48), A("df", 192, 216))
+        send(A("ns", 24 * t + 12, 24 * t + 24), A("nl%d" % t), "n", t, False)
+        for h in (1, 0):
+            for b in range(4):
+                w, o = A("dx", C * b, C * b + C), A("y1", C * b + H * h, C * b + H * h + H)
+                act(o, IND(w, A("pl", 12 * h, 12 * h + 12)))
+                tt(A("yt", 768 * h + b, 768 * h + 768, 4), IND(w, A("pl", 24 + 12 * h, 36 + 12 * h)), o, ALU.add)
+            if h:
+                sq, ss = A("sq", H * t, H * t + H), A("ss", H * t, H * t + H)
+                qz(sq, ss, A("yt", 768, 1536))
+                send(sq, A("zq%d" % t, H, C), "c", t, True)
+                send(ss, A("zs%d" % t, H, C), "s", t, False)
+            else:
+                qz(A("zq%d" % t, 0, H), A("zs%d" % t, 0, H), A("yt", 0, 768))
+        act(A("fb", 8, 8 + H), IND(A("w01"), A("ns", 24 * t, 24 * t + 12)))
+        act(A("fb", 8 + H, 8 + C), IND(A("w01"), A("nl%d" % t)))
+        ms(col("fb", 7 + H), 0.0)
+        half_layer(t, 0)
+        if t < 2:
+            tables()
+            scores(0, 6)
+            half_layer(t, 1)
+            scores(1, 0)
+        else:
+            store(0)
+            cp(A("oi"), A("vw", 0, C))
+            ts(A("oi"), A("oi"), 511, ALU.bitwise_and)
+            cp(A("of"), A("oi"))
+            dma("s", [fk], [], T.ol[:, C:2 * C], T.fb[0:128:16, 8:8 + C])
+            dma("s", [A("of")], [], T.ol[:, 0:C], T.of[0:128:16, :])
+            half_layer(t, 1)
+            store(1)
+    for k in range(4):
+        dma("s" if k % 2 else "a", [A("xs")], [], T.osc[4 * k:4 * k + 4, :], T.xs[32 * k:32 * k + 4, :])
+    issue()

@@ -2,11 +2,14 @@ import numpy as np
 from concourse.mybir import dt, AluOpType as ALU, ActivationFunctionType as AF, AxisListType as AX
 
 C, H, K2, NS = 384, 192, 104, 112
-N1, N2 = 192, 208
+N1, N2 = 256, 320
+WN = 880
+BIG = 2.0 ** 20
 STEP = [1, 2, 1]
-WAKE, FAR = 100.0, 3000.0
-LOOK = {"v": 0.0, "a": 150.0, "p": 0.0, "g": 300.0, "s": 0.0, "r": 0.0}
-NA = (6, 6, 6)
+WAKE, FAR, CYC = 200.0, 3000.0, 0.83
+LOOK = {"v": 60.0, "a": 150.0, "p": 0.0, "g": 300.0, "s": 0.0, "r": 0.0}
+NA = (7, 9)
+ONV = (5, 6)
 F, B, I, U, Q, S8 = "float32", "bfloat16", "int32", "uint16", "float8_e4m3fn_x4", "uint8"
 
 
@@ -15,31 +18,32 @@ def _sb(n, d):
 
 
 SCRATCH = {
-    "xin": _sb(1536, B), "uin": _sb(512, B), "vin": _sb(512, B), "ein": _sb(2048, B), "ones": _sb(N2, B), "on5": _sb(512, B),
-    "xt": _sb(1536, B), "yt": _sb(1536, B), "dx": _sb(1536, B), "y1": _sb(1536, B), "rl": _sb(1536, F),
+    "xin": _sb(1544, B), "uin": _sb(512, B), "vin": _sb(512, B), "ein": _sb(2048, B), "ones": _sb(N2, B), "on5": _sb(512, B),
+    "xt": _sb(1536, B), "yt": _sb(1536, B), "wn": _sb(4 * WN, B), "gj": _sb(4 * NS, F), "rl": _sb(1536, F),
     "wq": _sb(512, Q), "wsc": _sb(512, S8), "uq": _sb(128, Q), "us": _sb(128, S8), "vq": _sb(128, Q), "vs": _sb(128, S8),
     "u2q": _sb(256, Q), "u2s": _sb(256, S8), "eq": _sb(512, Q), "es": _sb(512, S8),
-    "xq": _sb(C, Q), "xs": _sb(C, S8), "sq": _sb(3 * H, Q), "ss": _sb(3 * H, S8),
+    "xq": _sb(C + 2, Q), "xs": _sb(C + 2, S8), "xq2": _sb(C, Q), "xs2": _sb(C, S8), "sq": _sb(3 * H, Q), "ss": _sb(3 * H, S8),
     "zq0": _sb(C, Q), "zq1": _sb(C, Q), "zq2": _sb(C, Q), "zs0": _sb(C, S8), "zs1": _sb(C, S8), "zs2": _sb(C, S8),
-    "nl0": _sb(12, U), "nl1": _sb(12, U), "nl2": _sb(12, U), "ns": _sb(72, U),
+    "nl0": _sb(12, U), "nl1": _sb(12, U), "nl2": _sb(12, U), "pl": _sb(96, U),
     "ps": ("psum", [128, 4096], F),
-    "t16": _sb(C, F), "lm": _sb(224, F), "c0": _sb(N2, F), "z0": _sb(N2, B), "cv": _sb(C, F), "cv2": _sb(C, F), "ik": _sb(392, F),
-    "selt": _sb(N2, B), "cpl": _sb(392, F), "cpr": _sb(392, F), "cpv": _sb(C, F), "rx": _sb(NS, F), "pn": _sb(NS, F), "pn0": _sb(NS, F),
-    "one": _sb(C, F), "cs": _sb(128, F), "ci": _sb(8, I), "cu": _sb(64, U), "w01": _sb(16, F), "z3": _sb(24, F), "lm0": _sb(224, F),
-    "fb": _sb(400, F), "fr": _sb(C, F), "fc": _sb(C, F), "kr": _sb(C, F), "pkl": _sb(392, F), "pkr": _sb(392, F), "cap": _sb(392, F),
-    "hc": _sb(C, F), "kd": _sb(64, F), "sc": _sb(C, F), "sc2": _sb(C, F), "sc3": _sb(C, F), "dk": _sb(64, I),
-    "sl": _sb(392, F), "sr": _sb(392, F), "pm": _sb(392, F), "w": _sb(N1, F), "x1": _sb(224, F), "x2": _sb(N2, F), "x3": _sb(N2, B), "x4": _sb(N2, B),
-    "cmp": _sb(8 * N2, B), "cum2": _sb(8 * N2, B), "tau": _sb(8 * N2, B), "junk": _sb(4 * N2, B), "acc": _sb(112, F), "ru": _sb(16, U),
-    "sel": _sb(N2, B), "pre": _sb(N2, B), "cnt": _sb(3 * 120, B), "l3": _sb(32, U), "r2": _sb(224, F), "r3": _sb(224, F),
-    "i2": _sb(224, F), "i3": _sb(NS, F), "k2": _sb(224, F), "ew": _sb(N2, F),
-    "di": _sb(256, I), "df": _sb(256, F), "du": _sb(160, U), "inv": _sb(784, F),
-    "jp": _sb(512, F), "ja": _sb(768, F), "jm": _sb(768, F), "jn": _sb(768, F), "jy": _sb(6 * 224, F), "js": _sb(9 * NS, F),
-    "f0": _sb(224, F), "f1": _sb(224, F), "f2": _sb(224, F), "h0": _sb(336, F), "h1": _sb(336, F), "h2": _sb(336, F),
-    "ja2": _sb(NS, F), "jn2": _sb(NS, F), "si": _sb(8 * NS, I), "sf": _sb(13 * NS, F),
-    "tl": _sb(504, F), "tn": _sb(504, F), "tg": _sb(504, F), "cum": _sb(400, F), "vr": _sb(C, F), "gr": _sb(C, F),
-    "vw": _sb(392, F), "pl": _sb(72, U), "oi": _sb(C, I), "of": _sb(C, F), "yo": _sb(C, F),
+    "t16": _sb(C, F), "lm": _sb(336, F), "lm0": _sb(336, F), "c0": _sb(N2, F), "zr": _sb(N2, B), "c3": _sb(C, F),
+    "cv": _sb(C, F), "cv2": _sb(C, F), "ik": _sb(776, F), "alt": _sb(WN, F),
+    "selt": _sb(N1, B), "cpk": _sb(776, F), "cpv": _sb(C, F), "rx": _sb(NS, F), "pn": _sb(NS, F), "pn0": _sb(NS, F), "jc": _sb(NS, F),
+    "cs": _sb(224, F), "ci": _sb(8, I), "cu": _sb(64, U), "z3": _sb(30, F),
+    "fb": _sb(400, F), "fr": _sb(C, F), "fc": _sb(C, F), "kr": _sb(C, F), "pk": _sb(776, F), "cap": _sb(392, F),
+    "hc": _sb(C, F), "onp": _sb(C, F), "onn": _sb(C, F), "kd": _sb(160, F), "sc": _sb(C, F), "sc2": _sb(C, F), "sc3": _sb(C, F), "dk": _sb(128, I),
+    "sr": _sb(776, F), "w3": _sb(768, F), "x1": _sb(336, F), "x2": _sb(N2, F), "x3": _sb(N2, B), "x4": _sb(N2, B),
+    "cmp": _sb(12 * N2, B), "cum2": _sb(12 * N2, B), "tau": _sb(10 * N2, B), "junk": _sb(4 * N2, B), "acc": _sb(128, F), "ru": _sb(32, U),
+    "sel": _sb(N1, B), "pre": _sb(N1, B), "cnt": _sb(3 * 168, B), "l3": _sb(24, U), "r3": _sb(336, F), "k2": _sb(336, F), "ew": _sb(N2, F),
+    "di": _sb(64, I), "df": _sb(256, F), "du": _sb(160, U), "inv": _sb(784, F),
+    "jp": _sb(512, F), "ja": _sb(768, F), "jm": _sb(1024, F), "jn": _sb(768, F), "jy": _sb(6 * 224, F), "js": _sb(10 * NS, F),
+    "tz": _sb(336, F), "t1": _sb(336, F), "t2": _sb(336, F), "vz": _sb(336, F), "v1": _sb(336, F), "v2": _sb(336, F),
+    "nz": _sb(224, F), "n1": _sb(224, F), "n2": _sb(224, F), "q1": _sb(224, F), "q2": _sb(224, F),
+    "si": _sb(4 * NS, I), "sf": _sb(13 * NS, F),
+    "tl": _sb(520, F), "cum": _sb(800, F), "v0": _sb(520, F), "qs": _sb(C, F),
+    "vw": _sb(C, F), "of": _sb(C, F), "yo": _sb(C, F),
 }
-SEMAPHORES = (["v", "a", "p", "g"] + ["d%d" % i for i in range(1, 25)]
+SEMAPHORES = (["v", "a", "p", "g"] + ["d%d" % i for i in range(1, 30)]
               + ["%s%d" % (n, t) for n in ("ln", "lc", "ls", "rn", "rc", "rs") for t in range(3)])
 
 
@@ -106,19 +110,21 @@ def rank_program(g, core, T, topo):
         for x in w2:
             lastw[x[0]][x[1]:x[2]:x[3]] = me
         need.discard(-1)
+        need.discard(me)
         ops.append((e, sorted(need), call, sem, inc, busy, lat))
 
-    def run(e, rd, wr, call, per=1.0):
+    def run(e, rd, wr, call, per=1.0, more=0.0):
         x = rd[0] if rd else wr[0]
+        n = len(range(*wr[0][1:])) if wr[0][0] != "*" else len(range(*x[1:]))
         if wr[0][0] == "*":
-            c = 50 + 3.5 * len(range(*x[1:]))
+            c = 50 + 3.8 * CYC * n
         elif x[0] == "*":
-            c = 55 + 1.5 * len(range(*wr[0][1:]))
+            c = (50 if e == "v" else 65) + 1.56 * CYC * n
         elif e in "va":
-            c = max(64, per * len(range(*x[1:])))
+            c = max(64, per * len(range(*x[1:]))) * CYC
         else:
-            c = 150 + 2 * len(range(*wr[0][1:])) if e == "g" else 0.6 * (16 + len(range(*wr[0][1:])))
-        note(e, rd, wr, lambda s: call().then_inc(T.sem[s], 1), e, 1, c, c)
+            c = 130 + 2 * CYC * n if e == "g" else per * CYC * (16 + n)
+        note(e, rd, wr, lambda s: call().then_inc(T.sem[s], 1), e, 1, c + more, c + more)
 
     def issue():
         n = len(ops)
@@ -174,8 +180,8 @@ def rank_program(g, core, T, topo):
     def ms(o, c):
         run("v", [], [o], lambda: g.vector.memset(ap(o), c), half(o))
 
-    def scan(o, a, b, op0, op1):
-        run("v", [a, b], [o], lambda: g.vector.tensor_tensor_scan(ap(o), ap(a), ap(b), 0.0, op0, op1), half(o, a, b))
+    def scan(o, a, b, op0, op1, first=0.0):
+        run("v", [a, b, first], [o], lambda: g.vector.tensor_tensor_scan(ap(o), ap(a), ap(b), ap(first), op0, op1), half(o, a, b))
 
     def red(o, a):
         run("v", [a], [o], lambda: g.vector.tensor_reduce(ap(o), ap(a), AX.X, ALU.add))
@@ -189,7 +195,7 @@ def rank_program(g, core, T, topo):
         if acc is not None:
             kw["accum_out"] = ap(acc)
         fn = f if f is not None else (AF.Copy if bias is None and acc is None else AF.Identity)
-        run("a", [a, bias], [o] + ([acc] if acc else []), lambda: g.scalar.activation(ap(o), ap(a), fn, **kw))
+        run("a", [a, bias], [o] + ([acc] if acc else []), lambda: g.scalar.activation(ap(o), ap(a), fn, **kw), 1.0, 20.0 if acc else 0.0)
 
     def iota(o, pat, base, cm=0, behind=()):
         if SCRATCH[o[0]][2] == I:
@@ -198,11 +204,17 @@ def rank_program(g, core, T, topo):
             run("g", list(behind), [o], lambda: g.iota(ap(o), pat, base, cm, allow_small_or_imprecise_dtypes=True))
 
     def qz(oq, os_, a):
-        run("v", [a], [oq, os_], lambda: g.vector.quantize_mx(ap(oq), ap(os_), ap(a)), 0.23)
+        run("v", [a], [oq, os_], lambda: g.vector.quantize_mx(ap(oq), ap(os_), ap(a)), 0.27)
 
-    def mm(b, wq, ws, xq, xs):
+    def mm(b, wq, ws, xq, xs, xq2=None, xs2=None):
         o = A("ps", 512 * b, 512 * b + xq[2] - xq[1])
-        run("p", [wq, ws, xq, xs], [o], lambda: g.tensor.matmul_mx(ap(o), ap(wq), ap(ws), ap(xq), ap(xs), True, True))
+
+        def call():
+            if xq2 is None:
+                return g.tensor.matmul_mx(ap(o), ap(wq), ap(ws), ap(xq), ap(xs), True, True)
+            g.tensor.matmul_mx(ap(o), ap(wq), ap(ws), ap(xq), ap(xs), True, False)
+            return g.tensor.matmul_mx(ap(o), ap(wq), ap(ws), ap(xq2), ap(xs2), False, True)
+        run("p", [wq, ws, xq, xs, xq2, xs2], [o], call, 1.0 if xq2 is None else 2.0)
 
     def dma(e, rd, wr, out, in_, lat=2500.0):
         nd[0] += 1
@@ -221,54 +233,56 @@ def rank_program(g, core, T, topo):
         scan(A(tmp, lo, lo + n), A("cv", 0, n), src, ALU.add, ALU.max)
         return A(tmp, lo + 15, lo + n, 16)
 
-    qf, q1, corr, corr7, kD, kB, kP = col("cs", 0), col("cs", 1), col("cs", 2), col("cs", 3), A("cs", 8, 32), 32, 40
-    jk, jl = A("cs", 72, 79), A("cs", 64, 71)
-    ONV = (4, 5, 6)
+    qf, q1, corr = col("cs", 0), col("cs", 1), col("cs", 2)
+    c14, c384, c512, c225, chalf, corr2 = [col("cs", 3 + k) for k in range(5)] + [col("cs", 39)]
+    kD, kB, kP = A("cs", 8, 32), 32, 40
+    jl2, padv, k1D, i16, km, k2D, ce = A("cs", 56, 63), A("cs", 64, 71), A("cs", 72, 96), A("cs", 96, 120), A("cs", 120, 144), A("cs", 144, 168), 168
 
-    def window(n, m):
-        w = n - K2 + 16
-        lo = min(16 * m, n - w)
+    def window(m):
+        w = N1 - K2 + 16
+        lo = min(16 * m, N1 - w)
         return lo, lo + w
 
     dma("a", [], [A("uin")], T.uin[:], T.u[:])
     dma("s", [], [A("xin", 0, 768)], T.xin[:, 0:768], T.x[:, 0:768], 3000.0)
     dma("a", [], [A("xin", 768, 1536)], T.xin[:, 768:1536], T.x[:, 768:1536], 3500.0)
+    dma("s", [], [A("xin", 1536, 1544)], T.xin[:, 1536:1544], T.x[:, 0:8])
     iota(col("ci", 0), [[0, 1]], 0, 1)
-    iota(A("cs", 96, 120), [[16, 24]], 0)
+    iota(i16, [[16, 24]], 0)
     iota(A("t16"), [[0, 24], [1, 16]], 0)
-    iota(A("ik"), [[1, 392]], 0)
     ms(A("ones"), 1.0)
     ms(A("c0"), 0.0)
-    ms(A("z0"), 1.0)
+    ms(A("zr"), -1e4)
+    ms(A("c3"), 0.0)
     cp(A("cu", 0, 8), A("cs", 96, 104))
     ts(A("cu", 8, 16), A("cs", 96, 104), 1.0, ALU.add)
     ts(col("ci", 1), col("ci", 0), 15, ALU.bitwise_and)
     ms(A("c0", 0, N2, 16), 5e29)
+    ms(A("c3", 0, C, 3), -3e29)
     cp(qf, col("ci", 1))
-    ms(A("z0", 0, N2, 16), 0.0)
+    ms(A("zr", 0, N2, 16), -128.0)
     ts(q1, qf, 1.0, ALU.add)
     ts(corr, qf, 15.0, ALU.is_lt, 2.0 ** 21, ALU.mult)
-    ts(kD, A("cs", 96, 120), qf, ALU.add)
+    ts(kD, i16, qf, ALU.add)
     ms(A("selt", 0, K2), 1.0)
-    ms(A("selt", K2, N2), 0.0)
+    ms(A("selt", K2, N1), 0.0)
     ts(A("cs", kP, kP + 7), A("cs", 8, 15), 0.5, ALU.add)
     ts(A("cs", kB, kB + 7), A("cs", 8, 15), 0.5, ALU.add, -1.0, ALU.mult)
-    ts(A("lm0"), A("t16", 0, 224), qf, ALU.not_equal, 8e29, ALU.mult)
+    ts(A("lm0"), A("t16", 0, 336), qf, ALU.not_equal, 8e29, ALU.mult)
     act(A("lm"), A("lm0"), bias=-3e29)
-    ms(A("z3", 0, 24, 3), 0.0)
-    ms(A("z3", 1, 24, 3), -1.0)
-    ms(A("z3", 2, 24, 3), 1.0)
-    for n in ("pm", "sl", "sr"):
-        ms(A(n, C, 392), -2e29)
-    for k, n in enumerate((N1, N2)):
-        for m in range(7):
-            lo, hi = window(n, m)
-            ms(col("cs", 48 + 8 * k + m), float(-2 * lo - (hi - lo) * (2 if m in ONV else 1)))
+    ms(A("z3", 0, 30, 3), 0.0)
+    ms(A("z3", 1, 30, 3), -1.0)
+    ms(A("z3", 2, 30, 3), 1.0)
+    ms(A("sr", 768, 776), -2e29)
+    ts(A("cs", ce, ce + 10), A("cs", 97, 107), 128.0, ALU.add)
+    for m in range(7):
+        lo, hi = window(m)
+        ms(col("cs", 48 + m), float(-2 * lo - (hi - lo) * (2 if m in ONV else 1)))
     qz(A("uq"), A("us"), A("uin"))
 
     def repeat_u(k):
         o, w, l = A("u2q", 128 * k, 128 * k + 128), A("uq"), A("cu", 8 * k, 8 * k + 8)
-        run("v", [w, l], [o], lambda: g.vector.tensor_copy(ap(o).bitcast(dt.uint32), ap(w).bitcast(dt.uint32).indirect(ap(l))), 2.0)
+        run("v", [IND(w, l)], [o], lambda: g.vector.tensor_copy(ap(o).bitcast(dt.uint32), ap(w).bitcast(dt.uint32).indirect(ap(l))))
         act(A("u2s", 128 * k, 128 * k + 128), IND(A("us"), l))
 
     def unpacker(b):
@@ -277,103 +291,126 @@ def rank_program(g, core, T, topo):
 
     repeat_u(0)
     repeat_u(1)
-    for h in range(2):
-        qz(A("xq", H * h, H * h + H), A("xs", H * h, H * h + H), A("xin", 768 * h, 768 * h + 768))
+    qz(A("xq", 0, H), A("xs", 0, H), A("xin", 0, 768))
+    qz(A("xq", H, C + 2), A("xs", H, C + 2), A("xin", 768, 1544))
     dma("s", [A("xin")], [A("wq")], T.wq[:].bitcast(dt.uint8), T.wc[:])
     dma("s", [A("xin")], [A("wsc")], T.wsc[:], T.ws[:])
     dma("s", [A("xin")], [A("vin")], T.vin[:], T.v[:])
     ts(A("cv"), A("t16"), qf, ALU.is_equal, -2.0 ** 22, ALU.mult)
     ts(A("cv2"), A("t16"), q1, ALU.is_equal, 2.0 ** 21, ALU.mult)
     tt(A("cv"), A("cv"), A("cv2"), ALU.add)
-    iota(A("cpr"), [[2050, 392]], 1024)
-    iota(A("cpl"), [[2050, 392]], 1)
+    iota(A("cpk"), [[2050, 388], [1023, 2]], 1)
     iota(A("rx", 0, K2), [[4, 52], [-2, 2]], 3)
     iota(A("ja", 0, 768, 2), [[0, 384]], 2 ** 24 - 1)
     iota(A("jp"), [[0, 512]], 225)
-    iota(A("jn"), [[0, 768]], 1024000)
-    iota(A("f0", 0, 224, 2), [[0, NS]], 0)
-    iota(A("h0"), [[0, NS], [1, 3]], -1)
-    ms(A("h0", 0, 336, 3), 0.0)
+    iota(A("jn"), [[0, 768]], 1000000)
     iota(A("pn0"), [[-1, 56], [0, 2]], 56)
+    iota(A("jc"), [[2, 56], [0, 2]], 769)
     iota(A("on5"), [[0, 512]], 1)
     for b in range(4):
         unpacker(b)
-    iota(A("one"), [[0, C]], 1)
+        iota(A("wn", WN * b, WN * b + WN), [[0, WN]], 0)
+    for n in ("tz", "vz"):
+        iota(A(n, 0, 336, 3), [[0, NS]], 0)
+    iota(A("nz", 0, 224, 2), [[0, NS]], 0)
+    iota(A("n1", 0, 224, 2), [[0, NS]], 800)
+    iota(A("cum"), [[0, 800]], -512)
+    iota(A("tl"), [[0, 520]], 0)
+    iota(A("v0"), [[2, 520]], 0)
+    iota(A("onp"), [[0, C]], 1)
+    iota(A("onn"), [[0, C]], -1)
+    iota(A("ik"), [[1, 776]], 0)
+    iota(A("alt"), [[0, WN // 2], [1, 2]], 0)
     iota(A("cpv"), [[-2050, C]], 2050 * (C - 1) + 1)
     qz(A("eq"), A("es"), A("ein"))
     act(A("pn"), A("pn0"), scale=2.0 ** 18)
     ms(A("rx", K2, NS), 225.0)
     ms(A("ja", 225, 768, 256), 0.0)
-    ms(A("jm", 224, 768, 256), 2.0 ** 24)
-    ms(A("jm", 225, 768, 256), 2.0 ** 24)
+    ms(A("jm", 224, 1024, 256), 2.0 ** 24)
+    ms(A("jm", 225, 1024, 256), 2.0 ** 24)
     ms(A("jm", 0, 224, 2), 0.0)
-    ts(jk, A("cs", 8, 15), 104.0, ALU.is_lt)
-    ts(jl, A("cs", 8, 15), 392.0, ALU.add)
-    ts(corr7, corr, -7.0 * 1024, ALU.add)
-    ts(col("cs", 4), corr, 384.0, ALU.add)
-    ts(col("cs", 5), corr, 0.25, ALU.add)
-    ms(A("cum", 0, 8), 0.0)
-    ms(A("vw", C, 392), 2.0 ** 20)
-    ms(A("w01", 0, 1), 0.0)
-    ms(A("w01", 1, 16), 1.0)
+    ts(jl2, A("cs", 8, 15), 2.0, ALU.mult, 802.0, ALU.add)
+    ts(A("cs", 184, 191), A("cs", 8, 15), 104.0, ALU.is_ge)
+    tt(padv, A("cs", 184, 191), jl2, ALU.mult)
+    for c, v in ((c14, -14.0), (c384, 384.0), (c512, 512.0), (c225, 225.0), (chalf, 0.5)):
+        ts(c, corr, v, ALU.add)
+    ts(corr2, corr, 2.0, ALU.mult)
+    ts(k1D, kD, 1.0, ALU.add)
+    ts(km, kD, float(H - 1), ALU.not_equal)
+    ts(k2D, kD, 2.0, ALU.mult)
+    klc = A("kd", 0, 24)
+    ts(klc, kD, 0.0, ALU.mult, corr2, ALU.add)
+    ts(klc, klc, 1.0, ALU.add)
     ms(A("fb", 0, 8), 0.0)
-    ms(A("pkl", C, 392), 0.0)
-    ms(A("pkr", C, 392), 0.0)
+    ms(A("pk", 768, 776), 0.0)
     ts(A("cu", 16, 40), kD, -1.0, ALU.mult, 383.0, ALU.add)
     qz(A("vq"), A("vs"), A("vin"))
 
     fp, fk = A("fb", 7, 7 + C), A("fb", 8, 8 + C)
     rev = A("cu", 16, 40)
 
-    def tables():
+    def tables(t):
         act(A("cap", 0, C + 1), A("fb", 7, 8 + C), bias=1e29, scale=-2e29)
         act(A("fc"), fp, bias=2.0 ** 21, scale=2048.0 - 2.0 ** 21)
         act(A("fr"), IND(fk, rev), bias=-2.0 ** 21, scale=2.0 ** 21 - 2048.0)
-        scan(A("pkr", 0, C), A("fc"), A("cpr", 0, C), ALU.add, ALU.min)
-        d = to_d("sc3", A("pkr", 0, C), C)
+        pkr = A("pk", 1, 768, 2)
+        scan(pkr, A("fc"), A("cpk", 1, 768, 2), ALU.add, ALU.min)
+        d = to_d("sc3", pkr, C)
         ts(A("dk", 0, 24), d, corr, ALU.subtract)
         scan(A("kr"), A("fr"), A("cpv"), ALU.add, ALU.max)
         ts(A("dk", 32, 56), A("dk", 0, 24), 1023, ALU.bitwise_and, 1, ALU.logical_shift_right)
-        tt(A("kd", 0, 24), kD, A("dk", 32, 56), ALU.subtract)
-        cp(A("cu", 40, 64), A("dk", 32, 56))
-        ts(A("kd", 32, 56), A("kd", 0, 24), 2.0, ALU.mult)
-        act(A("pkl", 0, C), IND(A("kr"), rev))
-        act(A("hc"), fp, bias=2.0 ** 20, scale=1.0 - 2.0 ** 20)
+        tt(A("kd", 32, 56), k1D, A("dk", 32, 56), ALU.subtract)
+        cp(A("dk", 64, 76), A("pl", 32 * t, 32 * t + 12))
+        cp(A("dk", 76, 88), A("nl%d" % t))
+        ts(A("dk", 96, 120), A("dk", 64, 88), 1, ALU.bitwise_and)
+        tt(A("kd", 64, 88), A("dk", 96, 120), km, ALU.mult)
+        tt(A("kd", 96, 120), A("kd", 64, 88), A("kd", 32, 56), ALU.mult)
+        tt(A("kd", 128, 152), A("kd", 32, 56), A("kd", 96, 120), ALU.subtract)
+        ts(klc, A("kd", 128, 152), corr2, ALU.add)
+        tt(A("kd", 32, 56), A("kd", 64, 88), k2D, ALU.add)
+        cp(A("cu", 40, 64), A("kd", 32, 56))
+        act(A("v0", 0, C), IND(A("ik"), A("cu", 40, 64)))
+        act(A("pk", 0, 768, 2), IND(A("kr"), rev))
+        act(A("hc"), fp, bias=2 * BIG, scale=1.0 - 2 * BIG)
+        act(A("onp"), fk, bias=1.0, scale=BIG)
+        act(A("onn"), fk, bias=-1.0, scale=-BIG)
+        act(A("tl", 7, 7 + C), fp, scale=-BIG)
 
-    def ranks(n, rn, na):
+    def ranks(n, rv, na):
         L = n // 16
         scan(A("x2", 0, n), A("c0", 0, n), A("x1", 0, n), ALU.add, ALU.min)
         for m in range(na):
             e, j = 16 * m + 16, N2 * (m % 4)
-            act(A("tau", m * n, m * n + n), A(rn, 0, n), AF.Sign, bias=col("x2", 16 * m + 15), scale=-1.0)
+            act(A("tau", m * n, m * n + n), rv(0, n), AF.Sign, bias=col("x2", 16 * m + 15), scale=-1.0)
             act(A("junk", j, j + e), A("tau", m * n, m * n + e), AF.Relu, acc=col("acc", 3 * m))
             act(A("junk", j + e, j + n), A("tau", m * n + e, m * n + n), AF.Relu, scale=-1.0, acc=col("acc", 3 * m + 1))
-        tt(A("x3", 0, n), A("x2", 0, n), A(rn, 0, n), ALU.is_equal)
-        scan(A("x4", 0, n), A("z0", 0, n), A("x3", 0, n), ALU.mult, ALU.add)
+        tt(A("x3", 0, n), A("x2", 0, n), rv(0, n), ALU.is_equal)
+        scan(A("x4", 0, n), A("zr", 0, n), A("x3", 0, n), ALU.max, ALU.subtract, -128.0)
         for m in range(na, L):
             k, e, o = col("x2", 16 * m + 15), 16 * m + 16, (m - na) * n
-            ts(A("cmp", o, o + e), A(rn, 0, e), k, ALU.is_ge)
+            ts(A("cmp", o, o + e), rv(0, e), k, ALU.is_ge)
             if e < n:
-                ts(A("cmp", o + e, o + n), A(rn, e, n), k, ALU.is_gt)
-            scan(A("cum2", o, o + n), A("ones", 0, n), A("cmp", o, o + n), ALU.mult, ALU.add)
-        tt(A("acc", 2, 3 * na, 3), A("cs", 97, 97 + na), A("x4", 15, 16 * na, 16), ALU.subtract)
-        tt(A("acc", 64 + 3 * na + 2, 64 + 3 * L, 3), A("cum2", n - 1, o + n, n), A("x4", 16 * na + 15, n, 16), ALU.subtract)
+                ts(A("cmp", o + e, o + n), rv(e, n), k, ALU.is_gt)
+            scan(A("cum2", o, o + n), A("ones", 0, n), A("cmp", o, o + n), ALU.mult, ALU.add, col("x4", 16 * m + 15))
+        tt(A("acc", 2, 3 * na, 3), A("cs", ce, ce + na), A("x4", 15, 16 * na, 16), ALU.add)
         scan(A("acc", 64, 64 + 3 * na), A("z3", 0, 3 * na), A("acc", 0, 3 * na), ALU.mult, ALU.add)
-        cp(A("ru", 0, L), A("acc", 66, 64 + 3 * L, 3))
+        cp(A("ru", 0, na), A("acc", 66, 64 + 3 * na, 3))
+        ts(A("ru", na, L), A("cum2", n - 1, o + n, n), 128.0, ALU.add)
         return A("ru", 0, L)
 
-    def best(n, r, lvl):
-        cp(A("sel", 0, n), IND(A("selt", 0, n), r))
-        scan(A("pre", 0, n), A("ones", 0, n), A("sel", 0, n), ALU.mult, ALU.add)
+    def best(r):
+        cp(A("sel"), IND(A("selt"), r))
+        scan(A("pre"), A("ones", 0, N1), A("sel"), ALU.mult, ALU.add)
         for m in range(7):
-            lo, hi = window(n, m)
+            lo, hi = window(m)
             if m in ONV:
-                o = A("cnt", 120 * (m - 4), 120 * (m - 4) + hi - lo)
+                o = A("cnt", 168 * (m - 4), 168 * (m - 4) + hi - lo)
                 ts(o, A("pre", lo, hi), col("cs", kP + m), ALU.is_gt, 2.0, ALU.mult)
                 red(col("acc", 48 + m), o)
             else:
-                act(A("junk", N2 * m, N2 * m + hi - lo), A("pre", lo, hi), AF.Sign, bias=col("cs", kB + m), acc=col("acc", 48 + m))
-        tt(A("acc", 56, 63), A("acc", 48, 55), A("cs", 48 + 8 * lvl, 55 + 8 * lvl), ALU.add)
+                j = N2 * (m % 4)
+                act(A("junk", j, j + hi - lo), A("pre", lo, hi), AF.Sign, bias=col("cs", kB + m), acc=col("acc", 48 + m))
+        tt(A("acc", 56, 63), A("acc", 48, 55), A("cs", 48, 55), ALU.add)
         return A("acc", 56, 63)
 
     def si(k, o=0, st=1):
@@ -386,6 +423,9 @@ def rank_program(g, core, T, topo):
         k = k % 2 if n == "jp" else (k and 1 + k % 2) if n == "jn" else k % 3
         return A(n, 256 * k + o, 256 * k + w, st)
 
+    def E(b):
+        return A("eq", 128 * b, 128 * b + 128), A("es", 128 * b, 128 * b + 128)
+
     def finish(h, b):
         r, k = A("rl", C * b + H * h, C * b + H * h + H), b % 3
         act(r, A("ps", 512 * k, 512 * k + H), AF.Relu, scale=0.015625)
@@ -395,19 +435,21 @@ def rank_program(g, core, T, topo):
         zq, zs = A("zq%d" % t, H * h, H * h + H), A("zs%d" % t, H * h, H * h + H)
         for b in range(4):
             mm(b % 3, A("wq", 128 * b, 128 * b + 128), A("wsc", 128 * b, 128 * b + 128), zq, zs)
-            mm(3 + b % 3, A("eq", 128 * b, 128 * b + 128), A("es", 128 * b, 128 * b + 128), zq, zs)
+            mm(3 + b % 3, *E(b), zq, zs)
             finish(h, b)
         qz(A("xq", H * h, H * h + H), A("xs", H * h, H * h + H), A("xt", 768 * h, 768 * h + 768))
 
-    def scores(h, k0):
+    def scores(h, k0, capped):
         lo, hi = H * h, H * h + H
         for k in range(2):
             mm(k0 + k, A("u2q", 128 * k, 128 * k + 128), A("u2s", 128 * k, 128 * k + 128), A("xq", lo, hi), A("xs", lo, hi))
-        tt(A("sl", lo, hi), A("ps", 512 * k0, 512 * k0 + H), A("cap", lo, hi), ALU.min)
-        tt(A("sr", lo, hi), A("ps", 512 * k0 + 512, 512 * k0 + 512 + H), A("cap", 1 + lo, 1 + hi), ALU.min)
-        tt(A("pm", lo, hi), A("sl", lo, hi), A("sr", lo, hi), ALU.max)
-        tt(A("w", lo // 2, hi // 2), A("pm", lo, hi, 2), A("pm", lo + 1, hi, 2), ALU.max)
-        tt(A("x1", lo // 2, hi // 2), A("w", lo // 2, hi // 2), A("lm", lo // 2, hi // 2), ALU.max)
+            o, p = A("sr", 2 * lo + k, 2 * hi, 2), A("ps", 512 * (k0 + k), 512 * (k0 + k) + H)
+            if capped:
+                tt(o, p, A("cap", k + lo, k + hi), ALU.min)
+            else:
+                (cp if k else act)(o, p)
+        scan(A("w3", 2 * lo, 2 * hi), A("c3"), A("sr", 2 * lo, 2 * hi), ALU.add, ALU.max)
+        tt(A("x1", 128 * h, 128 * h + 128), A("w3", 2 * lo + 2, 2 * hi, 3), A("lm", 0, 128), ALU.max)
 
     def store(h):
         lo, hi = H * h, H * h + H
@@ -416,48 +458,34 @@ def rank_program(g, core, T, topo):
         cp(A("yo", lo, hi), A("ps", 512 * (6 + h), 512 * (6 + h) + H))
         dma("s", [A("yo", lo, hi)], [], T.y[:, lo:hi], T.yo[:, lo:hi])
 
-    for k in range(2):
-        mm(k, A("u2q", 128 * k, 128 * k + 128), A("u2s", 128 * k, 128 * k + 128), A("xq"), A("xs"))
-    act(A("sl", 0, C), A("ps", 0, C))
-    tt(A("pm", 0, C), A("ps", 512, 512 + C), A("sl", 0, C), ALU.max)
-    act(A("sr", 0, C), A("ps", 512, 512 + C))
-    tt(A("w"), A("pm", 0, C, 2), A("pm", 1, C, 2), ALU.max)
-    tt(A("x1", 0, N1), A("w"), A("lm", 0, N1), ALU.max)
+    scores(0, 0, False)
+    scores(1, 2, False)
     for t in range(3):
-        x = best(N1, ranks(N1, "w", NA[0]), 0)
-        for k in range(2):
+        x = best(ranks(N1, lambda a, b: A("w3", 3 * a + 2, 3 * b, 3), NA[0]))
+        for k in range(3):
             l = A("l3", 8 * k, 8 * k + 7)
-            ts(l, x, -1.0, ALU.mult, float(k), ALU.add)
-            act(A("r2", k, 224, 2), IND(A("pm"), l))
-            tt(A("x1", k, 224, 2), IND(A("pm"), l), A("lm", k, 224, 2), ALU.max)
-        behind = [A("l3", 0, 7)] if t else []
-        iota(A("inv"), [[0, 784]], 225, 0, behind)
-        iota(A("tn", 0, C), [[1025, C]], 0, 0, behind)
-        iota(A("tl", 0, C), [[0, C]], 0, 0, behind)
-        r = ranks(N2, "r2", NA[1])
-        for k in range(2):
-            act(A("i2", k, 224, 2), IND(A("ik"), A("l3", 8 * k, 8 * k + 7)))
-        x = best(N2, r, 1)
-        ts(A("l3", 16, 23), x, -0.5, ALU.mult)
-        cp(A("i3"), IND(A("i2"), A("l3", 16, 23)))
-        d = to_d("js", A("i3"), NS, 7 * NS)
-        l = A("l3", 24, 31)
-        ts(l, d, corr, ALU.subtract)
-        for k, n in enumerate(("sl", "sr")):
-            act(A("r3", k, 224, 2), IND(A(n), l))
-            tt(A("x1", k, 224, 2), IND(A(n), l), A("lm", k, 224, 2), ALU.max)
-        r = ranks(N2, "r3", NA[2])
-        for k, n in enumerate(("pkl", "pkr") if t else ("cpl", "cpr")):
-            act(A("k2", k, 224, 2), IND(A(n), l))
+            ts(l, x, -1.5, ALU.mult, float(k), ALU.add)
+            act(A("r3", k, 336, 3), IND(A("sr"), l))
+            tt(A("x1", k, 336, 3), IND(A("sr"), l), A("lm", k, 336, 3), ALU.max)
+        iota(A("inv"), [[0, 784]], 225, 0, [A("l3", 0, 7)] if t else [])
+        r = ranks(N2, lambda a, b: A("r3", a, b), NA[1])
+        for k in range(3):
+            act(A("k2", k, 336, 3), IND(A("pk" if t else "cpk"), A("l3", 8 * k, 8 * k + 7)))
         cp(IND(A("ew"), r), A("k2", 0, N2))
+        if t:
+            dma("s", [A("xq")], [A("xq2")], T.xq2[:].bitcast(dt.uint8), T.xq[:, 1:C + 1].bitcast(dt.uint8))
+            dma("s", [A("xs")], [A("xs2")], T.xs2[:], T.xs[:, 1:C + 1])
         for b in range(4):
-            mm(4 + b, A("eq", 128 * b, 128 * b + 128), A("es", 128 * b, 128 * b + 128), A("xq"), A("xs"))
-            act(A("dx", C * b, C * b + C), A("ps", 512 * (4 + b), 512 * (4 + b) + C), scale=0.5)
+            mm(4 + b, *E(b), A("xq", 0, C), A("xs", 0, C))
+            act(A("wn", WN * b, WN * b + 2 * C, 2), A("ps", 512 * (4 + b), 512 * (4 + b) + C))
+            if t:
+                mm(b, *E(b), A("xq", 0, C), A("xs", 0, C), A("xq2"), A("xs2"))
+                act(A("wn", WN * b + 1, WN * b + 2 * C, 2), A("ps", 512 * b, 512 * b + C), scale=0.5)
         d = to_d("js", A("ew", 0, NS), NS, 8 * NS)
         pi, ei, oi_ = A("di", 0, 7), A("di", 8, 15), A("di", 16, 23)
-        PK, PE, TO, PO, MI, TT, DD = [si(k) for k in range(7)]
-        a_, mx, df, mb, ab, rh, cc, cc2, nc, nm, tv, gv = [sf(k) for k in range(12)]
-        ts(A("du", 0, 7), d, col("cs", 4), ALU.subtract, 1.0 / 1024, ALU.mult)
+        PK, PE, PO, LF = [si(k) for k in range(4)]
+        dd, ab, cc, cc2, mb, hi, ncl, gv, mc = [sf(k) for k in range(9)]
+        ts(A("du", 0, 7), d, c384, ALU.subtract, 1.0 / 1024, ALU.mult)
         ts(pi, d, corr, ALU.subtract)
         cp(PK, A("ew", 0, NS))
         ts(ei, pi, 10, ALU.logical_shift_right)
@@ -466,108 +494,100 @@ def rank_program(g, core, T, topo):
         cp(IND(A("inv"), A("du", 0, 7)), A("rx"))
         act(J("jp", 0), IND(A("inv"), A("du", 8, 15)))
         act(cc, J("jp", 0), bias=56 * 2.0 ** 18 + 2.0 ** 17, scale=-2.0 ** 16)
-        ts(PE, PK, 10, ALU.logical_shift_right)
-        ts(PO, PK, 1023, ALU.bitwise_and)
-        tt(df, PO, PE, ALU.subtract)
-        act(ab, df, AF.Abs, scale=256.0)
-        act(J("ja", 0), ab, bias=256.0)
+        ts(PE, PK, 10, ALU.logical_shift_right, 1022, ALU.bitwise_and)
+        ts(PO, PK, 1022, ALU.bitwise_and)
+        ts(LF, PK, 1, ALU.bitwise_and)
+        tt(dd, PO, PE, ALU.subtract)
+        act(ab, dd, AF.Abs, scale=0.5)
+        act(J("ja", 0), ab, bias=1.0)
         d = to_d("js", J("jp", 0), NS)
-        tt(mx, PE, PO, ALU.min)
+        tt(J("jn", 0), PE, PO, ALU.min)
         ts(A("du", 16, 23), d, corr, ALU.subtract)
-        act(J("jn", 0), mx, scale=512.0)
-        act(A("jn2"), mx, scale=512.0)
-        ts(TO, PK, 1023, ALU.bitwise_and, 1, ALU.logical_shift_right)
+        cp(A("v1", 2, 336, 3), PO)
+        act(mc, A("v1", 2, 336, 3), bias=512.0, scale=256.0)
         ts(cc2, cc, 1.5 * 2.0 ** 41, ALU.add, 1.5 * 2.0 ** 41, ALU.subtract)
-        tt(mb, TO, J("ja", 0), ALU.add)
+        tt(mb, mc, J("ja", 0), ALU.add)
         tt(J("jm", 0), cc2, mb, ALU.add)
-        act(A("f1", 1, 224, 2), J("ja", 0), scale=-1.0 / 512)
-        act(A("h1", 2, 336, 3), df, AF.Relu, scale=-0.5)
-        act(a_, mx, scale=0.5)
-        lc = A("du", 64, 71)
-        ts(A("df", 0, 7), d, corr, ALU.subtract, 225.0, ALU.is_equal)
-        tt(A("df", 8, 15), ei, oi_, ALU.is_lt)
-        tt(A("di", 24, 31), ei, oi_, ALU.min)
-        tt(A("df", 16, 23), A("df", 8, 15), A("df", 0, 7), ALU.max)
-        ts(A("di", 32, 39), A("di", 24, 31), 1, ALU.logical_shift_right)
-        tt(A("df", 24, 31), A("di", 32, 39), jl, ALU.subtract)
-        tt(A("df", 48, 55), A("df", 16, 23), jk, ALU.min)
-        tt(A("df", 32, 39), A("df", 24, 31), A("df", 48, 55), ALU.mult)
-        tt(A("df", 40, 47), A("df", 32, 39), jl, ALU.add)
-        cp(lc, A("df", 40, 47))
+        act(A("t1", 2, 336, 3), ab, bias=-1.0, scale=-1.0)
+        act(A("v1", 1, 336, 3), dd, scale=-1.0)
+        tt(A("v1", 0, 336, 3), A("jc"), PE, ALU.subtract)
+        ts(A("di", 24, 31), pi, 10, ALU.logical_shift_right, 1022, ALU.bitwise_and)
+        cp(A("du", 104, 111), A("di", 24, 31))
+        for b in range(4):
+            act(A("gj", NS * b, NS * b + NS), IND(A("wn", WN * b, WN * b + WN), A("du", 104, 111)), scale=0.5)
+            tt(A("wn", WN * b + 769, WN * b + WN, 2), A("gj", NS * b, NS * b + NS, 2), A("gj", NS * b + 1, NS * b + NS, 2), ALU.add)
+        lc, dn, mxp = A("du", 64, 71), A("df", 8, 15), A("df", 56, 63)
+        ts(A("df", 0, 7), d, c225, ALU.not_equal)
+        tt(dn, A("df", 0, 7), jl2, ALU.mult)
+        tt(A("df", 16, 23), ei, oi_, ALU.is_gt)
+        tt(A("df", 24, 31), dn, A("df", 16, 23), ALU.mult)
+        tt(A("df", 32, 39), ei, oi_, ALU.min)
+        tt(A("df", 40, 47), A("df", 32, 39), padv, ALU.max)
+        tt(A("df", 48, 55), A("df", 40, 47), A("df", 24, 31), ALU.max)
+        ts(lc, A("df", 48, 55), 0.5, ALU.mult, 7.0, ALU.add)
+        tt(A("df", 64, 71), ei, oi_, ALU.max)
+        tt(mxp, A("df", 64, 71), padv, ALU.max)
         for k in range(6):
             l = A("du", 16 + 8 * k, 23 + 8 * k)
             if k < 5:
                 act(J("jp", k + 1), IND(J("jp", k, 0, 1, 226), l))
-                act(A("ja2"), J("ja", k))
                 d = to_d("js", J("jp", k + 1), NS, (k + 1) * NS)
                 ts(A("du", 24 + 8 * k, 31 + 8 * k), d, corr, ALU.subtract)
-                tt(J("ja", k + 1), IND(J("ja", k, 0, 1, 226), l), A("ja2"), ALU.add)
-            tt(J("jn", k + 1), IND(J("jn", k, 0, 1, 226), l), A("jn2"), ALU.min)
-            if k < 5:
-                act(A("jn2"), J("jn", k + 1))
+                act(sf(9 + k % 2), J("ja", k))
+                tt(J("ja", k + 1), IND(J("ja", k, 0, 1, 226), l), sf(9 + k % 2), ALU.add)
+            act(sf(11 + k % 2), J("jn", k))
+            tt(J("jn", k + 1), IND(J("jn", k, 0, 1, 226), l), sf(11 + k % 2), ALU.min)
             act(A("jy", 224 * k + 1, 224 * k + 224, 2), J("jm", k))
             act(A("jy", 224 * k, 224 * k + 224, 2), IND(J("jm", k, 0, 1, 226), l))
             scan(J("jm", k + 1, 0, 1), J("ja", k, 0, 1), A("jy", 224 * k, 224 * k + 224), ALU.add, ALU.min)
-        cp(MI, J("jm", 6))
+        m, nm, nc, cb, neg = J("jm", 6), A("n1", 1, 224, 2), A("tz", 1, 336, 3), A("vz", 2, 336, 3), A("nz", 1, 224, 2)
         for j in range(2):
-            tt(sf(9, j, 2), J("jn", 6, 1, 4), J("jn", 6, 3, 4), ALU.min)
-        tt(A("f0", 1, 224, 2), J("jn", 0), nm, ALU.is_equal)
-        tt(nc, J("jm", 6), A("pn"), ALU.is_lt)
-        ts(DD, MI, 9, ALU.logical_shift_right, 511, ALU.bitwise_and)
-        ts(TT, MI, 511, ALU.bitwise_and)
-        for k in range(2):
-            tt(A("h1", 3 * k + 1, 336, 6), si(6, 1 - k, 2), sf(8, k, 2), ALU.mult)
-            tt(A("h0", 3 * k + 1, 336, 6), si(5, 1 - k, 2), si(5, k, 2), ALU.is_ge)
-        d = to_d("js", nm, NS, 6 * NS)
-        Lf = A("f1", 0, 224, 2)
-        tt(Lf, DD, A("h1", 1, 336, 3), ALU.add)
-        act(A("h1", 0, 336, 3), Lf, bias=0.5, scale=-1.0)
-        ts(A("du", 72, 79), d, corr7, ALU.subtract, 1.0 / 1024, ALU.mult)
-        scan(A("f2"), A("f0"), A("f1"), ALU.mult, ALU.add)
-        cp(IND(A("tl"), lc), A("f2", 1, 224, 2))
-        scan(A("h2"), A("h0"), A("h1"), ALU.mult, ALU.add)
-        scan(A("cum", 8, 8 + C), A("tl", 0, C), A("one"), ALU.add, ALU.add)
-        act(rh, A("h2", 2, 336, 3), AF.Abs)
-        act(A("tg", 0, C), A("cum", 7, 7 + C))
-        tt(tv, nm, a_, ALU.add)
-        tt(gv, IND(A("cum", 0, 392), A("du", 72, 79)), rh, ALU.add)
-        cp(IND(A("tn"), lc), tv)
-        cp(IND(A("tg"), lc), gv)
-        pos = A("du", 80, 104)
+            tt(A("n1", 1 + 2 * j, 224, 4), J("jn", 6, 1, 4), J("jn", 6, 3, 4), ALU.min)
+        tt(A("tz", 2, 336, 3), J("jn", 0), nm, ALU.is_equal)
+        ts(hi, m, 2.0 ** 32 - 256.0, ALU.add, 2.0 ** 32, ALU.subtract)
+        tt(nc, m, A("pn"), ALU.is_lt)
+        tt(A("t1", 1, 336, 3), m, hi, ALU.subtract)
+        for j in range(2):
+            tt(A("t1", 3 * j, 336, 6), J("jm", 6, 3 - 2 * j, 4), sf(5, 1 - j, 2), ALU.subtract)
+            tt(A("vz", 2 + 3 * j, 336, 6), J("jm", 6, 3 - 2 * j, 4), J("jm", 6, 1 + 2 * j, 4), ALU.is_gt if j else ALU.is_ge)
+        scan(A("t2"), A("tz"), A("t1"), ALU.mult, ALU.add)
+        cp(IND(A("tl"), lc), A("t2", 2, 336, 3))
+        ms(col("cum", 7), 512.0)
+        scan(A("cum", 8, 8 + C), A("onp"), A("tl", 7, 7 + C), ALU.add, ALU.add, 512.0)
+        scan(A("cum", 408, 408 + C), A("onn"), A("tl", 7, 7 + C), ALU.add, ALU.subtract, -512.0)
+        tt(neg, cb, LF, ALU.is_equal)
+        scan(A("n2"), A("nz"), A("n1"), ALU.mult, ALU.add)
+        d = to_d("js", A("n2", 1, 224, 2), NS, 6 * NS)
+        ts(A("du", 72, 79), d, c14, ALU.subtract, 0.5, ALU.mult)
+        tt(ncl, nc, LF, ALU.mult)
+        tt(A("q1", 1, 224, 2), A("t1", 0, 336, 3), ncl, ALU.mult)
+        act(A("q1", 0, 224, 2), A("t2", 1, 336, 3), bias=2.0, scale=-1.0)
+        scan(A("q2"), A("nz"), A("q1"), ALU.mult, ALU.add)
+        tt(gv, IND(A("cum"), A("du", 72, 79)), A("q2", 1, 224, 2), ALU.add)
+        cp(IND(A("cum", 0, 520), lc), gv)
+        act(A("vz", 1, 336, 3), nc)
+        scan(A("v2"), A("vz"), A("v1"), ALU.mult, ALU.add)
+        d = to_d("js", cb, NS, 7 * NS)
+        ts(A("df", 72, 79), d, chalf, ALU.is_lt)
+        tt(A("df", 80, 87), A("df", 72, 79), dn, ALU.mult)
+        tt(A("df", 88, 95), A("df", 80, 87), mxp, ALU.max)
+        ts(A("du", 112, 119), A("df", 88, 95), 0.5, ALU.mult, -0.25, ALU.add)
+        cp(IND(A("v0"), A("du", 112, 119)), A("v2", 2, 336, 3))
         if t:
-            act(A("gr", 0, H), IND(A("tg", 0, C), A("cu", 40, 52)))
-            cp(A("gr", H, C), IND(A("tg", 0, C), A("cu", 52, 64)))
-            scan(A("vr"), A("hc"), A("tn", 0, C), ALU.add, ALU.min)
-            d = to_d("sc", A("gr"), C)
-            gi, pa, db = A("di", 64, 88), A("di", 96, 120), A("di", 128, 152)
-            ts(gi, d, corr, ALU.subtract, 2.0, ALU.mult)
-            ts(pa, d, col("cs", 5), ALU.subtract)
-            ts(db, gi, 1, ALU.bitwise_and)
-            tt(A("df", 64, 88), pa, A("kd", 0, 24), ALU.add)
-            tt(A("df", 96, 120), db, A("kd", 32, 56), ALU.mult)
-            tt(A("df", 128, 152), A("df", 64, 88), A("df", 96, 120), ALU.subtract)
-            cp(pos, A("df", 128, 152))
-        else:
-            ts(pos, to_d("sc", A("tg", 0, C), C), col("cs", 5), ALU.subtract)
-        cp(IND(A("vw", 0, C), pos), A("vr") if t else A("tn", 0, C))
-        v1, p1 = A("di", 160, 184), A("di", 192, 216)
-        d = to_d("sc", A("vw", 0, C), C)
-        d2 = to_d("sc2", A("vw", 1, C + 1), C)
-        ts(v1, d, corr, ALU.subtract)
-        tt(A("df", 96, 120), d2, d, ALU.subtract)
-        ts(p1, v1, 511, ALU.bitwise_and)
-        ts(A("df", 128, 152), A("df", 96, 120), 512.0, ALU.is_lt)
-        cp(A("pl", 0, 24), p1)
-        tt(A("df", 160, 184), A("df", 96, 120), A("df", 128, 152), ALU.mult)
-        cp(A("ns", 24 * t, 24 * t + 24), A("df", 128, 152))
-        tt(A("df", 192, 216), A("df", 160, 184), p1, ALU.add)
-        cp(A("pl", 24, 48), A("df", 192, 216))
-        send(A("ns", 24 * t + 12, 24 * t + 24), A("nl%d" % t), "n", t, False)
+            scan(A("qs"), A("hc"), A("cum", 7, 7 + C), ALU.add, ALU.min)
+        d = to_d("sc", A("qs") if t else A("cum", 7, 7 + C), C)
+        pos = A("du", 80, 104)
+        tt(A("df", 96, 120), klc, d, ALU.subtract)
+        tt(A("df", 128, 152), A("df", 96, 120), d, ALU.max)
+        ts(pos, A("df", 128, 152), c512, ALU.subtract)
+        cp(IND(A("vw"), pos), A("v0", 0, C))
         for h in (1, 0):
+            l = A("pl", 32 * t + 16 * h, 32 * t + 16 * h + 12)
+            ts(l, to_d("sc2", A("vw", H * h, H * h + H), H, H * h), corr, ALU.subtract)
+            if h:
+                send(l, A("nl%d" % t), "n", t, False)
             for b in range(4):
-                w, o = A("dx", C * b, C * b + C), A("y1", C * b + H * h, C * b + H * h + H)
-                act(o, IND(w, A("pl", 12 * h, 12 * h + 12)))
-                tt(A("yt", 768 * h + b, 768 * h + 768, 4), IND(w, A("pl", 24 + 12 * h, 36 + 12 * h)), o, ALU.add)
+                (act if b < 2 else cp)(A("yt", 768 * h + b, 768 * h + 768, 4), IND(A("wn", WN * b, WN * b + WN), l))
             if h:
                 sq, ss = A("sq", H * t, H * t + H), A("ss", H * t, H * t + H)
                 qz(sq, ss, A("yt", 768, 1536))
@@ -575,24 +595,26 @@ def rank_program(g, core, T, topo):
                 send(ss, A("zs%d" % t, H, C), "s", t, False)
             else:
                 qz(A("zq%d" % t, 0, H), A("zs%d" % t, 0, H), A("yt", 0, 768))
-        act(A("fb", 8, 8 + H), IND(A("w01"), A("ns", 24 * t, 24 * t + 12)))
-        act(A("fb", 8 + H, 8 + C), IND(A("w01"), A("nl%d" % t)))
+        act(A("fb", 8, 8 + H), IND(A("alt"), A("pl", 32 * t, 32 * t + 12)))
+        act(A("fb", 8 + H, 8 + C), IND(A("alt"), A("nl%d" % t)))
         ms(col("fb", 7 + H), 0.0)
         half_layer(t, 0)
         if t < 2:
-            tables()
-            scores(0, 6)
+            tables(t)
+            scores(0, 6, True)
             half_layer(t, 1)
-            scores(1, 0)
+            scores(1, 0, True)
         else:
             store(0)
-            cp(A("oi"), A("vw", 0, C))
-            ts(A("oi"), A("oi"), 511, ALU.bitwise_and)
-            cp(A("of"), A("oi"))
+            ts(A("df", 160, 184), d, -1.0, ALU.mult, corr2, ALU.add)
+            ts(A("df", 192, 216), A("df", 160, 184), 1.0, ALU.add)
+            tt(A("df", 224, 248), A("df", 192, 216), d, ALU.max)
+            ts(A("du", 128, 152), A("df", 224, 248), c512, ALU.subtract)
+            cp(IND(A("of"), A("du", 128, 152)), A("ik", 0, C))
             dma("s", [fk], [], T.ol[:, C:2 * C], T.fb[0:128:16, 8:8 + C])
             dma("s", [A("of")], [], T.ol[:, 0:C], T.of[0:128:16, :])
             half_layer(t, 1)
             store(1)
     for k in range(4):
-        dma("s" if k % 2 else "a", [A("xs")], [], T.osc[4 * k:4 * k + 4, :], T.xs[32 * k:32 * k + 4, :])
+        dma("s" if k % 2 else "a", [A("xs", 0, C)], [], T.osc[4 * k:4 * k + 4, :], T.xs[32 * k:32 * k + 4, 0:C])
     issue()

@@ -6,10 +6,12 @@ N1, N2 = 256, 320
 WN = 880
 BIG = 2.0 ** 20
 STEP = [1, 2, 1]
-WAKE, FAR, CYC = 200.0, 3000.0, 0.83
-LOOK = {"v": 60.0, "a": 150.0, "p": 0.0, "g": 300.0, "s": 0.0, "r": 0.0}
-NA = (7, 9)
-ONV = (5, 6)
+WAKE, FAR, CYC, PEC = 200.0, 3300.0, 0.83, 1.2
+LOOK = {"v": 250.0, "a": 300.0, "p": 0.0, "g": 300.0, "s": 0.0, "r": 0.0}
+TOL, TURNS = 40.0, 4
+NA = (7, 9, 9)
+YA = (2, 2)
+NB = 4
 F, B, I, U, Q, S8 = "float32", "bfloat16", "int32", "uint16", "float8_e4m3fn_x4", "uint8"
 
 
@@ -19,32 +21,33 @@ def _sb(n, d):
 
 SCRATCH = {
     "xin": _sb(1544, B), "uin": _sb(512, B), "vin": _sb(512, B), "ein": _sb(2048, B), "ones": _sb(N2, B), "on5": _sb(512, B),
-    "xt": _sb(1536, B), "yt": _sb(1536, B), "wn": _sb(4 * WN, B), "gj": _sb(4 * NS, F), "rl": _sb(1536, F),
+    "xt": _sb(1536, B), "yt": _sb(1536, B), "wn0": _sb(4 * WN, B), "wn1": _sb(4 * WN, B), "gj": _sb(8 * NS, B), "rl": _sb(1536, F),
     "wq": _sb(512, Q), "wsc": _sb(512, S8), "uq": _sb(128, Q), "us": _sb(128, S8), "vq": _sb(128, Q), "vs": _sb(128, S8),
     "u2q": _sb(256, Q), "u2s": _sb(256, S8), "eq": _sb(512, Q), "es": _sb(512, S8),
-    "xq": _sb(C + 2, Q), "xs": _sb(C + 2, S8), "xq2": _sb(C, Q), "xs2": _sb(C, S8), "sq": _sb(3 * H, Q), "ss": _sb(3 * H, S8),
-    "zq0": _sb(C, Q), "zq1": _sb(C, Q), "zq2": _sb(C, Q), "zs0": _sb(C, S8), "zs1": _sb(C, S8), "zs2": _sb(C, S8),
-    "nl0": _sb(12, U), "nl1": _sb(12, U), "nl2": _sb(12, U), "pl": _sb(96, U),
+    "xq": _sb(C + 2, Q), "xs": _sb(C + 2, S8), "xq2": _sb(2 * C, Q), "xs2": _sb(2 * C, S8), "zq": _sb(C, Q), "zs": _sb(C, S8),
+    "pq0": _sb(C + 2, Q), "pq1": _sb(C + 2, Q), "pq2": _sb(C + 2, Q), "pp0": _sb(C + 2, S8), "pp1": _sb(C + 2, S8), "pp2": _sb(C + 2, S8),
+    "sl0": _sb(8, U), "sl1": _sb(8, U), "sl2": _sb(8, U), "nl0": _sb(12, U), "nl1": _sb(12, U), "nl2": _sb(12, U), "pl": _sb(96, U),
     "ps": ("psum", [128, 4096], F),
-    "t16": _sb(C, F), "lm": _sb(336, F), "lm0": _sb(336, F), "c0": _sb(N2, F), "zr": _sb(N2, B), "c3": _sb(C, F),
+    "t16": _sb(C, F), "lm": _sb(336, F), "c0": _sb(N2, F), "zr": _sb(N2, B), "c3": _sb(C, F),
     "cv": _sb(C, F), "cv2": _sb(C, F), "ik": _sb(776, F), "alt": _sb(WN, F),
-    "selt": _sb(N1, B), "cpk": _sb(776, F), "cpv": _sb(C, F), "rx": _sb(NS, F), "pn": _sb(NS, F), "pn0": _sb(NS, F), "jc": _sb(NS, F),
-    "cs": _sb(224, F), "ci": _sb(8, I), "cu": _sb(64, U), "z3": _sb(30, F),
+    "selt": _sb(N1, B), "cpk": _sb(776, F), "cpv": _sb(C, F), "rx": _sb(NS, F), "pn": _sb(NS, F), "jc": _sb(NS, F),
+    "cs": _sb(224, F), "ci": _sb(8, I), "cu": _sb(64, U), "z4": _sb(48, F), "zj": _sb(NS, B),
+    "ac0": _sb(112, F), "ac1": _sb(112, F),
     "fb": _sb(400, F), "fr": _sb(C, F), "fc": _sb(C, F), "kr": _sb(C, F), "pk": _sb(776, F), "cap": _sb(392, F),
-    "hc": _sb(C, F), "onp": _sb(C, F), "onn": _sb(C, F), "kd": _sb(160, F), "sc": _sb(C, F), "sc2": _sb(C, F), "sc3": _sb(C, F), "dk": _sb(128, I),
+    "hc": _sb(C, F), "onp": _sb(C, F), "kd": _sb(160, F), "sc": _sb(C, F), "sc2": _sb(C, F), "sc3": _sb(C, F), "dk": _sb(128, I),
     "sr": _sb(776, F), "w3": _sb(768, F), "x1": _sb(336, F), "x2": _sb(N2, F), "x3": _sb(N2, B), "x4": _sb(N2, B),
-    "cmp": _sb(12 * N2, B), "cum2": _sb(12 * N2, B), "tau": _sb(10 * N2, B), "junk": _sb(4 * N2, B), "acc": _sb(128, F), "ru": _sb(32, U),
-    "sel": _sb(N1, B), "pre": _sb(N1, B), "cnt": _sb(3 * 168, B), "l3": _sb(24, U), "r3": _sb(336, F), "k2": _sb(336, F), "ew": _sb(N2, F),
+    "cmp": _sb(12 * N2, B), "cum2": _sb(12 * N2, B), "tau": _sb(11 * N2, B), "junk": _sb(4 * N2, B), "acc": _sb(128, F), "ru": _sb(32, U),
+    "sel": _sb(N1, B), "pre": _sb(N1, B), "cnt": _sb(4 * 168, B), "l3": _sb(24, U), "r3": _sb(336, F), "k2": _sb(336, F), "ew": _sb(N2, F),
     "di": _sb(64, I), "df": _sb(256, F), "du": _sb(160, U), "inv": _sb(784, F),
-    "jp": _sb(512, F), "ja": _sb(768, F), "jm": _sb(1024, F), "jn": _sb(768, F), "jy": _sb(6 * 224, F), "js": _sb(10 * NS, F),
+    "jp": _sb(8 * 128 + 512, B), "ja": _sb(768, F), "jm": _sb(1024, F), "jn": _sb(768, F), "jy": _sb(6 * 224, F), "js": _sb(3 * NS, F),
     "tz": _sb(336, F), "t1": _sb(336, F), "t2": _sb(336, F), "vz": _sb(336, F), "v1": _sb(336, F), "v2": _sb(336, F),
-    "nz": _sb(224, F), "n1": _sb(224, F), "n2": _sb(224, F), "q1": _sb(224, F), "q2": _sb(224, F),
-    "si": _sb(4 * NS, I), "sf": _sb(13 * NS, F),
-    "tl": _sb(520, F), "cum": _sb(800, F), "v0": _sb(520, F), "qs": _sb(C, F),
+    "nz": _sb(224, F), "n1": _sb(224, F), "n2": _sb(224, F), "qz": _sb(224, F), "q1": _sb(224, F), "q2": _sb(224, F),
+    "si": _sb(4 * NS, I), "sf": _sb(16 * NS, F),
+    "tl": _sb(520, F), "cum": _sb(520, F), "v0": _sb(520, F), "qs": _sb(C, F),
     "vw": _sb(C, F), "of": _sb(C, F), "yo": _sb(C, F),
 }
-SEMAPHORES = (["v", "a", "p", "g"] + ["d%d" % i for i in range(1, 30)]
-              + ["%s%d" % (n, t) for n in ("ln", "lc", "ls", "rn", "rc", "rs") for t in range(3)])
+SEMAPHORES = (["v", "a", "p", "g"] + ["d%d" % i for i in range(1, 34)]
+              + ["%s%d" % (n, t) for n in ("ln", "lc", "ls", "lj", "rn", "rc", "rs", "rj") for t in range(3)])
 
 
 def A(n, lo=0, hi=None, st=1):
@@ -126,30 +129,45 @@ def rank_program(g, core, T, topo):
             c = 130 + 2 * CYC * n if e == "g" else per * CYC * (16 + n)
         note(e, rd, wr, lambda s: call().then_inc(T.sem[s], 1), e, 1, c + more, c + more)
 
+    def plan(before, after, way, back):
+        n = len(ops)
+        left, ready, free = [len(x) for x in before], [ops[i][6] - ops[i][5] if back else 0.0 for i in range(n)], {e: 0.0 for e in list(eng) + ["r"]}
+        cand = {e: [i for i in range(n) if ops[i][0] == e and not left[i]] for e in free}
+        order, over = [], [0.0] * n
+        for _ in range(n):
+            now, e = min((max(free[e], min(ready[i] for i in c)), e) for e, c in cand.items() if c)
+            i = -max((way[i], -i) for i in cand[e] if ready[i] <= now + LOOK[e])[1]
+            fit = [(way[j], -j) for j in cand[e] if max(now, ready[j]) + ops[j][5] <= ready[i] + TOL]
+            if ready[i] > now and fit:
+                i = -max(fit)[1]
+            cand[e].remove(i)
+            now = max(now, ready[i])
+            free[e] = now + ops[i][5]
+            over[i] = now + ops[i][5 if back else 6]
+            order.append(i)
+            for j in after[i]:
+                ready[j] = max(ready[j], over[i] + WAKE + (ops[j][6] - ops[j][5] if back else 0.0))
+                left[j] -= 1
+                if not left[j]:
+                    cand[ops[j][0]].append(j)
+        return order, over
+
     def issue():
         n = len(ops)
-        after, way = [[] for _ in ops], [0.0] * n
+        before, after, way = [o[1] for o in ops], [[] for _ in ops], [0.0] * n
         for i, o in enumerate(ops):
             for d in o[1]:
                 after[d].append(i)
         for i in range(n - 1, -1, -1):
             way[i] = ops[i][6] + max([way[j] + WAKE for j in after[i]] + [0.0])
-        left, ready, free = [len(o[1]) for o in ops], [0.0] * n, {e: 0.0 for e in list(eng) + ["r"]}
-        cand = {e: [i for i in range(n) if ops[i][0] == e and not left[i]] for e in free}
-        tok, cnt, seen = [None] * n, {}, {e: {} for e in free}
-        for _ in range(n):
-            e = min((max(free[e], min(ready[i] for i in c)), e) for e, c in cand.items() if c)[1]
-            now = max(free[e], min(ready[i] for i in cand[e]))
-            i = -max((way[i], -i) for i in cand[e] if ready[i] <= now + LOOK[e])[1]
-            cand[e].remove(i)
-            now = max(now, ready[i])
-            _, need, call, sem, inc, busy, lat = ops[i]
-            free[e] = now + busy
-            for j in after[i]:
-                ready[j] = max(ready[j], now + lat + WAKE)
-                left[j] -= 1
-                if not left[j]:
-                    cand[ops[j][0]].append(j)
+        tries = []
+        for _ in range(TURNS):
+            order, over = plan(before, after, way, False)
+            tries.append((max(over), order))
+            way = plan(after, before, over, True)[1]
+        tok, cnt, seen = [None] * n, {}, {e: {} for e in eng}
+        for i in min(tries)[1]:
+            e, need, call, sem, inc = ops[i][:5]
             cnt[sem] = cnt.get(sem, 0) + inc
             tok[i] = (sem, cnt[sem])
             if e == "r":
@@ -186,7 +204,7 @@ def rank_program(g, core, T, topo):
     def red(o, a):
         run("v", [a], [o], lambda: g.vector.tensor_reduce(ap(o), ap(a), AX.X, ALU.add))
 
-    def act(o, a, f=None, bias=None, scale=None, acc=None):
+    def act(o, a, f=None, bias=None, scale=None, acc=None, behind=None):
         kw = {}
         if bias is not None:
             kw["bias"] = ap(bias)
@@ -195,7 +213,7 @@ def rank_program(g, core, T, topo):
         if acc is not None:
             kw["accum_out"] = ap(acc)
         fn = f if f is not None else (AF.Copy if bias is None and acc is None else AF.Identity)
-        run("a", [a, bias], [o] + ([acc] if acc else []), lambda: g.scalar.activation(ap(o), ap(a), fn, **kw), 1.0, 20.0 if acc else 0.0)
+        run("a", [a, bias, behind], [o] + ([acc] if acc else []), lambda: g.scalar.activation(ap(o), ap(a), fn, **kw), 1.0, 20.0 if acc else 0.0)
 
     def iota(o, pat, base, cm=0, behind=()):
         if SCRATCH[o[0]][2] == I:
@@ -206,7 +224,7 @@ def rank_program(g, core, T, topo):
     def qz(oq, os_, a):
         run("v", [a], [oq, os_], lambda: g.vector.quantize_mx(ap(oq), ap(os_), ap(a)), 0.27)
 
-    def mm(b, wq, ws, xq, xs, xq2=None, xs2=None):
+    def mm(b, wq, ws, xq, xs, xq2=None, xs2=None, behind=None):
         o = A("ps", 512 * b, 512 * b + xq[2] - xq[1])
 
         def call():
@@ -214,7 +232,7 @@ def rank_program(g, core, T, topo):
                 return g.tensor.matmul_mx(ap(o), ap(wq), ap(ws), ap(xq), ap(xs), True, True)
             g.tensor.matmul_mx(ap(o), ap(wq), ap(ws), ap(xq), ap(xs), True, False)
             return g.tensor.matmul_mx(ap(o), ap(wq), ap(ws), ap(xq2), ap(xs2), False, True)
-        run("p", [wq, ws, xq, xs, xq2, xs2], [o], call, 1.0 if xq2 is None else 2.0)
+        run("p", [wq, ws, xq, xs, xq2, xs2, behind], [o], call, PEC if xq2 is None else 2 * PEC)
 
     def dma(e, rd, wr, out, in_, lat=2500.0):
         nd[0] += 1
@@ -235,13 +253,8 @@ def rank_program(g, core, T, topo):
 
     qf, q1, corr = col("cs", 0), col("cs", 1), col("cs", 2)
     c14, c384, c512, c225, chalf, corr2 = [col("cs", 3 + k) for k in range(5)] + [col("cs", 39)]
-    kD, kB, kP = A("cs", 8, 32), 32, 40
+    kD, kB, kP, cb15 = A("cs", 8, 32), 32, 40, col("cs", 47)
     jl2, padv, k1D, i16, km, k2D, ce = A("cs", 56, 63), A("cs", 64, 71), A("cs", 72, 96), A("cs", 96, 120), A("cs", 120, 144), A("cs", 144, 168), 168
-
-    def window(m):
-        w = N1 - K2 + 16
-        lo = min(16 * m, N1 - w)
-        return lo, lo + w
 
     dma("a", [], [A("uin")], T.uin[:], T.u[:])
     dma("s", [], [A("xin", 0, 768)], T.xin[:, 0:768], T.x[:, 0:768], 3000.0)
@@ -268,16 +281,15 @@ def rank_program(g, core, T, topo):
     ms(A("selt", K2, N1), 0.0)
     ts(A("cs", kP, kP + 7), A("cs", 8, 15), 0.5, ALU.add)
     ts(A("cs", kB, kB + 7), A("cs", 8, 15), 0.5, ALU.add, -1.0, ALU.mult)
-    ts(A("lm0"), A("t16", 0, 336), qf, ALU.not_equal, 8e29, ALU.mult)
-    act(A("lm"), A("lm0"), bias=-3e29)
-    ms(A("z3", 0, 30, 3), 0.0)
-    ms(A("z3", 1, 30, 3), -1.0)
-    ms(A("z3", 2, 30, 3), 1.0)
+    ts(A("k2"), A("t16", 0, 336), qf, ALU.not_equal, 8e29, ALU.mult)
+    act(A("lm"), A("k2"), bias=-3e29)
+    ms(A("z4"), 1.0)
+    ms(A("z4", 0, 48, 4), 0.0)
+    ms(A("z4", 1, 48, 4), -1.0)
+    ms(A("ac0", 0, 48), 0.0)
+    ms(A("ac1", 0, 48), 0.0)
     ms(A("sr", 768, 776), -2e29)
-    ts(A("cs", ce, ce + 10), A("cs", 97, 107), 128.0, ALU.add)
-    for m in range(7):
-        lo, hi = window(m)
-        ms(col("cs", 48 + m), float(-2 * lo - (hi - lo) * (2 if m in ONV else 1)))
+    ts(A("cs", ce, ce + 12), A("cs", 97, 109), 128.0, ALU.add)
     qz(A("uq"), A("us"), A("uin"))
 
     def repeat_u(k):
@@ -300,31 +312,38 @@ def rank_program(g, core, T, topo):
     ts(A("cv2"), A("t16"), q1, ALU.is_equal, 2.0 ** 21, ALU.mult)
     tt(A("cv"), A("cv"), A("cv2"), ALU.add)
     iota(A("cpk"), [[2050, 388], [1023, 2]], 1)
-    iota(A("rx", 0, K2), [[4, 52], [-2, 2]], 3)
+    iota(A("rx", 0, K2), [[4, 52], [-2, 2]], 3 - 240)
     iota(A("ja", 0, 768, 2), [[0, 384]], 2 ** 24 - 1)
-    iota(A("jp"), [[0, 512]], 225)
+    iota(A("jp", 0, 512), [[0, 512]], -15)
+    ts(A("jp", 512, 512 + NS), A("t16", 0, NS), qf, ALU.is_equal, -1024.0, ALU.mult)
+    ts(A("jp", 640, 640 + NS), A("t16", 0, NS), q1, ALU.is_equal, 240.0, ALU.mult)
+    tt(A("jp", 512, 512 + NS), A("jp", 512, 512 + NS), A("jp", 640, 640 + NS), ALU.add)
+    ts(cb15, qf, 15.0, ALU.is_ge, -240.0, ALU.mult)
+    ts(c225, cb15, 225.0, ALU.add)
     iota(A("jn"), [[0, 768]], 1000000)
-    iota(A("pn0"), [[-1, 56], [0, 2]], 56)
+    iota(A("n2", 0, NS), [[-1, 56], [0, 2]], 56)
     iota(A("jc"), [[2, 56], [0, 2]], 769)
     iota(A("on5"), [[0, 512]], 1)
     for b in range(4):
         unpacker(b)
-        iota(A("wn", WN * b, WN * b + WN), [[0, WN]], 0)
+    for b in range(8):
+        iota(A("wn%d" % (b % 2), WN * (b // 2) + 1, WN * (b // 2) + 768, 2), [[0, C]], 0)
+    iota(A("zj"), [[0, NS // 2], [1, 2]], 0)
+    ms(A("du", 104, 112), 0)
     for n in ("tz", "vz"):
         iota(A(n, 0, 336, 3), [[0, NS]], 0)
-    iota(A("nz", 0, 224, 2), [[0, NS]], 0)
-    iota(A("n1", 0, 224, 2), [[0, NS]], 800)
-    iota(A("cum"), [[0, 800]], -512)
+    for n in ("nz", "qz"):
+        iota(A(n, 0, 224, 2), [[0, NS]], 0)
+    iota(A("cum"), [[0, 520]], 0)
     iota(A("tl"), [[0, 520]], 0)
     iota(A("v0"), [[2, 520]], 0)
     iota(A("onp"), [[0, C]], 1)
-    iota(A("onn"), [[0, C]], -1)
     iota(A("ik"), [[1, 776]], 0)
     iota(A("alt"), [[0, WN // 2], [1, 2]], 0)
     iota(A("cpv"), [[-2050, C]], 2050 * (C - 1) + 1)
     qz(A("eq"), A("es"), A("ein"))
-    act(A("pn"), A("pn0"), scale=2.0 ** 18)
-    ms(A("rx", K2, NS), 225.0)
+    act(A("pn"), A("n2", 0, NS), scale=2.0 ** 18)
+    ms(A("rx", K2, NS), -15.0)
     ms(A("ja", 225, 768, 256), 0.0)
     ms(A("jm", 224, 1024, 256), 2.0 ** 24)
     ms(A("jm", 225, 1024, 256), 2.0 ** 24)
@@ -332,32 +351,37 @@ def rank_program(g, core, T, topo):
     ts(jl2, A("cs", 8, 15), 2.0, ALU.mult, 802.0, ALU.add)
     ts(A("cs", 184, 191), A("cs", 8, 15), 104.0, ALU.is_ge)
     tt(padv, A("cs", 184, 191), jl2, ALU.mult)
-    for c, v in ((c14, -14.0), (c384, 384.0), (c512, 512.0), (c225, 225.0), (chalf, 0.5)):
+    for c, v in ((c14, -14.0), (c384, 384.0), (c512, 512.0), (chalf, 0.5)):
         ts(c, corr, v, ALU.add)
     ts(corr2, corr, 2.0, ALU.mult)
     ts(k1D, kD, 1.0, ALU.add)
     ts(km, kD, float(H - 1), ALU.not_equal)
     ts(k2D, kD, 2.0, ALU.mult)
     klc = A("kd", 0, 24)
-    ts(klc, kD, 0.0, ALU.mult, corr2, ALU.add)
-    ts(klc, klc, 1.0, ALU.add)
+    ms(A("ja", 1, 224, 2), 1.0)
+    ms(A("t1", 2, 336, 3), -1.0)
+    ms(A("v1", 1, 336, 3), 0.0)
     ms(A("fb", 0, 8), 0.0)
     ms(A("pk", 768, 776), 0.0)
-    ts(A("cu", 16, 40), kD, -1.0, ALU.mult, 383.0, ALU.add)
+    ts(A("cu", 16, 28), A("cs", 8, 20), -1.0, ALU.mult, H - 1.0, ALU.add)
     qz(A("vq"), A("vs"), A("vin"))
 
     fp, fk = A("fb", 7, 7 + C), A("fb", 8, 8 + C)
-    rev = A("cu", 16, 40)
+    rev = A("cu", 16, 28)
 
     def tables(t):
-        act(A("cap", 0, C + 1), A("fb", 7, 8 + C), bias=1e29, scale=-2e29)
-        act(A("fc"), fp, bias=2.0 ** 21, scale=2048.0 - 2.0 ** 21)
-        act(A("fr"), IND(fk, rev), bias=-2.0 ** 21, scale=2.0 ** 21 - 2048.0)
-        pkr = A("pk", 1, 768, 2)
-        scan(pkr, A("fc"), A("cpk", 1, 768, 2), ALU.add, ALU.min)
-        d = to_d("sc3", pkr, C)
-        ts(A("dk", 0, 24), d, corr, ALU.subtract)
-        scan(A("kr"), A("fr"), A("cpv"), ALU.add, ALU.max)
+        act(A("cap", 0, H + 1), A("fb", 7, 8 + H), bias=1e29, scale=-2e29)
+        act(A("cap", H + 1, C + 1), A("fb", 8 + H, 8 + C), bias=1e29, scale=-2e29)
+        for h in range(2):
+            lo, hi, back = H * h, H * h + H, (H - H * h, C - H * h)
+            act(A("fc", lo, hi), A("fb", 7 + lo, 7 + hi), bias=2.0 ** 21, scale=2048.0 - 2.0 ** 21)
+            act(A("fr", *back), IND(A("fb", 8 + lo, 8 + hi), rev), bias=-2.0 ** 21, scale=2.0 ** 21 - 2048.0)
+            pkr = A("pk", 2 * lo + 1, 2 * hi, 2)
+            scan(pkr, A("fc", lo, hi), A("cpk", 2 * lo + 1, 2 * hi, 2), ALU.add, ALU.min)
+            to_d("sc3", pkr, H, lo)
+            scan(A("kr", *back), A("fr", *back), A("cpv", *back), ALU.add, ALU.max)
+            act(A("pk", 2 * lo, 2 * hi, 2), IND(A("kr", *back), rev))
+        ts(A("dk", 0, 24), A("sc3", 15, C, 16), corr, ALU.subtract)
         ts(A("dk", 32, 56), A("dk", 0, 24), 1023, ALU.bitwise_and, 1, ALU.logical_shift_right)
         tt(A("kd", 32, 56), k1D, A("dk", 32, 56), ALU.subtract)
         cp(A("dk", 64, 76), A("pl", 32 * t, 32 * t + 12))
@@ -369,49 +393,56 @@ def rank_program(g, core, T, topo):
         ts(klc, A("kd", 128, 152), corr2, ALU.add)
         tt(A("kd", 32, 56), A("kd", 64, 88), k2D, ALU.add)
         cp(A("cu", 40, 64), A("kd", 32, 56))
-        act(A("v0", 0, C), IND(A("ik"), A("cu", 40, 64)))
-        act(A("pk", 0, 768, 2), IND(A("kr"), rev))
-        act(A("hc"), fp, bias=2 * BIG, scale=1.0 - 2 * BIG)
-        act(A("onp"), fk, bias=1.0, scale=BIG)
-        act(A("onn"), fk, bias=-1.0, scale=-BIG)
-        act(A("tl", 7, 7 + C), fp, scale=-BIG)
 
-    def ranks(n, rv, na):
-        L = n // 16
-        scan(A("x2", 0, n), A("c0", 0, n), A("x1", 0, n), ALU.add, ALU.min)
+    def late_tables(r):
+        act(A("v0", 0, C), IND(A("ik"), A("cu", 40, 64)), behind=r)
+        act(A("hc"), fp, bias=2 * BIG, scale=1.0 - 2 * BIG, behind=r)
+        act(A("onp"), fk, bias=1.0, scale=BIG, behind=r)
+        act(A("tl", 7, 7 + C), fp, scale=-BIG, behind=r)
+
+    def ranks(n, real, rv, na, acc, mid=0):
+        L, cuts = n // 16, [0] + ([mid] if mid else []) + [n]
+        for lo, hi in zip(cuts, cuts[1:]):
+            scan(A("x2", lo, hi), A("c0", lo, hi), A("x1", lo, hi), ALU.add, ALU.min)
+            tt(A("x3", lo, hi), A("x2", lo, hi), rv(lo, hi), ALU.is_equal)
+            scan(A("x4", lo, hi), A("zr", lo, hi), A("x3", lo, hi), ALU.max, ALU.subtract, -128.0)
         for m in range(na):
-            e, j = 16 * m + 16, N2 * (m % 4)
-            act(A("tau", m * n, m * n + n), rv(0, n), AF.Sign, bias=col("x2", 16 * m + 15), scale=-1.0)
-            act(A("junk", j, j + e), A("tau", m * n, m * n + e), AF.Relu, acc=col("acc", 3 * m))
-            act(A("junk", j + e, j + n), A("tau", m * n + e, m * n + n), AF.Relu, scale=-1.0, acc=col("acc", 3 * m + 1))
-        tt(A("x3", 0, n), A("x2", 0, n), rv(0, n), ALU.is_equal)
-        scan(A("x4", 0, n), A("zr", 0, n), A("x3", 0, n), ALU.max, ALU.subtract, -128.0)
+            e, j, o = 16 * m + 16, N2 * (m % 4), m * n
+            parts = [0, mid, real] if e <= mid else [0, real]
+            for lo, hi in zip(parts, parts[1:]):
+                act(A("tau", o + lo, o + hi), rv(lo, hi), AF.Sign, bias=col("x2", 16 * m + 15), scale=-1.0)
+            act(A("junk", j, j + e), A("tau", o, o + e), AF.Relu, acc=col(acc, 4 * m))
+            parts = [e] + parts[1:]
+            for k, (lo, hi) in enumerate(zip(parts, parts[1:])):
+                if lo < hi:
+                    act(A("junk", j + lo, j + hi), A("tau", o + lo, o + hi), AF.Relu, scale=-1.0, acc=col(acc, 4 * m + 1 + k))
         for m in range(na, L):
-            k, e, o = col("x2", 16 * m + 15), 16 * m + 16, (m - na) * n
+            k, e, w = col("x2", 16 * m + 15), 16 * m + 16, max(real, 16 * m + 16)
+            o = (m - na + 1) * n - w
             ts(A("cmp", o, o + e), rv(0, e), k, ALU.is_ge)
-            if e < n:
-                ts(A("cmp", o + e, o + n), rv(e, n), k, ALU.is_gt)
-            scan(A("cum2", o, o + n), A("ones", 0, n), A("cmp", o, o + n), ALU.mult, ALU.add, col("x4", 16 * m + 15))
-        tt(A("acc", 2, 3 * na, 3), A("cs", ce, ce + na), A("x4", 15, 16 * na, 16), ALU.add)
-        scan(A("acc", 64, 64 + 3 * na), A("z3", 0, 3 * na), A("acc", 0, 3 * na), ALU.mult, ALU.add)
-        cp(A("ru", 0, na), A("acc", 66, 64 + 3 * na, 3))
-        ts(A("ru", na, L), A("cum2", n - 1, o + n, n), 128.0, ALU.add)
+            if e < w:
+                ts(A("cmp", o + e, o + w), rv(e, w), k, ALU.is_gt)
+            scan(A("cum2", o, o + w), A("ones", 0, w), A("cmp", o, o + w), ALU.mult, ALU.add, col("x4", 16 * m + 15))
+        tt(A(acc, 3, 4 * na, 4), A("cs", ce, ce + na), A("x4", 15, 16 * na, 16), ALU.add)
+        scan(A(acc, 64, 64 + 4 * na), A("z4", 0, 4 * na), A(acc, 0, 4 * na), ALU.mult, ALU.add)
+        cp(A("ru", 0, na), A(acc, 67, 64 + 4 * na, 4))
+        ts(A("ru", na, L), A("cum2", n - 1, (L - na) * n, n), 128.0, ALU.add)
         return A("ru", 0, L)
 
     def best(r):
         cp(A("sel"), IND(A("selt"), r))
         scan(A("pre"), A("ones", 0, N1), A("sel"), ALU.mult, ALU.add)
-        for m in range(7):
-            lo, hi = window(m)
-            if m in ONV:
-                o = A("cnt", 168 * (m - 4), 168 * (m - 4) + hi - lo)
-                ts(o, A("pre", lo, hi), col("cs", kP + m), ALU.is_gt, 2.0, ALU.mult)
-                red(col("acc", 48 + m), o)
-            else:
-                j = N2 * (m % 4)
-                act(A("junk", j, j + hi - lo), A("pre", lo, hi), AF.Sign, bias=col("cs", kB + m), acc=col("acc", 48 + m))
-        tt(A("acc", 56, 63), A("acc", 48, 55), A("cs", 48, 55), ALU.add)
-        return A("acc", 56, 63)
+        w = N1 - K2 + 16
+        for m in range(NB):
+            o = A("cnt", w * m, w * m + w)
+            ts(o, A("pre", 16 * m, 16 * m + w), col("cs", kP + m), ALU.is_lt)
+            scan(A("cum2", w * m, w * m + w), A("ones", 0, w), o, ALU.mult, ALU.add, 16.0 * m)
+        for m in range(NB, 7):
+            j = N2 * (m % 4)
+            act(A("junk", j, j + N1 - 16 * NB), A("pre", 16 * NB, N1), AF.Sign, bias=col("cs", kB + m), acc=col("acc", m))
+        for k in range(3):
+            ts(A("l3", 8 * k, 8 * k + NB), A("cum2", w - 1, w * NB, w), 3.0, ALU.mult, float(k), ALU.add)
+            ts(A("l3", 8 * k + NB, 8 * k + 7), A("acc", NB, 7), -1.5, ALU.mult, 1.5 * (N1 + 16 * NB) + k, ALU.add)
 
     def si(k, o=0, st=1):
         return A("si", NS * k + o, NS * k + NS, st)
@@ -423,19 +454,24 @@ def rank_program(g, core, T, topo):
         k = k % 2 if n == "jp" else (k and 1 + k % 2) if n == "jn" else k % 3
         return A(n, 256 * k + o, 256 * k + w, st)
 
+    def slots_to_d(k):
+        lo = 768 + 128 * k
+        scan(A("jp", lo, lo + NS), A("jp", 512, 512 + NS), J("jp", k), ALU.add, ALU.max)
+        return A("jp", lo + 15, lo + NS, 16)
+
     def E(b):
         return A("eq", 128 * b, 128 * b + 128), A("es", 128 * b, 128 * b + 128)
 
     def finish(h, b):
-        r, k = A("rl", C * b + H * h, C * b + H * h + H), b % 3
-        act(r, A("ps", 512 * k, 512 * k + H), AF.Relu, scale=0.015625)
-        tt(A("xt", 768 * h + b, 768 * h + 768, 4), A("ps", 512 * (3 + k), 512 * (3 + k) + H), r, ALU.add)
+        r = A("rl", C * b + H * h, C * b + H * h + H)
+        act(r, A("ps", 512 * b, 512 * b + H), AF.Relu, scale=0.015625)
+        tt(A("xt", 768 * h + b, 768 * h + 768, 4), A("ps", 512 * (4 + b), 512 * (4 + b) + H), r, ALU.add)
 
     def half_layer(t, h):
-        zq, zs = A("zq%d" % t, H * h, H * h + H), A("zs%d" % t, H * h, H * h + H)
+        zq, zs = A("zq", H * h, H * h + H), A("zs", H * h, H * h + H)
         for b in range(4):
-            mm(b % 3, A("wq", 128 * b, 128 * b + 128), A("wsc", 128 * b, 128 * b + 128), zq, zs)
-            mm(3 + b % 3, *E(b), zq, zs)
+            mm(b, A("wq", 128 * b, 128 * b + 128), A("wsc", 128 * b, 128 * b + 128), zq, zs)
+            mm(4 + b, *E(b), zq, zs)
             finish(h, b)
         qz(A("xq", H * h, H * h + H), A("xs", H * h, H * h + H), A("xt", 768 * h, 768 * h + 768))
 
@@ -448,8 +484,9 @@ def rank_program(g, core, T, topo):
                 tt(o, p, A("cap", k + lo, k + hi), ALU.min)
             else:
                 (cp if k else act)(o, p)
-        scan(A("w3", 2 * lo, 2 * hi), A("c3"), A("sr", 2 * lo, 2 * hi), ALU.add, ALU.max)
-        tt(A("x1", 128 * h, 128 * h + 128), A("w3", 2 * lo + 2, 2 * hi, 3), A("lm", 0, 128), ALU.max)
+        for j in (2 * h, 2 * h + 1):
+            scan(A("w3", H * j, H * j + H), A("c3", 0, H), A("sr", H * j, H * j + H), ALU.add, ALU.max)
+            tt(A("x1", 64 * j, 64 * j + 64), A("w3", H * j + 2, H * j + H, 3), A("lm", 0, 64), ALU.max)
 
     def store(h):
         lo, hi = H * h, H * h + H
@@ -458,33 +495,42 @@ def rank_program(g, core, T, topo):
         cp(A("yo", lo, hi), A("ps", 512 * (6 + h), 512 * (6 + h) + H))
         dma("s", [A("yo", lo, hi)], [], T.y[:, lo:hi], T.yo[:, lo:hi])
 
+    def windows(t, r):
+        pairs = (("xq", "xs"), ("pq%d" % t, "pp%d" % t))
+        for w, (q, p) in enumerate(pairs):
+            for b in range(4):
+                mm(4 + b, *E(b), A(q, 0, C), A(p, 0, C), behind=A("l3", 0, 7))
+                act(A("wn%d" % w, WN * b, WN * b + 2 * C, 2), A("ps", 512 * (4 + b), 512 * (4 + b) + C), behind=r)
+        for w, (q, p) in enumerate(pairs if t else ()):
+            q2, p2 = A("xq2", C * w, C * w + C), A("xs2", C * w, C * w + C)
+            dma("s", [A(q)], [q2], ap(q2).bitcast(dt.uint8), T[q][:, 1:C + 1].bitcast(dt.uint8))
+            dma("s", [A(p)], [p2], ap(p2), T[p][:, 1:C + 1])
+            for b in range(4):
+                mm(b, *E(b), A(q, 0, C), A(p, 0, C), q2, p2, A("l3", 0, 7))
+                act(A("wn%d" % w, WN * b + 1, WN * b + 2 * C, 2), A("ps", 512 * b, 512 * b + C), scale=0.5, behind=r)
+
     scores(0, 0, False)
     scores(1, 2, False)
     for t in range(3):
-        x = best(ranks(N1, lambda a, b: A("w3", 3 * a + 2, 3 * b, 3), NA[0]))
+        send(A("xq"), A("pq%d" % t), "c", t, True)
+        send(A("xs"), A("pp%d" % t), "s", t, False)
+        best(ranks(N1, N1, lambda a, b: A("w3", 3 * a + 2, 3 * b, 3), NA[1 if t else 0], "ac1" if t else "ac0", N1 // 2 if t else 0))
         for k in range(3):
             l = A("l3", 8 * k, 8 * k + 7)
-            ts(l, x, -1.5, ALU.mult, float(k), ALU.add)
             act(A("r3", k, 336, 3), IND(A("sr"), l))
             tt(A("x1", k, 336, 3), IND(A("sr"), l), A("lm", k, 336, 3), ALU.max)
-        iota(A("inv"), [[0, 784]], 225, 0, [A("l3", 0, 7)] if t else [])
-        r = ranks(N2, lambda a, b: A("r3", a, b), NA[1])
+        iota(A("inv"), [[0, 784]], -15, 0, [A("l3", 0, 7)] if t else [])
+        r = ranks(N2, 3 * K2, lambda a, b: A("r3", a, b), NA[2], "ac0")
         for k in range(3):
             act(A("k2", k, 336, 3), IND(A("pk" if t else "cpk"), A("l3", 8 * k, 8 * k + 7)))
         cp(IND(A("ew"), r), A("k2", 0, N2))
+        windows(t, r)
         if t:
-            dma("s", [A("xq")], [A("xq2")], T.xq2[:].bitcast(dt.uint8), T.xq[:, 1:C + 1].bitcast(dt.uint8))
-            dma("s", [A("xs")], [A("xs2")], T.xs2[:], T.xs[:, 1:C + 1])
-        for b in range(4):
-            mm(4 + b, *E(b), A("xq", 0, C), A("xs", 0, C))
-            act(A("wn", WN * b, WN * b + 2 * C, 2), A("ps", 512 * (4 + b), 512 * (4 + b) + C))
-            if t:
-                mm(b, *E(b), A("xq", 0, C), A("xs", 0, C), A("xq2"), A("xs2"))
-                act(A("wn", WN * b + 1, WN * b + 2 * C, 2), A("ps", 512 * b, 512 * b + C), scale=0.5)
-        d = to_d("js", A("ew", 0, NS), NS, 8 * NS)
+            late_tables(r)
+        d = to_d("js", A("ew", 0, NS), NS)
         pi, ei, oi_ = A("di", 0, 7), A("di", 8, 15), A("di", 16, 23)
         PK, PE, PO, LF = [si(k) for k in range(4)]
-        dd, ab, cc, cc2, mb, hi, ncl, gv, mc = [sf(k) for k in range(9)]
+        dd, ab, cc, cc2, mb, hi, neg, rd_, mc = [sf(k) for k in range(9)]
         ts(A("du", 0, 7), d, c384, ALU.subtract, 1.0 / 1024, ALU.mult)
         ts(pi, d, corr, ALU.subtract)
         cp(PK, A("ew", 0, NS))
@@ -493,29 +539,39 @@ def rank_program(g, core, T, topo):
         cp(A("du", 8, 15), oi_)
         cp(IND(A("inv"), A("du", 0, 7)), A("rx"))
         act(J("jp", 0), IND(A("inv"), A("du", 8, 15)))
-        act(cc, J("jp", 0), bias=56 * 2.0 ** 18 + 2.0 ** 17, scale=-2.0 ** 16)
+        act(cc, J("jp", 0), bias=56 * 2.0 ** 18 + 2.0 ** 17 - 240 * 2.0 ** 16, scale=-2.0 ** 16)
         ts(PE, PK, 10, ALU.logical_shift_right, 1022, ALU.bitwise_and)
-        ts(PO, PK, 1022, ALU.bitwise_and)
-        ts(LF, PK, 1, ALU.bitwise_and)
-        tt(dd, PO, PE, ALU.subtract)
-        act(ab, dd, AF.Abs, scale=0.5)
-        act(J("ja", 0), ab, bias=1.0)
-        d = to_d("js", J("jp", 0), NS)
-        tt(J("jn", 0), PE, PO, ALU.min)
-        ts(A("du", 16, 23), d, corr, ALU.subtract)
-        cp(A("v1", 2, 336, 3), PO)
-        act(mc, A("v1", 2, 336, 3), bias=512.0, scale=256.0)
+        d = slots_to_d(0)
+        ts(A("du", 16, 23), d, cb15, ALU.subtract)
         ts(cc2, cc, 1.5 * 2.0 ** 41, ALU.add, 1.5 * 2.0 ** 41, ALU.subtract)
-        tt(mb, mc, J("ja", 0), ALU.add)
+        if t:
+            ts(PO, PK, 1022, ALU.bitwise_and)
+            ts(LF, PK, 1, ALU.bitwise_and)
+            tt(dd, PO, PE, ALU.subtract)
+            act(ab, dd, AF.Abs, scale=0.5)
+            act(J("ja", 0), ab, bias=1.0)
+            tt(J("jn", 0), PE, PO, ALU.min)
+            cp(A("v1", 2, 336, 3), PO)
+            act(mc, A("v1", 2, 336, 3), bias=512.0, scale=256.0)
+            tt(mb, mc, J("ja", 0), ALU.add)
+            act(A("t1", 2, 336, 3), ab, bias=-1.0, scale=-1.0)
+            act(A("v1", 1, 336, 3), dd, scale=-1.0)
+            act(rd_, dd, AF.Relu, scale=-0.5)
+            tt(A("q1", 1, 224, 2), LF, rd_, ALU.subtract)
+        else:
+            cp(J("jn", 0), PE)
+            act(A("v1", 2, 336, 3), J("jn", 0))
+            act(mb, J("jn", 0), bias=513.0, scale=256.0)
         tt(J("jm", 0), cc2, mb, ALU.add)
-        act(A("t1", 2, 336, 3), ab, bias=-1.0, scale=-1.0)
-        act(A("v1", 1, 336, 3), dd, scale=-1.0)
         tt(A("v1", 0, 336, 3), A("jc"), PE, ALU.subtract)
         ts(A("di", 24, 31), pi, 10, ALU.logical_shift_right, 1022, ALU.bitwise_and)
         cp(A("du", 104, 111), A("di", 24, 31))
-        for b in range(4):
-            act(A("gj", NS * b, NS * b + NS), IND(A("wn", WN * b, WN * b + WN), A("du", 104, 111)), scale=0.5)
-            tt(A("wn", WN * b + 769, WN * b + WN, 2), A("gj", NS * b, NS * b + NS, 2), A("gj", NS * b + 1, NS * b + NS, 2), ALU.add)
+        send(A("du", 104, 112), A("sl%d" % t), "j", t, False)
+        for w, l in enumerate((A("du", 104, 111), A("sl%d" % t, 0, 7))):
+            for b in range(4):
+                o = NS * (4 * w + b)
+                act(A("gj", o, o + NS), IND(A("wn%d" % w, WN * b, WN * b + 768), l), scale=0.5)
+                scan(A("wn%d" % w, WN * b + 768, WN * b + WN), A("zj"), A("gj", o, o + NS), ALU.mult, ALU.add)
         lc, dn, mxp = A("du", 64, 71), A("df", 8, 15), A("df", 56, 63)
         ts(A("df", 0, 7), d, c225, ALU.not_equal)
         tt(dn, A("df", 0, 7), jl2, ALU.mult)
@@ -531,8 +587,7 @@ def rank_program(g, core, T, topo):
             l = A("du", 16 + 8 * k, 23 + 8 * k)
             if k < 5:
                 act(J("jp", k + 1), IND(J("jp", k, 0, 1, 226), l))
-                d = to_d("js", J("jp", k + 1), NS, (k + 1) * NS)
-                ts(A("du", 24 + 8 * k, 31 + 8 * k), d, corr, ALU.subtract)
+                ts(A("du", 24 + 8 * k, 31 + 8 * k), slots_to_d(k + 1), cb15, ALU.subtract)
                 act(sf(9 + k % 2), J("ja", k))
                 tt(J("ja", k + 1), IND(J("ja", k, 0, 1, 226), l), sf(9 + k % 2), ALU.add)
             act(sf(11 + k % 2), J("jn", k))
@@ -540,9 +595,9 @@ def rank_program(g, core, T, topo):
             act(A("jy", 224 * k + 1, 224 * k + 224, 2), J("jm", k))
             act(A("jy", 224 * k, 224 * k + 224, 2), IND(J("jm", k, 0, 1, 226), l))
             scan(J("jm", k + 1, 0, 1), J("ja", k, 0, 1), A("jy", 224 * k, 224 * k + 224), ALU.add, ALU.min)
-        m, nm, nc, cb, neg = J("jm", 6), A("n1", 1, 224, 2), A("tz", 1, 336, 3), A("vz", 2, 336, 3), A("nz", 1, 224, 2)
+        m, nm, nc, cb = J("jm", 6), sf(13), A("tz", 1, 336, 3), A("vz", 2, 336, 3)
         for j in range(2):
-            tt(A("n1", 1 + 2 * j, 224, 4), J("jn", 6, 1, 4), J("jn", 6, 3, 4), ALU.min)
+            tt(sf(13, j, 2), J("jn", 6, 1, 4), J("jn", 6, 3, 4), ALU.min)
         tt(A("tz", 2, 336, 3), J("jn", 0), nm, ALU.is_equal)
         ts(hi, m, 2.0 ** 32 - 256.0, ALU.add, 2.0 ** 32, ALU.subtract)
         tt(nc, m, A("pn"), ALU.is_lt)
@@ -554,54 +609,54 @@ def rank_program(g, core, T, topo):
         cp(IND(A("tl"), lc), A("t2", 2, 336, 3))
         ms(col("cum", 7), 512.0)
         scan(A("cum", 8, 8 + C), A("onp"), A("tl", 7, 7 + C), ALU.add, ALU.add, 512.0)
-        scan(A("cum", 408, 408 + C), A("onn"), A("tl", 7, 7 + C), ALU.add, ALU.subtract, -512.0)
-        tt(neg, cb, LF, ALU.is_equal)
-        scan(A("n2"), A("nz"), A("n1"), ALU.mult, ALU.add)
-        d = to_d("js", A("n2", 1, 224, 2), NS, 6 * NS)
+        d = to_d("js", nm, NS, NS)
         ts(A("du", 72, 79), d, c14, ALU.subtract, 0.5, ALU.mult)
-        tt(ncl, nc, LF, ALU.mult)
-        tt(A("q1", 1, 224, 2), A("t1", 0, 336, 3), ncl, ALU.mult)
-        act(A("q1", 0, 224, 2), A("t2", 1, 336, 3), bias=2.0, scale=-1.0)
-        scan(A("q2"), A("nz"), A("q1"), ALU.mult, ALU.add)
-        tt(gv, IND(A("cum"), A("du", 72, 79)), A("q2", 1, 224, 2), ALU.add)
-        cp(IND(A("cum", 0, 520), lc), gv)
+        act(A("nz", 1, 224, 2), cb, bias=1.0, scale=-2.0)
+        act(sf(14), A("t2", 1, 336, 3), bias=0.0 if t else 0.5, scale=0.5)
+        act(A("n1", 1, 224, 2), A("t2", 1, 336, 3), bias=-1.0 if t else -0.5, scale=0.5)
+        tt(A("n1", 0, 224, 2), sf(14), A("t1", 1, 336, 3), ALU.subtract)
+        scan(A("n2"), A("nz"), A("n1"), ALU.mult, ALU.add)
+        tt(A("q1", 0, 224, 2), IND(A("cum"), A("du", 72, 79)), A("n2", 1, 224, 2), ALU.add)
+        if t:
+            tt(neg, cb, LF, ALU.is_equal)
+            act(A("qz", 1, 224, 2), neg, bias=1.0, scale=-2.0)
+            scan(A("q2"), A("qz"), A("q1"), ALU.mult, ALU.add)
+        cp(IND(A("cum"), lc), A("q2", 1, 224, 2) if t else A("q1", 0, 224, 2))
         act(A("vz", 1, 336, 3), nc)
-        scan(A("v2"), A("vz"), A("v1"), ALU.mult, ALU.add)
-        d = to_d("js", cb, NS, 7 * NS)
+        for lo, hi in ((0, 192), (192, 336)):
+            scan(A("v2", lo, hi), A("vz", lo, hi), A("v1", lo, hi), ALU.mult, ALU.add)
+        d = to_d("js", cb, NS, 2 * NS)
         ts(A("df", 72, 79), d, chalf, ALU.is_lt)
         tt(A("df", 80, 87), A("df", 72, 79), dn, ALU.mult)
         tt(A("df", 88, 95), A("df", 80, 87), mxp, ALU.max)
         ts(A("du", 112, 119), A("df", 88, 95), 0.5, ALU.mult, -0.25, ALU.add)
-        cp(IND(A("v0"), A("du", 112, 119)), A("v2", 2, 336, 3))
-        if t:
-            scan(A("qs"), A("hc"), A("cum", 7, 7 + C), ALU.add, ALU.min)
-        d = to_d("sc", A("qs") if t else A("cum", 7, 7 + C), C)
+        for lo, hi in ((0, 4), (4, 7)):
+            cp(IND(A("v0"), A("du", 112 + lo, 112 + hi)), A("v2", 48 * lo + 2, 48 * hi, 3))
+        for lo, hi in ((0, H), (H, C)) if t else ():
+            scan(A("qs", lo, hi), A("hc", lo, hi), A("cum", 7 + lo, 7 + hi), ALU.add, ALU.min)
+            to_d("sc", A("qs", lo, hi), H, lo)
+        d = A("sc", 15, C, 16) if t else to_d("sc", A("cum", 7, 7 + C), C)
         pos = A("du", 80, 104)
-        tt(A("df", 96, 120), klc, d, ALU.subtract)
-        tt(A("df", 128, 152), A("df", 96, 120), d, ALU.max)
-        ts(pos, A("df", 128, 152), c512, ALU.subtract)
+        if t:
+            tt(A("df", 96, 120), klc, d, ALU.subtract)
+            tt(A("df", 128, 152), A("df", 96, 120), d, ALU.max)
+        ts(pos, A("df", 128, 152) if t else d, c512, ALU.subtract)
         cp(IND(A("vw"), pos), A("v0", 0, C))
         for h in (1, 0):
             l = A("pl", 32 * t + 16 * h, 32 * t + 16 * h + 12)
             ts(l, to_d("sc2", A("vw", H * h, H * h + H), H, H * h), corr, ALU.subtract)
-            if h:
-                send(l, A("nl%d" % t), "n", t, False)
+        send(A("pl", 32 * t + 16, 32 * t + 28), A("nl%d" % t), "n", t, False)
+        for h, l in enumerate((l, A("nl%d" % t))):
             for b in range(4):
-                (act if b < 2 else cp)(A("yt", 768 * h + b, 768 * h + 768, 4), IND(A("wn", WN * b, WN * b + WN), l))
-            if h:
-                sq, ss = A("sq", H * t, H * t + H), A("ss", H * t, H * t + H)
-                qz(sq, ss, A("yt", 768, 1536))
-                send(sq, A("zq%d" % t, H, C), "c", t, True)
-                send(ss, A("zs%d" % t, H, C), "s", t, False)
-            else:
-                qz(A("zq%d" % t, 0, H), A("zs%d" % t, 0, H), A("yt", 0, 768))
+                (act if b < YA[h] else cp)(A("yt", 768 * h + b, 768 * h + 768, 4), IND(A("wn%d" % h, WN * b, WN * b + WN), l))
+            qz(A("zq", H * h, H * h + H), A("zs", H * h, H * h + H), A("yt", 768 * h, 768 * h + 768))
         act(A("fb", 8, 8 + H), IND(A("alt"), A("pl", 32 * t, 32 * t + 12)))
         act(A("fb", 8 + H, 8 + C), IND(A("alt"), A("nl%d" % t)))
         ms(col("fb", 7 + H), 0.0)
         half_layer(t, 0)
         if t < 2:
             tables(t)
-            scores(0, 6, True)
+            scores(0, 2, True)
             half_layer(t, 1)
             scores(1, 0, True)
         else:

@@ -8,8 +8,9 @@ BIG = 2.0 ** 20
 STEP = [1, 2, 1]
 WAKE, FAR, CYC, PEC = 200.0, 3300.0, 0.83, 1.2
 LOOK = {"v": 250.0, "a": 300.0, "p": 0.0, "g": 300.0, "s": 0.0, "r": 0.0}
-TOL, TURNS = 40.0, 4
-NA = (7, 9, 9)
+TOL, TURNS, SPAN, SHAKE = 40.0, 1500, 1500.0, 400.0
+KEPT = []
+NA = (7, 9, 8)
 YA = (2, 2)
 NB = 4
 F, B, I, U, Q, S8 = "float32", "bfloat16", "int32", "uint16", "float8_e4m3fn_x4", "uint8"
@@ -20,7 +21,7 @@ def _sb(n, d):
 
 
 SCRATCH = {
-    "xin": _sb(1544, B), "uin": _sb(512, B), "vin": _sb(512, B), "ein": _sb(2048, B), "ones": _sb(N2, B), "on5": _sb(512, B),
+    "xin": _sb(1544, B), "uin": _sb(512, B), "vin": _sb(512, B), "ein": _sb(2048, B), "ones": _sb(N2, B), "on5": _sb(256, B),
     "xt": _sb(1536, B), "yt": _sb(1536, B), "wn0": _sb(4 * WN, B), "wn1": _sb(4 * WN, B), "gj": _sb(8 * NS, B), "rl": _sb(1536, F),
     "wq": _sb(512, Q), "wsc": _sb(512, S8), "uq": _sb(128, Q), "us": _sb(128, S8), "vq": _sb(128, Q), "vs": _sb(128, S8),
     "u2q": _sb(256, Q), "u2s": _sb(256, S8), "eq": _sb(512, Q), "es": _sb(512, S8),
@@ -28,8 +29,8 @@ SCRATCH = {
     "pq0": _sb(C + 2, Q), "pq1": _sb(C + 2, Q), "pq2": _sb(C + 2, Q), "pp0": _sb(C + 2, S8), "pp1": _sb(C + 2, S8), "pp2": _sb(C + 2, S8),
     "sl0": _sb(8, U), "sl1": _sb(8, U), "sl2": _sb(8, U), "nl0": _sb(12, U), "nl1": _sb(12, U), "nl2": _sb(12, U), "pl": _sb(96, U),
     "ps": ("psum", [128, 4096], F),
-    "t16": _sb(C, F), "lm": _sb(336, F), "c0": _sb(N2, F), "zr": _sb(N2, B), "c3": _sb(C, F),
-    "cv": _sb(C, F), "cv2": _sb(C, F), "ik": _sb(776, F), "alt": _sb(WN, F),
+    "t16": _sb(80, F), "lm": _sb(336, F), "c0": _sb(N2, F), "zr": _sb(N2, B), "c3": _sb(H, F),
+    "cv": _sb(C, F), "ik": _sb(776, F), "alt": _sb(WN, F),
     "selt": _sb(N1, B), "cpk": _sb(776, F), "cpv": _sb(C, F), "rx": _sb(NS, F), "pn": _sb(NS, F), "jc": _sb(NS, F),
     "cs": _sb(224, F), "ci": _sb(8, I), "cu": _sb(64, U), "z4": _sb(48, F), "zj": _sb(NS, B),
     "ac0": _sb(112, F), "ac1": _sb(112, F),
@@ -46,7 +47,7 @@ SCRATCH = {
     "tl": _sb(520, F), "cum": _sb(520, F), "v0": _sb(520, F), "qs": _sb(C, F),
     "vw": _sb(C, F), "of": _sb(C, F), "yo": _sb(C, F),
 }
-SEMAPHORES = (["v", "a", "p", "g"] + ["d%d" % i for i in range(1, 34)]
+SEMAPHORES = (["v", "a", "p", "g"] + ["d%d" % i for i in range(1, 38)]
               + ["%s%d" % (n, t) for n in ("ln", "lc", "ls", "lj", "rn", "rc", "rs", "rj") for t in range(3)])
 
 
@@ -71,7 +72,7 @@ def rank_program(g, core, T, topo):
     if rank is None:
         return
     eng = {"v": g.vector, "a": g.scalar, "p": g.tensor, "g": g, "s": g.sync}
-    ops, nd = [], [0]
+    ops, nd, soft = [], [0], set()
     lastw = {n: np.full(v[1][1], -1) for n, v in SCRATCH.items()}
     reads = {n: [] for n in SCRATCH}
     bank = [{} for _ in range(8)]
@@ -126,7 +127,7 @@ def rank_program(g, core, T, topo):
         elif e in "va":
             c = max(64, per * len(range(*x[1:]))) * CYC
         else:
-            c = 130 + 2 * CYC * n if e == "g" else per * CYC * (16 + n)
+            c = 130 + 2.6 * CYC * n if e == "g" else per * CYC * (16 + n)
         note(e, rd, wr, lambda s: call().then_inc(T.sem[s], 1), e, 1, c + more, c + more)
 
     def plan(before, after, way, back):
@@ -146,7 +147,8 @@ def rank_program(g, core, T, topo):
             over[i] = now + ops[i][5 if back else 6]
             order.append(i)
             for j in after[i]:
-                ready[j] = max(ready[j], over[i] + WAKE + (ops[j][6] - ops[j][5] if back else 0.0))
+                if (min(i, j), max(i, j)) not in soft:
+                    ready[j] = max(ready[j], over[i] + WAKE + (ops[j][6] - ops[j][5] if back else 0.0))
                 left[j] -= 1
                 if not left[j]:
                     cand[ops[j][0]].append(j)
@@ -154,19 +156,28 @@ def rank_program(g, core, T, topo):
 
     def issue():
         n = len(ops)
-        before, after, way = [o[1] for o in ops], [[] for _ in ops], [0.0] * n
-        for i, o in enumerate(ops):
-            for d in o[1]:
+        before, after, way = [o[1] + [a for a, b in soft if b == i] for i, o in enumerate(ops)], [[] for _ in ops], [0.0] * n
+        for i in range(n):
+            for d in before[i]:
                 after[d].append(i)
         for i in range(n - 1, -1, -1):
             way[i] = ops[i][6] + max([way[j] + WAKE for j in after[i]] + [0.0])
-        tries = []
-        for _ in range(TURNS):
-            order, over = plan(before, after, way, False)
-            tries.append((max(over), order))
-            way = plan(after, before, over, True)[1]
+        if not KEPT:
+            tries = []
+            for _ in range(3):
+                order, over = plan(before, after, way, False)
+                tries.append((max(over), order, way))
+                way = plan(after, before, over, True)[1]
+            kept, rng = min(tries), np.random.default_rng(1)
+            for _ in range(TURNS):
+                lo = rng.random() * kept[0]
+                way = [w + (x if lo < w < lo + SPAN else 0.0) for w, x in zip(kept[2], (rng.normal(size=n) * SHAKE).tolist())]
+                order, over = plan(before, after, way, False)
+                if max(over) <= kept[0]:
+                    kept = (max(over), order, way)
+            KEPT.append(kept[1])
         tok, cnt, seen = [None] * n, {}, {e: {} for e in eng}
-        for i in min(tries)[1]:
+        for i in KEPT[0]:
             e, need, call, sem, inc = ops[i][:5]
             cnt[sem] = cnt.get(sem, 0) + inc
             tok[i] = (sem, cnt[sem])
@@ -213,7 +224,11 @@ def rank_program(g, core, T, topo):
         if acc is not None:
             kw["accum_out"] = ap(acc)
         fn = f if f is not None else (AF.Copy if bias is None and acc is None else AF.Identity)
-        run("a", [a, bias, behind], [o] + ([acc] if acc else []), lambda: g.scalar.activation(ap(o), ap(a), fn, **kw), 1.0, 20.0 if acc else 0.0)
+        run("a", [a, bias, behind], [o] + ([acc] if acc else []), lambda: g.scalar.activation(ap(o), ap(a), fn, **kw), 1.0,
+            (20.0 if acc else 0.0) + (0.0 if a[0] == "*" else 15.0))
+
+    def fill(o, c):
+        iota(o, [[0, len(range(*o[1:]))]], c)
 
     def iota(o, pat, base, cm=0, behind=()):
         if SCRATCH[o[0]][2] == I:
@@ -243,7 +258,7 @@ def rank_program(g, core, T, topo):
         rid, pid = topo.addr(to)[:2]
         a, b = (ap(dst).bitcast(dt.uint8), ap(src).bitcast(dt.uint8)) if cast else (ap(dst), ap(src))
         note("g", [src], [], lambda s: g.remote_dma(a, b, T.sem["r%s%d" % (kind, t)], T.sem[s], pid, rid, topo.mask(core, to)),
-             "l%s%d" % (kind, t), len(topo.engines(core, to)), 500.0, FAR)
+             "l%s%d" % (kind, t), len(topo.engines(core, to)), 500.0 if t or kind != "c" else 4000.0, FAR * (3 if kind in "cs" else 1))
         ops.append(("r", [len(ops) - 1], None, "r%s%d" % (kind, t), len(topo.engines(to, core)), 0.0, 0.0))
         lastw[dst[0]][dst[1]:dst[2]] = len(ops) - 1
 
@@ -262,8 +277,8 @@ def rank_program(g, core, T, topo):
     dma("s", [], [A("xin", 1536, 1544)], T.xin[:, 1536:1544], T.x[:, 0:8])
     iota(col("ci", 0), [[0, 1]], 0, 1)
     iota(i16, [[16, 24]], 0)
-    iota(A("t16"), [[0, 24], [1, 16]], 0)
-    ms(A("ones"), 1.0)
+    iota(A("t16", 0, 16), [[1, 16]], 0)
+    fill(A("ones"), 1)
     ms(A("c0"), 0.0)
     ms(A("zr"), -1e4)
     ms(A("c3"), 0.0)
@@ -271,35 +286,40 @@ def rank_program(g, core, T, topo):
     ts(A("cu", 8, 16), A("cs", 96, 104), 1.0, ALU.add)
     ts(col("ci", 1), col("ci", 0), 15, ALU.bitwise_and)
     ms(A("c0", 0, N2, 16), 5e29)
-    ms(A("c3", 0, C, 3), -3e29)
+    ms(A("c3", 0, H, 3), -3e29)
     cp(qf, col("ci", 1))
     ms(A("zr", 0, N2, 16), -128.0)
     ts(q1, qf, 1.0, ALU.add)
     ts(corr, qf, 15.0, ALU.is_lt, 2.0 ** 21, ALU.mult)
     ts(kD, i16, qf, ALU.add)
-    ms(A("selt", 0, K2), 1.0)
-    ms(A("selt", K2, N1), 0.0)
+    fill(A("selt", 0, K2), 1)
+    fill(A("selt", K2, N1), 0)
     ts(A("cs", kP, kP + 7), A("cs", 8, 15), 0.5, ALU.add)
     ts(A("cs", kB, kB + 7), A("cs", 8, 15), 0.5, ALU.add, -1.0, ALU.mult)
-    ts(A("k2"), A("t16", 0, 336), qf, ALU.not_equal, 8e29, ALU.mult)
-    act(A("lm"), A("k2"), bias=-3e29)
+    ts(A("cu", 40, 64), i16, 0.0, ALU.mult, qf, ALU.add)
+    ts(A("t16", 16, 32), A("t16", 0, 16), qf, ALU.not_equal, 8e29, ALU.mult)
+    act(A("lm"), IND(A("t16", 16, 32), A("cu", 40, 61)), bias=-3e29)
     ms(A("z4"), 1.0)
     ms(A("z4", 0, 48, 4), 0.0)
     ms(A("z4", 1, 48, 4), -1.0)
-    ms(A("ac0", 0, 48), 0.0)
-    ms(A("ac1", 0, 48), 0.0)
+    fill(A("ac0", 0, 48), 0)
+    fill(A("ac1", 0, 48), 0)
     ms(A("sr", 768, 776), -2e29)
     ts(A("cs", ce, ce + 12), A("cs", 97, 109), 128.0, ALU.add)
+    ms(A("on5", 0, 128), 1.0)
+    run("g", [A("on5", 0, 128)], [A("on5", 128, 256)],
+        lambda: g.affine_select(T.on5[:, 128:256], T.on5[:, 0:128], [[-1, 128]], ALU.is_equal, 0.0, 0, 1))
+    ms(A("ein"), 0.0)
+    for b in range(4):
+        act(A("ein", 512 * b + b, 512 * b + 512, 4), A("on5", 128, 256))
+    qz(A("eq"), A("es"), A("ein"))
     qz(A("uq"), A("us"), A("uin"))
+    soft.add((len(ops) - 2, len(ops) - 1))
 
     def repeat_u(k):
         o, w, l = A("u2q", 128 * k, 128 * k + 128), A("uq"), A("cu", 8 * k, 8 * k + 8)
         run("v", [IND(w, l)], [o], lambda: g.vector.tensor_copy(ap(o).bitcast(dt.uint32), ap(w).bitcast(dt.uint32).indirect(ap(l))))
         act(A("u2s", 128 * k, 128 * k + 128), IND(A("us"), l))
-
-    def unpacker(b):
-        o = A("ein", 512 * b, 512 * b + 512)
-        run("g", [A("on5")], [o], lambda: g.affine_select(ap(o), T.on5[:], [[-1, 128], [1000, 4]], ALU.is_equal, 0.0, -1000 * b, 1))
 
     repeat_u(0)
     repeat_u(1)
@@ -308,26 +328,30 @@ def rank_program(g, core, T, topo):
     dma("s", [A("xin")], [A("wq")], T.wq[:].bitcast(dt.uint8), T.wc[:])
     dma("s", [A("xin")], [A("wsc")], T.wsc[:], T.ws[:])
     dma("s", [A("xin")], [A("vin")], T.vin[:], T.v[:])
-    ts(A("cv"), A("t16"), qf, ALU.is_equal, -2.0 ** 22, ALU.mult)
-    ts(A("cv2"), A("t16"), q1, ALU.is_equal, 2.0 ** 21, ALU.mult)
-    tt(A("cv"), A("cv"), A("cv2"), ALU.add)
+    ts(A("t16", 32, 48), A("t16", 0, 16), qf, ALU.is_equal, -4.0, ALU.mult)
+    ts(A("t16", 48, 64), A("t16", 0, 16), q1, ALU.is_equal)
+    tt(A("t16", 64, 80), A("t16", 32, 48), A("t16", 48, 64), ALU.add)
+    act(A("cv"), IND(A("t16", 64, 80), A("cu", 40, 64)), scale=2.0 ** 21)
+    act(A("jp", 512, 512 + NS), IND(A("t16", 64, 80), A("cu", 40, 47)), scale=242.0)
     iota(A("cpk"), [[2050, 388], [1023, 2]], 1)
-    iota(A("rx", 0, K2), [[4, 52], [-2, 2]], 3 - 240)
+    iota(A("rx", 0, K2), [[4, 52], [-2, 2]], 3 - 242)
     iota(A("ja", 0, 768, 2), [[0, 384]], 2 ** 24 - 1)
-    iota(A("jp", 0, 512), [[0, 512]], -15)
-    ts(A("jp", 512, 512 + NS), A("t16", 0, NS), qf, ALU.is_equal, -1024.0, ALU.mult)
-    ts(A("jp", 640, 640 + NS), A("t16", 0, NS), q1, ALU.is_equal, 240.0, ALU.mult)
-    tt(A("jp", 512, 512 + NS), A("jp", 512, 512 + NS), A("jp", 640, 640 + NS), ALU.add)
-    ts(cb15, qf, 15.0, ALU.is_ge, -240.0, ALU.mult)
+    iota(A("jp", 0, 512), [[0, 512]], -17)
+    ts(cb15, qf, 15.0, ALU.is_ge, -242.0, ALU.mult)
+    for n in ("t2", "v2", "vz"):
+        iota(A(n, 3 * K2, 3 * NS), [[0, 24]], 0)
+    for n in ("n2", "q2"):
+        iota(A(n, 2 * K2, 2 * NS), [[0, 16]], 0)
+    iota(A("sf", 9 * NS, 14 * NS), [[0, 5 * NS]], 0)
+    for k in range(3):
+        iota(A("jm", 256 * k + 2 * K2, 256 * k + 2 * NS), [[0, 16]], 0)
     ts(c225, cb15, 225.0, ALU.add)
     iota(A("jn"), [[0, 768]], 1000000)
     iota(A("n2", 0, NS), [[-1, 56], [0, 2]], 56)
     iota(A("jc"), [[2, 56], [0, 2]], 769)
-    iota(A("on5"), [[0, 512]], 1)
-    for b in range(4):
-        unpacker(b)
-    for b in range(8):
-        iota(A("wn%d" % (b % 2), WN * (b // 2) + 1, WN * (b // 2) + 768, 2), [[0, C]], 0)
+    for w in ("wn0", "wn1"):
+        for lo in range(0, 4 * WN, 2 * WN):
+            dma("s", [A("ein")], [A(w, lo, lo + 2 * WN)], T[w][:, lo:lo + 2 * WN], T.ein[:, 0:2 * WN])
     iota(A("zj"), [[0, NS // 2], [1, 2]], 0)
     ms(A("du", 104, 112), 0)
     for n in ("tz", "vz"):
@@ -341,13 +365,12 @@ def rank_program(g, core, T, topo):
     iota(A("ik"), [[1, 776]], 0)
     iota(A("alt"), [[0, WN // 2], [1, 2]], 0)
     iota(A("cpv"), [[-2050, C]], 2050 * (C - 1) + 1)
-    qz(A("eq"), A("es"), A("ein"))
     act(A("pn"), A("n2", 0, NS), scale=2.0 ** 18)
-    ms(A("rx", K2, NS), -15.0)
-    ms(A("ja", 225, 768, 256), 0.0)
-    ms(A("jm", 224, 1024, 256), 2.0 ** 24)
-    ms(A("jm", 225, 1024, 256), 2.0 ** 24)
-    ms(A("jm", 0, 224, 2), 0.0)
+    fill(A("rx", K2, NS), -17)
+    fill(A("ja", 225, 768, 256), 0)
+    fill(A("jm", 224, 1024, 256), 2 ** 24 - 1)
+    fill(A("jm", 225, 1024, 256), 2 ** 24 - 1)
+    fill(A("jm", 0, 208, 2), 0)
     ts(jl2, A("cs", 8, 15), 2.0, ALU.mult, 802.0, ALU.add)
     ts(A("cs", 184, 191), A("cs", 8, 15), 104.0, ALU.is_ge)
     tt(padv, A("cs", 184, 191), jl2, ALU.mult)
@@ -358,11 +381,11 @@ def rank_program(g, core, T, topo):
     ts(km, kD, float(H - 1), ALU.not_equal)
     ts(k2D, kD, 2.0, ALU.mult)
     klc = A("kd", 0, 24)
-    ms(A("ja", 1, 224, 2), 1.0)
-    ms(A("t1", 2, 336, 3), -1.0)
-    ms(A("v1", 1, 336, 3), 0.0)
-    ms(A("fb", 0, 8), 0.0)
-    ms(A("pk", 768, 776), 0.0)
+    fill(A("ja", 1, 224, 2), 1)
+    fill(A("t1", 2, 336, 3), -1)
+    fill(A("v1", 1, 336, 3), 0)
+    fill(A("fb", 0, 8), 0)
+    fill(A("pk", 768, 776), 0)
     ts(A("cu", 16, 28), A("cs", 8, 20), -1.0, ALU.mult, H - 1.0, ALU.add)
     qz(A("vq"), A("vs"), A("vin"))
 
@@ -403,7 +426,8 @@ def rank_program(g, core, T, topo):
     def ranks(n, real, rv, na, acc, mid=0):
         L, cuts = n // 16, [0] + ([mid] if mid else []) + [n]
         for lo, hi in zip(cuts, cuts[1:]):
-            scan(A("x2", lo, hi), A("c0", lo, hi), A("x1", lo, hi), ALU.add, ALU.min)
+            for a, b in ((lo, lo + 64), (lo + 64, hi)):
+                scan(A("x2", a, b), A("c0", a, b), A("x1", a, b), ALU.add, ALU.min)
             tt(A("x3", lo, hi), A("x2", lo, hi), rv(lo, hi), ALU.is_equal)
             scan(A("x4", lo, hi), A("zr", lo, hi), A("x3", lo, hi), ALU.max, ALU.subtract, -128.0)
         for m in range(na):
@@ -445,18 +469,21 @@ def rank_program(g, core, T, topo):
             ts(A("l3", 8 * k + NB, 8 * k + 7), A("acc", NB, 7), -1.5, ALU.mult, 1.5 * (N1 + 16 * NB) + k, ALU.add)
 
     def si(k, o=0, st=1):
-        return A("si", NS * k + o, NS * k + NS, st)
+        return A("si", NS * k + o, NS * k + K2, st)
 
-    def sf(k, o=0, st=1):
-        return A("sf", NS * k + o, NS * k + NS, st)
+    def sf(k, o=0, st=1, w=K2):
+        return A("sf", NS * k + o, NS * k + w, st)
 
-    def J(n, k, o=1, st=2, w=224):
+    def S(n, k, st):
+        return A(n, k, st * K2, st)
+
+    def J(n, k, o=1, st=2, w=208):
         k = k % 2 if n == "jp" else (k and 1 + k % 2) if n == "jn" else k % 3
         return A(n, 256 * k + o, 256 * k + w, st)
 
     def slots_to_d(k):
         lo = 768 + 128 * k
-        scan(A("jp", lo, lo + NS), A("jp", 512, 512 + NS), J("jp", k), ALU.add, ALU.max)
+        scan(A("jp", lo, lo + NS), A("jp", 512, 512 + NS), J("jp", k, w=224), ALU.add, ALU.max)
         return A("jp", lo + 15, lo + NS, 16)
 
     def E(b):
@@ -509,6 +536,12 @@ def rank_program(g, core, T, topo):
                 mm(b, *E(b), A(q, 0, C), A(p, 0, C), q2, p2, A("l3", 0, 7))
                 act(A("wn%d" % w, WN * b + 1, WN * b + 2 * C, 2), A("ps", 512 * b, 512 * b + C), scale=0.5, behind=r)
 
+    def pair_means(w, l):
+        for b in range(4):
+            o = NS * (4 * w + b)
+            act(A("gj", o, o + NS), IND(A("wn%d" % w, WN * b, WN * b + 768), l), scale=0.5)
+            scan(A("wn%d" % w, WN * b + 768, WN * b + WN), A("zj"), A("gj", o, o + NS), ALU.mult, ALU.add)
+
     scores(0, 0, False)
     scores(1, 2, False)
     for t in range(3):
@@ -519,7 +552,7 @@ def rank_program(g, core, T, topo):
             l = A("l3", 8 * k, 8 * k + 7)
             act(A("r3", k, 336, 3), IND(A("sr"), l))
             tt(A("x1", k, 336, 3), IND(A("sr"), l), A("lm", k, 336, 3), ALU.max)
-        iota(A("inv"), [[0, 784]], -15, 0, [A("l3", 0, 7)] if t else [])
+        iota(A("inv"), [[0, 784]], -17, 0, [A("l3", 0, 7)] if t else [])
         r = ranks(N2, 3 * K2, lambda a, b: A("r3", a, b), NA[2], "ac0")
         for k in range(3):
             act(A("k2", k, 336, 3), IND(A("pk" if t else "cpk"), A("l3", 8 * k, 8 * k + 7)))
@@ -533,17 +566,18 @@ def rank_program(g, core, T, topo):
         dd, ab, cc, cc2, mb, hi, neg, rd_, mc = [sf(k) for k in range(9)]
         ts(A("du", 0, 7), d, c384, ALU.subtract, 1.0 / 1024, ALU.mult)
         ts(pi, d, corr, ALU.subtract)
-        cp(PK, A("ew", 0, NS))
+        cp(PK, A("ew", 0, K2))
         ts(ei, pi, 10, ALU.logical_shift_right)
         ts(oi_, pi, 1023, ALU.bitwise_and)
-        cp(A("du", 8, 15), oi_)
         cp(IND(A("inv"), A("du", 0, 7)), A("rx"))
-        act(J("jp", 0), IND(A("inv"), A("du", 8, 15)))
-        act(cc, J("jp", 0), bias=56 * 2.0 ** 18 + 2.0 ** 17 - 240 * 2.0 ** 16, scale=-2.0 ** 16)
+        soft.add((len(ops) - 2, len(ops) - 1))
+        cp(A("du", 8, 15), oi_)
+        act(J("jp", 0, w=224), IND(A("inv"), A("du", 8, 15)))
+        act(cc, J("jp", 0), bias=1.5 * 2.0 ** 41 - 4 * 2.0 ** 18, scale=-2.0 ** 16)
+        act(cc2, cc, bias=-1.5 * 2.0 ** 41)
         ts(PE, PK, 10, ALU.logical_shift_right, 1022, ALU.bitwise_and)
         d = slots_to_d(0)
         ts(A("du", 16, 23), d, cb15, ALU.subtract)
-        ts(cc2, cc, 1.5 * 2.0 ** 41, ALU.add, 1.5 * 2.0 ** 41, ALU.subtract)
         if t:
             ts(PO, PK, 1022, ALU.bitwise_and)
             ts(LF, PK, 1, ALU.bitwise_and)
@@ -551,27 +585,23 @@ def rank_program(g, core, T, topo):
             act(ab, dd, AF.Abs, scale=0.5)
             act(J("ja", 0), ab, bias=1.0)
             tt(J("jn", 0), PE, PO, ALU.min)
-            cp(A("v1", 2, 336, 3), PO)
-            act(mc, A("v1", 2, 336, 3), bias=512.0, scale=256.0)
-            tt(mb, mc, J("ja", 0), ALU.add)
-            act(A("t1", 2, 336, 3), ab, bias=-1.0, scale=-1.0)
-            act(A("v1", 1, 336, 3), dd, scale=-1.0)
+            cp(S("v1", 2, 3), PO)
+            act(mc, S("v1", 2, 3), bias=513.0, scale=256.0)
+            tt(mb, mc, ab, ALU.add)
+            act(S("t1", 2, 3), ab, bias=-1.0, scale=-1.0)
+            act(S("v1", 1, 3), dd, scale=-1.0)
             act(rd_, dd, AF.Relu, scale=-0.5)
-            tt(A("q1", 1, 224, 2), LF, rd_, ALU.subtract)
+            tt(S("q1", 1, 2), LF, rd_, ALU.subtract)
         else:
             cp(J("jn", 0), PE)
-            act(A("v1", 2, 336, 3), J("jn", 0))
+            act(S("v1", 2, 3), J("jn", 0))
             act(mb, J("jn", 0), bias=513.0, scale=256.0)
         tt(J("jm", 0), cc2, mb, ALU.add)
-        tt(A("v1", 0, 336, 3), A("jc"), PE, ALU.subtract)
+        tt(S("v1", 0, 3), A("jc", 0, K2), PE, ALU.subtract)
         ts(A("di", 24, 31), pi, 10, ALU.logical_shift_right, 1022, ALU.bitwise_and)
         cp(A("du", 104, 111), A("di", 24, 31))
         send(A("du", 104, 112), A("sl%d" % t), "j", t, False)
-        for w, l in enumerate((A("du", 104, 111), A("sl%d" % t, 0, 7))):
-            for b in range(4):
-                o = NS * (4 * w + b)
-                act(A("gj", o, o + NS), IND(A("wn%d" % w, WN * b, WN * b + 768), l), scale=0.5)
-                scan(A("wn%d" % w, WN * b + 768, WN * b + WN), A("zj"), A("gj", o, o + NS), ALU.mult, ALU.add)
+        pair_means(0, A("du", 104, 111))
         lc, dn, mxp = A("du", 64, 71), A("df", 8, 15), A("df", 56, 63)
         ts(A("df", 0, 7), d, c225, ALU.not_equal)
         tt(dn, A("df", 0, 7), jl2, ALU.mult)
@@ -586,46 +616,48 @@ def rank_program(g, core, T, topo):
         for k in range(6):
             l = A("du", 16 + 8 * k, 23 + 8 * k)
             if k < 5:
-                act(J("jp", k + 1), IND(J("jp", k, 0, 1, 226), l))
+                act(J("jp", k + 1, w=224), IND(J("jp", k, 0, 1, 226), l))
                 ts(A("du", 24 + 8 * k, 31 + 8 * k), slots_to_d(k + 1), cb15, ALU.subtract)
                 act(sf(9 + k % 2), J("ja", k))
-                tt(J("ja", k + 1), IND(J("ja", k, 0, 1, 226), l), sf(9 + k % 2), ALU.add)
+                tt(J("ja", k + 1, w=224), IND(J("ja", k, 0, 1, 226), l), sf(9 + k % 2, w=NS), ALU.add)
             act(sf(11 + k % 2), J("jn", k))
-            tt(J("jn", k + 1), IND(J("jn", k, 0, 1, 226), l), sf(11 + k % 2), ALU.min)
-            act(A("jy", 224 * k + 1, 224 * k + 224, 2), J("jm", k))
-            act(A("jy", 224 * k, 224 * k + 224, 2), IND(J("jm", k, 0, 1, 226), l))
-            scan(J("jm", k + 1, 0, 1), J("ja", k, 0, 1), A("jy", 224 * k, 224 * k + 224), ALU.add, ALU.min)
-        m, nm, nc, cb = J("jm", 6), sf(13), A("tz", 1, 336, 3), A("vz", 2, 336, 3)
+            tt(J("jn", k + 1, w=224), IND(J("jn", k, 0, 1, 226), l), sf(11 + k % 2, w=NS), ALU.min)
+            cp(A("jy", 224 * k + 1, 224 * k + 208, 2), J("jm", k))
+            for a, b in ((0, 4), (4, 7)):
+                act(A("jy", 224 * k + 32 * a, 224 * k + 32 * b, 2), IND(J("jm", k, 0, 1, 226), A("du", l[1] + a, l[1] + b)))
+                e = min(32 * b, 208)
+                scan(J("jm", k + 1, 32 * a, 1, e), J("ja", k, 32 * a, 1, e), A("jy", 224 * k + 32 * a, 224 * k + e), ALU.add, ALU.min)
+        m, nm, nc, cb = J("jm", 6), sf(13), S("tz", 1, 3), S("vz", 2, 3)
         for j in range(2):
             tt(sf(13, j, 2), J("jn", 6, 1, 4), J("jn", 6, 3, 4), ALU.min)
-        tt(A("tz", 2, 336, 3), J("jn", 0), nm, ALU.is_equal)
+        tt(S("tz", 2, 3), J("jn", 0), nm, ALU.is_equal)
         ts(hi, m, 2.0 ** 32 - 256.0, ALU.add, 2.0 ** 32, ALU.subtract)
-        tt(nc, m, A("pn"), ALU.is_lt)
-        tt(A("t1", 1, 336, 3), m, hi, ALU.subtract)
+        tt(nc, m, A("pn", 0, K2), ALU.is_lt)
+        tt(S("t1", 1, 3), m, hi, ALU.subtract)
         for j in range(2):
-            tt(A("t1", 3 * j, 336, 6), J("jm", 6, 3 - 2 * j, 4), sf(5, 1 - j, 2), ALU.subtract)
-            tt(A("vz", 2 + 3 * j, 336, 6), J("jm", 6, 3 - 2 * j, 4), J("jm", 6, 1 + 2 * j, 4), ALU.is_gt if j else ALU.is_ge)
-        scan(A("t2"), A("tz"), A("t1"), ALU.mult, ALU.add)
+            tt(A("t1", 3 * j, 312, 6), J("jm", 6, 3 - 2 * j, 4), sf(5, 1 - j, 2), ALU.subtract)
+            tt(A("vz", 2 + 3 * j, 312, 6), J("jm", 6, 3 - 2 * j, 4), J("jm", 6, 1 + 2 * j, 4), ALU.is_gt if j else ALU.is_ge)
+        scan(A("t2", 0, 312), A("tz", 0, 312), A("t1", 0, 312), ALU.mult, ALU.add)
         cp(IND(A("tl"), lc), A("t2", 2, 336, 3))
         ms(col("cum", 7), 512.0)
         scan(A("cum", 8, 8 + C), A("onp"), A("tl", 7, 7 + C), ALU.add, ALU.add, 512.0)
-        d = to_d("js", nm, NS, NS)
+        d = to_d("js", sf(13, w=NS), NS, NS)
         ts(A("du", 72, 79), d, c14, ALU.subtract, 0.5, ALU.mult)
-        act(A("nz", 1, 224, 2), cb, bias=1.0, scale=-2.0)
-        act(sf(14), A("t2", 1, 336, 3), bias=0.0 if t else 0.5, scale=0.5)
-        act(A("n1", 1, 224, 2), A("t2", 1, 336, 3), bias=-1.0 if t else -0.5, scale=0.5)
-        tt(A("n1", 0, 224, 2), sf(14), A("t1", 1, 336, 3), ALU.subtract)
-        scan(A("n2"), A("nz"), A("n1"), ALU.mult, ALU.add)
+        act(S("nz", 1, 2), cb, bias=1.0, scale=-2.0)
+        act(sf(14), S("t2", 1, 3), bias=0.0 if t else 0.5, scale=0.5)
+        act(S("n1", 1, 2), S("t2", 1, 3), bias=-1.0 if t else -0.5, scale=0.5)
+        tt(S("n1", 0, 2), sf(14), S("t1", 1, 3), ALU.subtract)
+        scan(A("n2", 0, 208), A("nz", 0, 208), A("n1", 0, 208), ALU.mult, ALU.add)
         tt(A("q1", 0, 224, 2), IND(A("cum"), A("du", 72, 79)), A("n2", 1, 224, 2), ALU.add)
         if t:
             tt(neg, cb, LF, ALU.is_equal)
-            act(A("qz", 1, 224, 2), neg, bias=1.0, scale=-2.0)
-            scan(A("q2"), A("qz"), A("q1"), ALU.mult, ALU.add)
+            act(S("qz", 1, 2), neg, bias=1.0, scale=-2.0)
+            scan(A("q2", 0, 208), A("qz", 0, 208), A("q1", 0, 208), ALU.mult, ALU.add)
         cp(IND(A("cum"), lc), A("q2", 1, 224, 2) if t else A("q1", 0, 224, 2))
-        act(A("vz", 1, 336, 3), nc)
-        for lo, hi in ((0, 192), (192, 336)):
+        act(S("vz", 1, 3), nc)
+        for lo, hi in ((0, 192), (192, 312)):
             scan(A("v2", lo, hi), A("vz", lo, hi), A("v1", lo, hi), ALU.mult, ALU.add)
-        d = to_d("js", cb, NS, 2 * NS)
+        d = to_d("js", A("vz", 2, 336, 3), NS, 2 * NS)
         ts(A("df", 72, 79), d, chalf, ALU.is_lt)
         tt(A("df", 80, 87), A("df", 72, 79), dn, ALU.mult)
         tt(A("df", 88, 95), A("df", 80, 87), mxp, ALU.max)
@@ -642,6 +674,7 @@ def rank_program(g, core, T, topo):
             tt(A("df", 128, 152), A("df", 96, 120), d, ALU.max)
         ts(pos, A("df", 128, 152) if t else d, c512, ALU.subtract)
         cp(IND(A("vw"), pos), A("v0", 0, C))
+        pair_means(1, A("sl%d" % t, 0, 7))
         for h in (1, 0):
             l = A("pl", 32 * t + 16 * h, 32 * t + 16 * h + 12)
             ts(l, to_d("sc2", A("vw", H * h, H * h + H), H, H * h), corr, ALU.subtract)

import numpy as np
from concourse.mybir import dt, AluOpType as ALU, ActivationFunctionType as AF, AxisListType as AX

C, H, K2, NS = 384, 192, 104, 112
N1, N2 = 256, 320
WN = 880
BIG = 2.0 ** 20
STEP = [1, 2, 1]
WAKE, FAR, CYC, PEC = 200.0, 3300.0, 0.83, 1.2
LOOK = {"v": 250.0, "a": 300.0, "p": 0.0, "g": 300.0, "s": 0.0, "r": 0.0}
TOL, TURNS, SPAN, SHAKE = 40.0, 1500, 1500.0, 400.0
KEPT = []
NA = (7, 9, 8)
YA = (2, 2)
NB = 4
F, B, I, U, Q, S8 = "float32", "bfloat16", "int32", "uint16", "float8_e4m3fn_x4", "uint8"


def _sb(n, d):
    return ("sbuf", [128, n], d)


SCRATCH = {
    "xin": _sb(1544, B), "uin": _sb(512, B), "vin": _sb(512, B), "ein": _sb(2048, B), "ones": _sb(N2, B), "on5": _sb(256, B),
    "xt": _sb(1536, B), "yt": _sb(1536, B), "wn0": _sb(4 * WN, B), "wn1": _sb(4 * WN, B), "gj": _sb(8 * NS, B), "rl": _sb(1536, F),
    "wq": _sb(512, Q), "wsc": _sb(512, S8), "uq": _sb(128, Q), "us": _sb(128, S8), "vq": _sb(128, Q), "vs": _sb(128, S8),
    "u2q": _sb(256, Q), "u2s": _sb(256, S8), "eq": _sb(512, Q), "es": _sb(512, S8),
    "xq": _sb(C + 2, Q), "xs": _sb(C + 2, S8), "xq2": _sb(2 * C, Q), "xs2": _sb(2 * C, S8), "zq": _sb(C, Q), "zs": _sb(C, S8),
    "pq0": _sb(C + 2, Q), "pq1": _sb(C + 2, Q), "pq2": _sb(C + 2, Q), "pp0": _sb(C + 2, S8), "pp1": _sb(C + 2, S8), "pp2": _sb(C + 2, S8),
    "sl0": _sb(8, U), "sl1": _sb(8, U), "sl2": _sb(8, U), "nl0": _sb(12, U), "nl1": _sb(12, U), "nl2": _sb(12, U), "pl": _sb(96, U),
    "ps": ("psum", [128, 4096], F),
    "t16": _sb(80, F), "lm": _sb(336, F), "c0": _sb(N2, F), "zr": _sb(N2, B), "c3": _sb(H, F),
    "cv": _sb(C, F), "ik": _sb(776, F), "alt": _sb(WN, F),
    "selt": _sb(N1, B), "cpk": _sb(776, F), "cpv": _sb(C, F), "rx": _sb(NS, F), "pn": _sb(NS, F), "jc": _sb(NS, F),
    "cs": _sb(224, F), "ci": _sb(8, I), "cu": _sb(64, U), "z4": _sb(48, F), "zj": _sb(NS, B),
    "ac0": _sb(112, F), "ac1": _sb(112, F),
    "fb": _sb(400, F), "fr": _sb(C, F), "fc": _sb(C, F), "kr": _sb(C, F), "pk": _sb(776, F), "cap": _sb(392, F),
    "hc": _sb(C, F), "onp": _sb(C, F), "kd": _sb(160, F), "sc": _sb(C, F), "sc2": _sb(C, F), "sc3": _sb(C, F), "dk": _sb(128, I),
    "sr": _sb(776, F), "w3": _sb(768, F), "x1": _sb(336, F), "x2": _sb(N2, F), "x3": _sb(N2, B), "x4": _sb(N2, B),
    "cmp": _sb(12 * N2, B), "cum2": _sb(12 * N2, B), "tau": _sb(11 * N2, B), "junk": _sb(4 * N2, B), "acc": _sb(128, F), "ru": _sb(32, U),
    "sel": _sb(N1, B), "pre": _sb(N1, B), "cnt": _sb(4 * 168, B), "l3": _sb(24, U), "r3": _sb(336, F), "k2": _sb(336, F), "ew": _sb(N2, F),
    "di": _sb(64, I), "df": _sb(256, F), "du": _sb(160, U), "inv": _sb(784, F),
    "jp": _sb(8 * 128 + 512, B), "ja": _sb(768, F), "jm": _sb(1024, F), "jn": _sb(768, F), "jy": _sb(6 * 224, F), "js": _sb(3 * NS, F),
    "tz": _sb(336, F), "t1": _sb(336, F), "t2": _sb(336, F), "vz": _sb(336, F), "v1": _sb(336, F), "v2": _sb(336, F),
    "nz": _sb(224, F), "n1": _sb(224, F), "n2": _sb(224, F), "qz": _sb(224, F), "q1": _sb(224, F), "q2": _sb(224, F),
    "si": _sb(4 * NS, I), "sf": _sb(16 * NS, F),
    "tl": _sb(520, F), "cum": _sb(520, F), "v0": _sb(520, F), "qs": _sb(C, F),
    "vw": _sb(C, F), "of": _sb(C, F), "yo": _sb(C, F),
}
SEMAPHORES = (["v", "a", "p", "g"] + ["d%d" % i for i in range(1, 38)]
              + ["%s%d" % (n, t) for n in ("ln", "lc", "ls", "lj", "rn", "rc", "rs", "rj") for t in range(3)])


def A(n, lo=0, hi=None, st=1):
    return (n, lo, SCRATCH[n][1][1] if hi is None else hi, st)


def half(*xs):
    return 0.5 if all(x[0] != "*" and SCRATCH[x[0]][2] in (B, U) for x in xs) else 1.0


def col(n, c):
    return (n, c, c + 1, 1)


def IND(w, o):
    return ("*", w, o)


def rank_program(g, core, T, topo):
    rank = T.rank_of(core)
    if rank is None:
        return
    eng = {"v": g.vector, "a": g.scalar, "p": g.tensor, "g": g, "s": g.sync}
    ops, nd, soft = [], [0], set()
    lastw = {n: np.full(v[1][1], -1) for n, v in SCRATCH.items()}
    reads = {n: [] for n in SCRATCH}
    bank = [{} for _ in range(8)]

    def ap(x):
        if not isinstance(x, tuple):
            return x
        if x[0] == "*":
            return ap(x[1]).indirect(ap(x[2]))
        return T[x[0]][:, x[1]:x[2]:x[3]] if x[3] != 1 else T[x[0]][:, x[1]:x[2]]

    def note(e, rd, wr, call, sem, inc, busy, lat):
        need, me, r2, w2 = set(), len(ops), [], []
        for x in rd:
            if isinstance(x, tuple):
                r2 += [x[1], x[2]] if x[0] == "*" else [x]
        for x in wr:
            if x[0] == "*":
                w2.append(x[1])
                r2.append(x[2])
            else:
                w2.append(x)
        for x in r2 + w2:
            need.update(np.unique(lastw[x[0]][x[1]:x[2]:x[3]]).tolist())
            if x[0] == "ps":
                for b in range(x[1] // 512, (x[2] - 1) // 512 + 1):
                    need.update(i for k, v in bank[b].items() if k != e for i in v)
                    bank[b] = {e: bank[b].get(e, []) + [me]}
        for x in w2:
            mine, keep = set(range(x[1], x[2], x[3])), []
            for i, cols in reads[x[0]]:
                if cols & mine:
                    need.add(i)
                if not cols <= mine:
                    keep.append((i, cols))
            reads[x[0]] = keep
        for x in r2:
            reads[x[0]].append((me, set(range(x[1], x[2], x[3]))))
        for x in w2:
            lastw[x[0]][x[1]:x[2]:x[3]] = me
        need.discard(-1)
        need.discard(me)
        ops.append((e, sorted(need), call, sem, inc, busy, lat))

    def run(e, rd, wr, call, per=1.0, more=0.0):
        x = rd[0] if rd else wr[0]
        n = len(range(*wr[0][1:])) if wr[0][0] != "*" else len(range(*x[1:]))
        if wr[0][0] == "*":
            c = 50 + 3.8 * CYC * n
        elif x[0] == "*":
            c = (50 if e == "v" else 65) + 1.56 * CYC * n
        elif e in "va":
            c = max(64, per * len(range(*x[1:]))) * CYC
        else:
            c = 130 + 2.6 * CYC * n if e == "g" else per * CYC * (16 + n)
        note(e, rd, wr, lambda s: call().then_inc(T.sem[s], 1), e, 1, c + more, c + more)

    def plan(before, after, way, back):
        n = len(ops)
        left, ready, free = [len(x) for x in before], [ops[i][6] - ops[i][5] if back else 0.0 for i in range(n)], {e: 0.0 for e in list(eng) + ["r"]}
        cand = {e: [i for i in range(n) if ops[i][0] == e and not left[i]] for e in free}
        order, over = [], [0.0] * n
        for _ in range(n):
            now, e = min((max(free[e], min(ready[i] for i in c)), e) for e, c in cand.items() if c)
            i = -max((way[i], -i) for i in cand[e] if ready[i] <= now + LOOK[e])[1]
            fit = [(way[j], -j) for j in cand[e] if max(now, ready[j]) + ops[j][5] <= ready[i] + TOL]
            if ready[i] > now and fit:
                i = -max(fit)[1]
            cand[e].remove(i)
            now = max(now, ready[i])
            free[e] = now + ops[i][5]
            over[i] = now + ops[i][5 if back else 6]
            order.append(i)
            for j in after[i]:
                if (min(i, j), max(i, j)) not in soft:
                    ready[j] = max(ready[j], over[i] + WAKE + (ops[j][6] - ops[j][5] if back else 0.0))
                left[j] -= 1
                if not left[j]:
                    cand[ops[j][0]].append(j)
        return order, over

    def issue():
        n = len(ops)
        before, after, way = [o[1] + [a for a, b in soft if b == i] for i, o in enumerate(ops)], [[] for _ in ops], [0.0] * n
        for i in range(n):
            for d in before[i]:
                after[d].append(i)
        for i in range(n - 1, -1, -1):
            way[i] = ops[i][6] + max([way[j] + WAKE for j in after[i]] + [0.0])
        if not KEPT:
            tries = []
            for _ in range(3):
                order, over = plan(before, after, way, False)
                tries.append((max(over), order, way))
                way = plan(after, before, over, True)[1]
            kept, rng = min(tries), np.random.default_rng(1)
            for _ in range(TURNS):
                lo = rng.random() * kept[0]
                way = [w + (x if lo < w < lo + SPAN else 0.0) for w, x in zip(kept[2], (rng.normal(size=n) * SHAKE).tolist())]
                order, over = plan(before, after, way, False)
                if max(over) <= kept[0]:
                    kept = (max(over), order, way)
            KEPT.append(kept[1])
        tok, cnt, seen = [None] * n, {}, {e: {} for e in eng}
        for i in KEPT[0]:
            e, need, call, sem, inc = ops[i][:5]
            cnt[sem] = cnt.get(sem, 0) + inc
            tok[i] = (sem, cnt[sem])
            if e == "r":
                continue
            most = {}
            for d in need:
                most[tok[d][0]] = max(most.get(tok[d][0], 0), tok[d][1])
            for s in sorted(most):
                if seen[e].get(s, 0) < most[s]:
                    eng[e].wait_ge(T.sem[s], most[s])
                    seen[e][s] = most[s]
            call(sem)
        for s in sorted(cnt):
            g.wait_ge(T.sem[s], cnt[s])

    def tt(o, a, b, op):
        run("v", [a, b], [o], lambda: g.vector.tensor_tensor(ap(o), ap(a), ap(b), op), 1.0 if "ps" in (a[0], b[0]) else 2.0)

    def ts(o, a, s1, op0, s2=None, op1=None):
        if op1 is None:
            run("v", [a, s1], [o], lambda: g.vector.tensor_scalar(ap(o), ap(a), ap(s1), None, op0), half(o, a))
        else:
            run("v", [a, s1, s2], [o], lambda: g.vector.tensor_scalar(ap(o), ap(a), ap(s1), ap(s2), op0, op1), half(o, a))

    def cp(o, a):
        run("v", [a], [o], lambda: g.vector.tensor_copy(ap(o), ap(a)))

    def ms(o, c):
        run("v", [], [o], lambda: g.vector.memset(ap(o), c), half(o))

    def scan(o, a, b, op0, op1, first=0.0):
        run("v", [a, b, first], [o], lambda: g.vector.tensor_tensor_scan(ap(o), ap(a), ap(b), ap(first), op0, op1), half(o, a, b))

    def red(o, a):
        run("v", [a], [o], lambda: g.vector.tensor_reduce(ap(o), ap(a), AX.X, ALU.add))

    def act(o, a, f=None, bias=None, scale=None, acc=None, behind=None):
        kw = {}
        if bias is not None:
            kw["bias"] = ap(bias)
        if scale is not None:
            kw["scale"] = scale
        if acc is not None:
            kw["accum_out"] = ap(acc)
        fn = f if f is not None else (AF.Copy if bias is None and acc is None else AF.Identity)
        run("a", [a, bias, behind], [o] + ([acc] if acc else []), lambda: g.scalar.activation(ap(o), ap(a), fn, **kw), 1.0,
            (20.0 if acc else 0.0) + (0.0 if a[0] == "*" else 15.0))

    def fill(o, c):
        iota(o, [[0, len(range(*o[1:]))]], c)

    def iota(o, pat, base, cm=0, behind=()):
        if SCRATCH[o[0]][2] == I:
            run("g", [], [o], lambda: g.iota(ap(o), pat, base, cm))
        else:
            run("g", list(behind), [o], lambda: g.iota(ap(o), pat, base, cm, allow_small_or_imprecise_dtypes=True))

    def qz(oq, os_, a):
        run("v", [a], [oq, os_], lambda: g.vector.quantize_mx(ap(oq), ap(os_), ap(a)), 0.27)

    def mm(b, wq, ws, xq, xs, xq2=None, xs2=None, behind=None):
        o = A("ps", 512 * b, 512 * b + xq[2] - xq[1])

        def call():
            if xq2 is None:
                return g.tensor.matmul_mx(ap(o), ap(wq), ap(ws), ap(xq), ap(xs), True, True)
            g.tensor.matmul_mx(ap(o), ap(wq), ap(ws), ap(xq), ap(xs), True, False)
            return g.tensor.matmul_mx(ap(o), ap(wq), ap(ws), ap(xq2), ap(xs2), False, True)
        run("p", [wq, ws, xq, xs, xq2, xs2, behind], [o], call, PEC if xq2 is None else 2 * PEC)

    def dma(e, rd, wr, out, in_, lat=2500.0):
        nd[0] += 1
        note(e, rd, wr, lambda s: eng[e].dma_start(out, in_).then_inc(T.sem[s], 16), "d%d" % nd[0], 16, 60.0, lat)

    def send(src, dst, kind, t, cast):
        to = T.cores[rank ^ STEP[t]]
        rid, pid = topo.addr(to)[:2]
        a, b = (ap(dst).bitcast(dt.uint8), ap(src).bitcast(dt.uint8)) if cast else (ap(dst), ap(src))
        note("g", [src], [], lambda s: g.remote_dma(a, b, T.sem["r%s%d" % (kind, t)], T.sem[s], pid, rid, topo.mask(core, to)),
             "l%s%d" % (kind, t), len(topo.engines(core, to)), 500.0 if t or kind != "c" else 4000.0, FAR * (3 if kind in "cs" else 1))
        ops.append(("r", [len(ops) - 1], None, "r%s%d" % (kind, t), len(topo.engines(to, core)), 0.0, 0.0))
        lastw[dst[0]][dst[1]:dst[2]] = len(ops) - 1

    def to_d(tmp, src, n, lo=0):
        scan(A(tmp, lo, lo + n), A("cv", 0, n), src, ALU.add, ALU.max)
        return A(tmp, lo + 15, lo + n, 16)

    qf, q1, corr = col("cs", 0), col("cs", 1), col("cs", 2)
    c14, c384, c512, c225, chalf, corr2 = [col("cs", 3 + k) for k in range(5)] + [col("cs", 39)]
    kD, kB, kP, cb15 = A("cs", 8, 32), 32, 40, col("cs", 47)
    jl2, padv, k1D, i16, km, k2D, ce = A("cs", 56, 63), A("cs", 64, 71), A("cs", 72, 96), A("cs", 96, 120), A("cs", 120, 144), A("cs", 144, 168), 168

    dma("a", [], [A("uin")], T.uin[:], T.u[:])
    dma("s", [], [A("xin", 0, 768)], T.xin[:, 0:768], T.x[:, 0:768], 3000.0)
    dma("a", [], [A("xin", 768, 1536)], T.xin[:, 768:1536], T.x[:, 768:1536], 3500.0)
    dma("s", [], [A("xin", 1536, 1544)], T.xin[:, 1536:1544], T.x[:, 0:8])
    iota(col("ci", 0), [[0, 1]], 0, 1)
    iota(i16, [[16, 24]], 0)
    iota(A("t16", 0, 16), [[1, 16]], 0)
    fill(A("ones"), 1)
    ms(A("c0"), 0.0)
    ms(A("zr"), -1e4)
    ms(A("c3"), 0.0)
    cp(A("cu", 0, 8), A("cs", 96, 104))
    ts(A("cu", 8, 16), A("cs", 96, 104), 1.0, ALU.add)
    ts(col("ci", 1), col("ci", 0), 15, ALU.bitwise_and)
    ms(A("c0", 0, N2, 16), 5e29)
    ms(A("c3", 0, H, 3), -3e29)
    cp(qf, col("ci", 1))
    ms(A("zr", 0, N2, 16), -128.0)
    ts(q1, qf, 1.0, ALU.add)
    ts(corr, qf, 15.0, ALU.is_lt, 2.0 ** 21, ALU.mult)
    ts(kD, i16, qf, ALU.add)
    fill(A("selt", 0, K2), 1)
    fill(A("selt", K2, N1), 0)
    ts(A("cs", kP, kP + 7), A("cs", 8, 15), 0.5, ALU.add)
    ts(A("cs", kB, kB + 7), A("cs", 8, 15), 0.5, ALU.add, -1.0, ALU.mult)
    ts(A("cu", 40, 64), i16, 0.0, ALU.mult, qf, ALU.add)
    ts(A("t16", 16, 32), A("t16", 0, 16), qf, ALU.not_equal, 8e29, ALU.mult)
    act(A("lm"), IND(A("t16", 16, 32), A("cu", 40, 61)), bias=-3e29)
    ms(A("z4"), 1.0)
    ms(A("z4", 0, 48, 4), 0.0)
    ms(A("z4", 1, 48, 4), -1.0)
    fill(A("ac0", 0, 48), 0)
    fill(A("ac1", 0, 48), 0)
    ms(A("sr", 768, 776), -2e29)
    ts(A("cs", ce, ce + 12), A("cs", 97, 109), 128.0, ALU.add)
    ms(A("on5", 0, 128), 1.0)
    run("g", [A("on5", 0, 128)], [A("on5", 128, 256)],
        lambda: g.affine_select(T.on5[:, 128:256], T.on5[:, 0:128], [[-1, 128]], ALU.is_equal, 0.0, 0, 1))
    ms(A("ein"), 0.0)
    for b in range(4):
        act(A("ein", 512 * b + b, 512 * b + 512, 4), A("on5", 128, 256))
    qz(A("eq"), A("es"), A("ein"))
    qz(A("uq"), A("us"), A("uin"))
    soft.add((len(ops) - 2, len(ops) - 1))

    def repeat_u(k):
        o, w, l = A("u2q", 128 * k, 128 * k + 128), A("uq"), A("cu", 8 * k, 8 * k + 8)
        run("v", [IND(w, l)], [o], lambda: g.vector.tensor_copy(ap(o).bitcast(dt.uint32), ap(w).bitcast(dt.uint32).indirect(ap(l))))
        act(A("u2s", 128 * k, 128 * k + 128), IND(A("us"), l))

    repeat_u(0)
    repeat_u(1)
    qz(A("xq", 0, H), A("xs", 0, H), A("xin", 0, 768))
    qz(A("xq", H, C + 2), A("xs", H, C + 2), A("xin", 768, 1544))
    dma("s", [A("xin")], [A("wq")], T.wq[:].bitcast(dt.uint8), T.wc[:])
    dma("s", [A("xin")], [A("wsc")], T.wsc[:], T.ws[:])
    dma("s", [A("xin")], [A("vin")], T.vin[:], T.v[:])
    ts(A("t16", 32, 48), A("t16", 0, 16), qf, ALU.is_equal, -4.0, ALU.mult)
    ts(A("t16", 48, 64), A("t16", 0, 16), q1, ALU.is_equal)
    tt(A("t16", 64, 80), A("t16", 32, 48), A("t16", 48, 64), ALU.add)
    act(A("cv"), IND(A("t16", 64, 80), A("cu", 40, 64)), scale=2.0 ** 21)
    act(A("jp", 512, 512 + NS), IND(A("t16", 64, 80), A("cu", 40, 47)), scale=242.0)
    iota(A("cpk"), [[2050, 388], [1023, 2]], 1)
    iota(A("rx", 0, K2), [[4, 52], [-2, 2]], 3 - 242)
    iota(A("ja", 0, 768, 2), [[0, 384]], 2 ** 24 - 1)
    iota(A("jp", 0, 512), [[0, 512]], -17)
    ts(cb15, qf, 15.0, ALU.is_ge, -242.0, ALU.mult)
    for n in ("t2", "v2", "vz"):
        iota(A(n, 3 * K2, 3 * NS), [[0, 24]], 0)
    for n in ("n2", "q2"):
        iota(A(n, 2 * K2, 2 * NS), [[0, 16]], 0)
    iota(A("sf", 9 * NS, 14 * NS), [[0, 5 * NS]], 0)
    for k in range(3):
        iota(A("jm", 256 * k + 2 * K2, 256 * k + 2 * NS), [[0, 16]], 0)
    ts(c225, cb15, 225.0, ALU.add)
    iota(A("jn"), [[0, 768]], 1000000)
    iota(A("n2", 0, NS), [[-1, 56], [0, 2]], 56)
    iota(A("jc"), [[2, 56], [0, 2]], 769)
    for w in ("wn0", "wn1"):
        for lo in range(0, 4 * WN, 2 * WN):
            dma("s", [A("ein")], [A(w, lo, lo + 2 * WN)], T[w][:, lo:lo + 2 * WN], T.ein[:, 0:2 * WN])
    iota(A("zj"), [[0, NS // 2], [1, 2]], 0)
    ms(A("du", 104, 112), 0)
    for n in ("tz", "vz"):
        iota(A(n, 0, 336, 3), [[0, NS]], 0)
    for n in ("nz", "qz"):
        iota(A(n, 0, 224, 2), [[0, NS]], 0)
    iota(A("cum"), [[0, 520]], 0)
    iota(A("tl"), [[0, 520]], 0)
    iota(A("v0"), [[2, 520]], 0)
    iota(A("onp"), [[0, C]], 1)
    iota(A("ik"), [[1, 776]], 0)
    iota(A("alt"), [[0, WN // 2], [1, 2]], 0)
    iota(A("cpv"), [[-2050, C]], 2050 * (C - 1) + 1)
    act(A("pn"), A("n2", 0, NS), scale=2.0 ** 18)
    fill(A("rx", K2, NS), -17)
    fill(A("ja", 225, 768, 256), 0)
    fill(A("jm", 224, 1024, 256), 2 ** 24 - 1)
    fill(A("jm", 225, 1024, 256), 2 ** 24 - 1)
    fill(A("jm", 0, 208, 2), 0)
    ts(jl2, A("cs", 8, 15), 2.0, ALU.mult, 802.0, ALU.add)
    ts(A("cs", 184, 191), A("cs", 8, 15), 104.0, ALU.is_ge)
    tt(padv, A("cs", 184, 191), jl2, ALU.mult)
    for c, v in ((c14, -14.0), (c384, 384.0), (c512, 512.0), (chalf, 0.5)):
        ts(c, corr, v, ALU.add)
    ts(corr2, corr, 2.0, ALU.mult)
    ts(k1D, kD, 1.0, ALU.add)
    ts(km, kD, float(H - 1), ALU.not_equal)
    ts(k2D, kD, 2.0, ALU.mult)
    klc = A("kd", 0, 24)
    fill(A("ja", 1, 224, 2), 1)
    fill(A("t1", 2, 336, 3), -1)
    fill(A("v1", 1, 336, 3), 0)
    fill(A("fb", 0, 8), 0)
    fill(A("pk", 768, 776), 0)
    ts(A("cu", 16, 28), A("cs", 8, 20), -1.0, ALU.mult, H - 1.0, ALU.add)
    qz(A("vq"), A("vs"), A("vin"))

    fp, fk = A("fb", 7, 7 + C), A("fb", 8, 8 + C)
    rev = A("cu", 16, 28)

    def tables(t):
        act(A("cap", 0, H + 1), A("fb", 7, 8 + H), bias=1e29, scale=-2e29)
        act(A("cap", H + 1, C + 1), A("fb", 8 + H, 8 + C), bias=1e29, scale=-2e29)
        for h in range(2):
            lo, hi, back = H * h, H * h + H, (H - H * h, C - H * h)
            act(A("fc", lo, hi), A("fb", 7 + lo, 7 + hi), bias=2.0 ** 21, scale=2048.0 - 2.0 ** 21)
            act(A("fr", *back), IND(A("fb", 8 + lo, 8 + hi), rev), bias=-2.0 ** 21, scale=2.0 ** 21 - 2048.0)
            pkr = A("pk", 2 * lo + 1, 2 * hi, 2)
            scan(pkr, A("fc", lo, hi), A("cpk", 2 * lo + 1, 2 * hi, 2), ALU.add, ALU.min)
            to_d("sc3", pkr, H, lo)
            scan(A("kr", *back), A("fr", *back), A("cpv", *back), ALU.add, ALU.max)
            act(A("pk", 2 * lo, 2 * hi, 2), IND(A("kr", *back), rev))
        ts(A("dk", 0, 24), A("sc3", 15, C, 16), corr, ALU.subtract)
        ts(A("dk", 32, 56), A("dk", 0, 24), 1023, ALU.bitwise_and, 1, ALU.logical_shift_right)
        tt(A("kd", 32, 56), k1D, A("dk", 32, 56), ALU.subtract)
        cp(A("dk", 64, 76), A("pl", 32 * t, 32 * t + 12))
        cp(A("dk", 76, 88), A("nl%d" % t))
        ts(A("dk", 96, 120), A("dk", 64, 88), 1, ALU.bitwise_and)
        tt(A("kd", 64, 88), A("dk", 96, 120), km, ALU.mult)
        tt(A("kd", 96, 120), A("kd", 64, 88), A("kd", 32, 56), ALU.mult)
        tt(A("kd", 128, 152), A("kd", 32, 56), A("kd", 96, 120), ALU.subtract)
        ts(klc, A("kd", 128, 152), corr2, ALU.add)
        tt(A("kd", 32, 56), A("kd", 64, 88), k2D, ALU.add)
        cp(A("cu", 40, 64), A("kd", 32, 56))

    def late_tables(r):
        act(A("v0", 0, C), IND(A("ik"), A("cu", 40, 64)), behind=r)
        act(A("hc"), fp, bias=2 * BIG, scale=1.0 - 2 * BIG, behind=r)
        act(A("onp"), fk, bias=1.0, scale=BIG, behind=r)
        act(A("tl", 7, 7 + C), fp, scale=-BIG, behind=r)

    def ranks(n, real, rv, na, acc, mid=0):
        L, cuts = n // 16, [0] + ([mid] if mid else []) + [n]
        for lo, hi in zip(cuts, cuts[1:]):
            for a, b in ((lo, lo + 64), (lo + 64, hi)):
                scan(A("x2", a, b), A("c0", a, b), A("x1", a, b), ALU.add, ALU.min)
            tt(A("x3", lo, hi), A("x2", lo, hi), rv(lo, hi), ALU.is_equal)
            scan(A("x4", lo, hi), A("zr", lo, hi), A("x3", lo, hi), ALU.max, ALU.subtract, -128.0)
        for m in range(na):
            e, j, o = 16 * m + 16, N2 * (m % 4), m * n
            parts = [0, mid, real] if e <= mid else [0, real]
            for lo, hi in zip(parts, parts[1:]):
                act(A("tau", o + lo, o + hi), rv(lo, hi), AF.Sign, bias=col("x2", 16 * m + 15), scale=-1.0)
            act(A("junk", j, j + e), A("tau", o, o + e), AF.Relu, acc=col(acc, 4 * m))
            parts = [e] + parts[1:]
            for k, (lo, hi) in enumerate(zip(parts, parts[1:])):
                if lo < hi:
                    act(A("junk", j + lo, j + hi), A("tau", o + lo, o + hi), AF.Relu, scale=-1.0, acc=col(acc, 4 * m + 1 + k))
        for m in range(na, L):
            k, e, w = col("x2", 16 * m + 15), 16 * m + 16, max(real, 16 * m + 16)
            o = (m - na + 1) * n - w
            ts(A("cmp", o, o + e), rv(0, e), k, ALU.is_ge)
            if e < w:
                ts(A("cmp", o + e, o + w), rv(e, w), k, ALU.is_gt)
            scan(A("cum2", o, o + w), A("ones", 0, w), A("cmp", o, o + w), ALU.mult, ALU.add, col("x4", 16 * m + 15))
        tt(A(acc, 3, 4 * na, 4), A("cs", ce, ce + na), A("x4", 15, 16 * na, 16), ALU.add)
        scan(A(acc, 64, 64 + 4 * na), A("z4", 0, 4 * na), A(acc, 0, 4 * na), ALU.mult, ALU.add)
        cp(A("ru", 0, na), A(acc, 67, 64 + 4 * na, 4))
        ts(A("ru", na, L), A("cum2", n - 1, (L - na) * n, n), 128.0, ALU.add)
        return A("ru", 0, L)

    def best(r):
        cp(A("sel"), IND(A("selt"), r))
        scan(A("pre"), A("ones", 0, N1), A("sel"), ALU.mult, ALU.add)
        w = N1 - K2 + 16
        for m in range(NB):
            o = A("cnt", w * m, w * m + w)
            ts(o, A("pre", 16 * m, 16 * m + w), col("cs", kP + m), ALU.is_lt)
            scan(A("cum2", w * m, w * m + w), A("ones", 0, w), o, ALU.mult, ALU.add, 16.0 * m)
        for m in range(NB, 7):
            j = N2 * (m % 4)
            act(A("junk", j, j + N1 - 16 * NB), A("pre", 16 * NB, N1), AF.Sign, bias=col("cs", kB + m), acc=col("acc", m))
        for k in range(3):
            ts(A("l3", 8 * k, 8 * k + NB), A("cum2", w - 1, w * NB, w), 3.0, ALU.mult, float(k), ALU.add)
            ts(A("l3", 8 * k + NB, 8 * k + 7), A("acc", NB, 7), -1.5, ALU.mult, 1.5 * (N1 + 16 * NB) + k, ALU.add)

    def si(k, o=0, st=1):
        return A("si", NS * k + o, NS * k + K2, st)

    def sf(k, o=0, st=1, w=K2):
        return A("sf", NS * k + o, NS * k + w, st)

    def S(n, k, st):
        return A(n, k, st * K2, st)

    def J(n, k, o=1, st=2, w=208):
        k = k % 2 if n == "jp" else (k and 1 + k % 2) if n == "jn" else k % 3
        return A(n, 256 * k + o, 256 * k + w, st)

    def slots_to_d(k):
        lo = 768 + 128 * k
        scan(A("jp", lo, lo + NS), A("jp", 512, 512 + NS), J("jp", k, w=224), ALU.add, ALU.max)
        return A("jp", lo + 15, lo + NS, 16)

    def E(b):
        return A("eq", 128 * b, 128 * b + 128), A("es", 128 * b, 128 * b + 128)

    def finish(h, b):
        r = A("rl", C * b + H * h, C * b + H * h + H)
        act(r, A("ps", 512 * b, 512 * b + H), AF.Relu, scale=0.015625)
        tt(A("xt", 768 * h + b, 768 * h + 768, 4), A("ps", 512 * (4 + b), 512 * (4 + b) + H), r, ALU.add)

    def half_layer(t, h):
        zq, zs = A("zq", H * h, H * h + H), A("zs", H * h, H * h + H)
        for b in range(4):
            mm(b, A("wq", 128 * b, 128 * b + 128), A("wsc", 128 * b, 128 * b + 128), zq, zs)
            mm(4 + b, *E(b), zq, zs)
            finish(h, b)
        qz(A("xq", H * h, H * h + H), A("xs", H * h, H * h + H), A("xt", 768 * h, 768 * h + 768))

    def scores(h, k0, capped):
        lo, hi = H * h, H * h + H
        for k in range(2):
            mm(k0 + k, A("u2q", 128 * k, 128 * k + 128), A("u2s", 128 * k, 128 * k + 128), A("xq", lo, hi), A("xs", lo, hi))
            o, p = A("sr", 2 * lo + k, 2 * hi, 2), A("ps", 512 * (k0 + k), 512 * (k0 + k) + H)
            if capped:
                tt(o, p, A("cap", k + lo, k + hi), ALU.min)
            else:
                (cp if k else act)(o, p)
        for j in (2 * h, 2 * h + 1):
            scan(A("w3", H * j, H * j + H), A("c3", 0, H), A("sr", H * j, H * j + H), ALU.add, ALU.max)
            tt(A("x1", 64 * j, 64 * j + 64), A("w3", H * j + 2, H * j + H, 3), A("lm", 0, 64), ALU.max)

    def store(h):
        lo, hi = H * h, H * h + H
        mm(6 + h, A("vq"), A("vs"), A("xq", lo, hi), A("xs", lo, hi))
        dma("a", [A("xq", lo, hi)], [], T.oc[:, 4 * lo:4 * hi], T.xq[:, lo:hi].bitcast(dt.uint8))
        cp(A("yo", lo, hi), A("ps", 512 * (6 + h), 512 * (6 + h) + H))
        dma("s", [A("yo", lo, hi)], [], T.y[:, lo:hi], T.yo[:, lo:hi])

    def windows(t, r):
        pairs = (("xq", "xs"), ("pq%d" % t, "pp%d" % t))
        for w, (q, p) in enumerate(pairs):
            for b in range(4):
                mm(4 + b, *E(b), A(q, 0, C), A(p, 0, C), behind=A("l3", 0, 7))
                act(A("wn%d" % w, WN * b, WN * b + 2 * C, 2), A("ps", 512 * (4 + b), 512 * (4 + b) + C), behind=r)
        for w, (q, p) in enumerate(pairs if t else ()):
            q2, p2 = A("xq2", C * w, C * w + C), A("xs2", C * w, C * w + C)
            dma("s", [A(q)], [q2], ap(q2).bitcast(dt.uint8), T[q][:, 1:C + 1].bitcast(dt.uint8))
            dma("s", [A(p)], [p2], ap(p2), T[p][:, 1:C + 1])
            for b in range(4):
                mm(b, *E(b), A(q, 0, C), A(p, 0, C), q2, p2, A("l3", 0, 7))
                act(A("wn%d" % w, WN * b + 1, WN * b + 2 * C, 2), A("ps", 512 * b, 512 * b + C), scale=0.5, behind=r)

    def pair_means(w, l):
        for b in range(4):
            o = NS * (4 * w + b)
            act(A("gj", o, o + NS), IND(A("wn%d" % w, WN * b, WN * b + 768), l), scale=0.5)
            scan(A("wn%d" % w, WN * b + 768, WN * b + WN), A("zj"), A("gj", o, o + NS), ALU.mult, ALU.add)

    scores(0, 0, False)
    scores(1, 2, False)
    for t in range(3):
        send(A("xq"), A("pq%d" % t), "c", t, True)
        send(A("xs"), A("pp%d" % t), "s", t, False)
        best(ranks(N1, N1, lambda a, b: A("w3", 3 * a + 2, 3 * b, 3), NA[1 if t else 0], "ac1" if t else "ac0", N1 // 2 if t else 0))
        for k in range(3):
            l = A("l3", 8 * k, 8 * k + 7)
            act(A("r3", k, 336, 3), IND(A("sr"), l))
            tt(A("x1", k, 336, 3), IND(A("sr"), l), A("lm", k, 336, 3), ALU.max)
        iota(A("inv"), [[0, 784]], -17, 0, [A("l3", 0, 7)] if t else [])
        r = ranks(N2, 3 * K2, lambda a, b: A("r3", a, b), NA[2], "ac0")
        for k in range(3):
            act(A("k2", k, 336, 3), IND(A("pk" if t else "cpk"), A("l3", 8 * k, 8 * k + 7)))
        cp(IND(A("ew"), r), A("k2", 0, N2))
        windows(t, r)
        if t:
            late_tables(r)
        d = to_d("js", A("ew", 0, NS), NS)
        pi, ei, oi_ = A("di", 0, 7), A("di", 8, 15), A("di", 16, 23)
        PK, PE, PO, LF = [si(k) for k in range(4)]
        dd, ab, cc, cc2, mb, hi, neg, rd_, mc = [sf(k) for k in range(9)]
        ts(A("du", 0, 7), d, c384, ALU.subtract, 1.0 / 1024, ALU.mult)
        ts(pi, d, corr, ALU.subtract)
        cp(PK, A("ew", 0, K2))
        ts(ei, pi, 10, ALU.logical_shift_right)
        ts(oi_, pi, 1023, ALU.bitwise_and)
        cp(IND(A("inv"), A("du", 0, 7)), A("rx"))
        soft.add((len(ops) - 2, len(ops) - 1))
        cp(A("du", 8, 15), oi_)
        act(J("jp", 0, w=224), IND(A("inv"), A("du", 8, 15)))
        act(cc, J("jp", 0), bias=1.5 * 2.0 ** 41 - 4 * 2.0 ** 18, scale=-2.0 ** 16)
        act(cc2, cc, bias=-1.5 * 2.0 ** 41)
        ts(PE, PK, 10, ALU.logical_shift_right, 1022, ALU.bitwise_and)
        d = slots_to_d(0)
        ts(A("du", 16, 23), d, cb15, ALU.subtract)
        if t:
            ts(PO, PK, 1022, ALU.bitwise_and)
            ts(LF, PK, 1, ALU.bitwise_and)
            tt(dd, PO, PE, ALU.subtract)
            act(ab, dd, AF.Abs, scale=0.5)
            act(J("ja", 0), ab, bias=1.0)
            tt(J("jn", 0), PE, PO, ALU.min)
            cp(S("v1", 2, 3), PO)
            act(mc, S("v1", 2, 3), bias=513.0, scale=256.0)
            tt(mb, mc, ab, ALU.add)
            act(S("t1", 2, 3), ab, bias=-1.0, scale=-1.0)
            act(S("v1", 1, 3), dd, scale=-1.0)
            act(rd_, dd, AF.Relu, scale=-0.5)
            tt(S("q1", 1, 2), LF, rd_, ALU.subtract)
        else:
            cp(J("jn", 0), PE)
            act(S("v1", 2, 3), J("jn", 0))
            act(mb, J("jn", 0), bias=513.0, scale=256.0)
        tt(J("jm", 0), cc2, mb, ALU.add)
        tt(S("v1", 0, 3), A("jc", 0, K2), PE, ALU.subtract)
        ts(A("di", 24, 31), pi, 10, ALU.logical_shift_right, 1022, ALU.bitwise_and)
        cp(A("du", 104, 111), A("di", 24, 31))
        send(A("du", 104, 112), A("sl%d" % t), "j", t, False)
        pair_means(0, A("du", 104, 111))
        lc, dn, mxp = A("du", 64, 71), A("df", 8, 15), A("df", 56, 63)
        ts(A("df", 0, 7), d, c225, ALU.not_equal)
        tt(dn, A("df", 0, 7), jl2, ALU.mult)
        tt(A("df", 16, 23), ei, oi_, ALU.is_gt)
        tt(A("df", 24, 31), dn, A("df", 16, 23), ALU.mult)
        tt(A("df", 32, 39), ei, oi_, ALU.min)
        tt(A("df", 40, 47), A("df", 32, 39), padv, ALU.max)
        tt(A("df", 48, 55), A("df", 40, 47), A("df", 24, 31), ALU.max)
        ts(lc, A("df", 48, 55), 0.5, ALU.mult, 7.0, ALU.add)
        tt(A("df", 64, 71), ei, oi_, ALU.max)
        tt(mxp, A("df", 64, 71), padv, ALU.max)
        for k in range(6):
            l = A("du", 16 + 8 * k, 23 + 8 * k)
            if k < 5:
                act(J("jp", k + 1, w=224), IND(J("jp", k, 0, 1, 226), l))
                ts(A("du", 24 + 8 * k, 31 + 8 * k), slots_to_d(k + 1), cb15, ALU.subtract)
                act(sf(9 + k % 2), J("ja", k))
                tt(J("ja", k + 1, w=224), IND(J("ja", k, 0, 1, 226), l), sf(9 + k % 2, w=NS), ALU.add)
            act(sf(11 + k % 2), J("jn", k))
            tt(J("jn", k + 1, w=224), IND(J("jn", k, 0, 1, 226), l), sf(11 + k % 2, w=NS), ALU.min)
            cp(A("jy", 224 * k + 1, 224 * k + 208, 2), J("jm", k))
            for a, b in ((0, 4), (4, 7)):
                act(A("jy", 224 * k + 32 * a, 224 * k + 32 * b, 2), IND(J("jm", k, 0, 1, 226), A("du", l[1] + a, l[1] + b)))
                e = min(32 * b, 208)
                scan(J("jm", k + 1, 32 * a, 1, e), J("ja", k, 32 * a, 1, e), A("jy", 224 * k + 32 * a, 224 * k + e), ALU.add, ALU.min)
        m, nm, nc, cb = J("jm", 6), sf(13), S("tz", 1, 3), S("vz", 2, 3)
        for j in range(2):
            tt(sf(13, j, 2), J("jn", 6, 1, 4), J("jn", 6, 3, 4), ALU.min)
        tt(S("tz", 2, 3), J("jn", 0), nm, ALU.is_equal)
        ts(hi, m, 2.0 ** 32 - 256.0, ALU.add, 2.0 ** 32, ALU.subtract)
        tt(nc, m, A("pn", 0, K2), ALU.is_lt)
        tt(S("t1", 1, 3), m, hi, ALU.subtract)
        for j in range(2):
            tt(A("t1", 3 * j, 312, 6), J("jm", 6, 3 - 2 * j, 4), sf(5, 1 - j, 2), ALU.subtract)
            tt(A("vz", 2 + 3 * j, 312, 6), J("jm", 6, 3 - 2 * j, 4), J("jm", 6, 1 + 2 * j, 4), ALU.is_gt if j else ALU.is_ge)
        scan(A("t2", 0, 312), A("tz", 0, 312), A("t1", 0, 312), ALU.mult, ALU.add)
        cp(IND(A("tl"), lc), A("t2", 2, 336, 3))
        ms(col("cum", 7), 512.0)
        scan(A("cum", 8, 8 + C), A("onp"), A("tl", 7, 7 + C), ALU.add, ALU.add, 512.0)
        d = to_d("js", sf(13, w=NS), NS, NS)
        ts(A("du", 72, 79), d, c14, ALU.subtract, 0.5, ALU.mult)
        act(S("nz", 1, 2), cb, bias=1.0, scale=-2.0)
        act(sf(14), S("t2", 1, 3), bias=0.0 if t else 0.5, scale=0.5)
        act(S("n1", 1, 2), S("t2", 1, 3), bias=-1.0 if t else -0.5, scale=0.5)
        tt(S("n1", 0, 2), sf(14), S("t1", 1, 3), ALU.subtract)
        scan(A("n2", 0, 208), A("nz", 0, 208), A("n1", 0, 208), ALU.mult, ALU.add)
        tt(A("q1", 0, 224, 2), IND(A("cum"), A("du", 72, 79)), A("n2", 1, 224, 2), ALU.add)
        if t:
            tt(neg, cb, LF, ALU.is_equal)
            act(S("qz", 1, 2), neg, bias=1.0, scale=-2.0)
            scan(A("q2", 0, 208), A("qz", 0, 208), A("q1", 0, 208), ALU.mult, ALU.add)
        cp(IND(A("cum"), lc), A("q2", 1, 224, 2) if t else A("q1", 0, 224, 2))
        act(S("vz", 1, 3), nc)
        for lo, hi in ((0, 192), (192, 312)):
            scan(A("v2", lo, hi), A("vz", lo, hi), A("v1", lo, hi), ALU.mult, ALU.add)
        d = to_d("js", A("vz", 2, 336, 3), NS, 2 * NS)
        ts(A("df", 72, 79), d, chalf, ALU.is_lt)
        tt(A("df", 80, 87), A("df", 72, 79), dn, ALU.mult)
        tt(A("df", 88, 95), A("df", 80, 87), mxp, ALU.max)
        ts(A("du", 112, 119), A("df", 88, 95), 0.5, ALU.mult, -0.25, ALU.add)
        for lo, hi in ((0, 4), (4, 7)):
            cp(IND(A("v0"), A("du", 112 + lo, 112 + hi)), A("v2", 48 * lo + 2, 48 * hi, 3))
        for lo, hi in ((0, H), (H, C)) if t else ():
            scan(A("qs", lo, hi), A("hc", lo, hi), A("cum", 7 + lo, 7 + hi), ALU.add, ALU.min)
            to_d("sc", A("qs", lo, hi), H, lo)
        d = A("sc", 15, C, 16) if t else to_d("sc", A("cum", 7, 7 + C), C)
        pos = A("du", 80, 104)
        if t:
            tt(A("df", 96, 120), klc, d, ALU.subtract)
            tt(A("df", 128, 152), A("df", 96, 120), d, ALU.max)
        ts(pos, A("df", 128, 152) if t else d, c512, ALU.subtract)
        cp(IND(A("vw"), pos), A("v0", 0, C))
        pair_means(1, A("sl%d" % t, 0, 7))
        for h in (1, 0):
            l = A("pl", 32 * t + 16 * h, 32 * t + 16 * h + 12)
            ts(l, to_d("sc2", A("vw", H * h, H * h + H), H, H * h), corr, ALU.subtract)
        send(A("pl", 32 * t + 16, 32 * t + 28), A("nl%d" % t), "n", t, False)
        for h, l in enumerate((l, A("nl%d" % t))):
            for b in range(4):
                (act if b < YA[h] else cp)(A("yt", 768 * h + b, 768 * h + 768, 4), IND(A("wn%d" % h, WN * b, WN * b + WN), l))
            qz(A("zq", H * h, H * h + H), A("zs", H * h, H * h + H), A("yt", 768 * h, 768 * h + 768))
        act(A("fb", 8, 8 + H), IND(A("alt"), A("pl", 32 * t, 32 * t + 12)))
        act(A("fb", 8 + H, 8 + C), IND(A("alt"), A("nl%d" % t)))
        ms(col("fb", 7 + H), 0.0)
        half_layer(t, 0)
        if t < 2:
            tables(t)
            scores(0, 2, True)
            half_layer(t, 1)
            scores(1, 0, True)
        else:
            store(0)
            ts(A("df", 160, 184), d, -1.0, ALU.mult, corr2, ALU.add)
            ts(A("df", 192, 216), A("df", 160, 184), 1.0, ALU.add)
            tt(A("df", 224, 248), A("df", 192, 216), d, ALU.max)
            ts(A("du", 128, 152), A("df", 224, 248), c512, ALU.subtract)
            cp(IND(A("of"), A("du", 128, 152)), A("ik", 0, C))
            dma("s", [fk], [], T.ol[:, C:2 * C], T.fb[0:128:16, 8:8 + C])
            dma("s", [A("of")], [], T.ol[:, 0:C], T.of[0:128:16, :])
            half_layer(t, 1)
            store(1)
    for k in range(4):
        dma("s" if k % 2 else "a", [A("xs", 0, C)], [], T.osc[4 * k:4 * k + 4, :], T.xs[32 * k:32 * k + 4, 0:C])
    issue()
